import numpy as np, ml_dtypes
CORES = [1,5,17,21,33,37,49,53]
N = 8
BF = ml_dtypes.bfloat16
def gentries(a):
    return np.ascontiguousarray(a.reshape(8, 16, -1).transpose(0, 2, 1)).reshape(8, -1)
def gtable(e):
    e = np.asarray(e); return np.ascontiguousarray(e.reshape(8, -1, 16).transpose(0, 2, 1)).reshape(128, -1).astype(np.int32)
W, C, M, V, E = 4096, 192, 16, 5, 2
def parts(rng):
    u = rng.random((N, 8, 16, W), dtype=np.float32); z = rng.random((N, 8, 16, W), dtype=np.float32); ty = rng.integers(0, 3, (N, 8, 1, W))
    u = np.where(ty == 0, np.minimum(u, z), np.where(ty == 1, u, np.maximum(u, z)))
    here = rng.random((N, 8, 16, W)) < 0.35 + 0.65 * rng.random((N, 8, 1, W))
    x = np.where(here, np.minimum(1 + (255 * u).astype(np.int64), 255), 0)
    L = rng.integers(0, W, (N, 8, C, 16)); k = (rng.random((N, 8, C, 16)) < 0.25).astype(np.int64)
    o = np.argsort(rng.random((N, 8, W)), axis=-1)[..., :M * C]
    t = rng.integers(0, 256, (N, 8, 16, C)); w = rng.integers(0, 4096, (N, 8, 16)); th = rng.integers(3, 10, (N, 8, V))
    return x, L, k, np.ascontiguousarray(o), t, w, th
def deep(rng, x, L, k, o, th, g):
    n = C // 4; z = n * (M // 4); slots = np.concatenate([np.array([0]), 1 + rng.permutation(C - 2)[:n - 2], np.array([C - 1])])
    p = rng.permutation(W); u, d, full, none, half = p[:3], p[3:6], p[6:10], p[10:12], p[12:14]; used = p[14:14 + N * z].reshape(N, z)
    y = x[:, g]; y[..., u] = 1; y[..., used.reshape(-1)] = 1; y[..., full] = 255; y[..., none] = 0
    y[..., d] = np.where(np.argsort(rng.random((N, 16, 3)), axis=1) < 2, 255, 1)
    y[..., half] = np.where(np.argsort(rng.random((N, 16, 2)), axis=1) < 8, 255, 1)
    for r in range(N):
        a = np.zeros((C, M), np.int64); rest = np.ones((C, M), bool); rest[slots, ::4] = False
        a[~rest] = rng.permutation(used[r]); a[rest] = rng.permutation(np.setdiff1d(p, used[r]))[:M * C - z]
        o[r, g] = a.reshape(-1)
    kind = rng.integers(0, 3, (N, C, 1)); ff = rng.choice(full, (N, C, 16)); fe = rng.choice(np.concatenate([full, none]), (N, C, 16))
    a = np.where(kind < 2, fe, ff); a[..., 0] = np.where(kind[..., 0] == 2, rng.choice(u, (N, C)), a[..., 0]); b = np.where(kind < 2, rng.integers(0, 2, (N, C, 16)), 0)
    q = ff[:, slots]; q[..., 0] = rng.choice(u, (N, n)); q[..., 1:3] = rng.choice(d, (N, n, 2)); q[..., 3] = rng.choice(half, (N, n)); a[:, slots] = q; b[:, slots] = 1
    L[:, g] = a; k[:, g] = b; th[:, g] = rng.choice(np.array([8, 15]), (N, V)); th[:, g, :2] = 1
    if g == 7:
        th[:, g, 2:5] = 15; th[:, g, 5:] = 8
def pack(x, L, k, o, t, w, th):
    return {"dep": np.ascontiguousarray(x.reshape(N, 128, W)).astype(np.float32).astype(BF), "nam": np.stack([gtable(a.reshape(8, -1)) for a in L]), "mrk": np.stack([gtable(a.reshape(8, -1)) for a in k]),
            "own": np.stack([gtable(a) for a in o]), "pic": np.ascontiguousarray(t.reshape(N, 128, C)).astype(np.float32).astype(BF), "wt": w.reshape(N, 128, 1).astype(np.int32), "thr": np.ascontiguousarray(th).astype(np.int32)}
def setup_inputs(rng):
    return pack(*parts(rng))
def setup_inputs_spread(rng):
    x, L, k, o, t, w, th = parts(rng)
    x = np.minimum(np.exp2(8 * np.sqrt(rng.random((N, 8, 1, W))) * rng.random((N, 8, 16, W))).astype(np.int64) - 1, 255)
    t = np.minimum(np.exp2(8 * rng.random((N, 8, 16, C))).astype(np.int64) - 1, 255); w = np.minimum(np.exp2(12 * rng.random((N, 8, 16))).astype(np.int64) - 1, 4095)
    L = np.minimum((W * rng.random((N, 8, C, 16)) ** 3).astype(np.int64), W - 1); k = (rng.random((N, 8, C, 16)) < rng.random((N, 8, C, 1))).astype(np.int64)
    th = 1 + (14 * rng.random((N, 8, V)) ** 2).astype(np.int64)
    return pack(x, L, k, o, t, w, th)
def setup_inputs_ends(rng):
    x, L, k, o, t, w, th = parts(rng); lane = np.arange(16)[:, None]
    b = 255 * rng.integers(0, 2, (N, 8, 16, W)); q = rng.random((N, 8, 1, W))
    x = np.where(q < 0.2, b, np.where(q < 0.42, 255, np.where(q < 0.65, 1, np.where(q < 0.75, np.maximum(b, 1), np.where(q < 0.9, np.where(lane == 15, 1, 255), 0)))))
    for g in range(8):
        if g % 2 == 0 or g == 7:
            x[:, g, :, 0] = 1; x[:, g, :, W - 1] = 255
        else:
            x[:, g, :, 0] = 255; x[:, g, 15, 0] = 1; x[:, g, :, W - 1] = 1
    u = rng.random((N, 8, C, 16)); L = np.where(u < 0.36, 0, np.where(u < 0.72, W - 1, L)); k = rng.integers(0, 2, (N, 8, C, 16))
    L[:, 7, 0] = W - 1; L[:, 7, C - 1] = W - 1
    L[:, 7, 1] = 0; L[:, 7, C - 2] = 0; L[:, 7, 1, 15] = W - 1; L[:, 7, C - 2, 15] = W - 1; k[:, 7, 1] = 0; k[:, 7, C - 2] = 1
    h = (M * C) // 2; mid = np.concatenate([np.arange(1, M * C - h), np.arange(W - h, W - 1)]); c = (C - 1) * M
    for r in range(N):
        for g in range(8):
            p = rng.permutation(mid); o[r, g] = np.concatenate([p[:c], np.array([0]), p[c:c + M // 2 - 1], np.array([W - 1]), p[c + M // 2 - 1:]])
    t = 255 * rng.integers(0, 2, (N, 8, 16, C)); t[:, 7] = 255; w = 4095 * rng.integers(0, 2, (N, 8, 16)); w[:, 7] = 4095; w[:, 6, 0] = 4095; w[:, 3] = 0
    th = np.where(rng.random((N, 8, V)) < 0.6, 1, 15)
    return pack(x, L, k, o, t, w, th)
def setup_inputs_corners(rng):
    x, L, k, o, t, w, th = parts(rng); lane = np.arange(16)
    pal = [np.full(16, 100), np.full(16, 255), np.where(lane < 8, 200, 50), np.where((lane >= 8) & (lane < 8 + E), 10, 0), np.where((lane >= 8) & (lane < 7 + E), 10, 0),
           np.zeros(16, np.int64), np.full(16, 1), np.where(lane < 8, 101, 100), np.where(lane < 7, 101, 100), np.full(16, 200)]
    f = rng.choice(np.array([0, 5]), (N, 8, C, 16)); f[..., 0] = 0
    s = (np.arange(C) + rng.integers(0, 12, (N, 8, 1))) % 12
    f[s == 1, 15] = 2
    f[s == 2, 1] = 2
    f[s == 3, 1] = 2; f[s == 3, 15] = 3
    f[s == 4, 15] = 2; f[s == 4, 14] = 3; f[s == 4, 13] = 4
    f[s == 5, 2] = 2; f[s == 5, 1] = 3
    f[s == 6] = 3; f[s == 6, 0] = 0; f[s == 6, 1] = 2
    f[s == 7, 1] = 8; f[s == 7, 2] = 7; f[s == 7, 3] = 1
    f[s == 8, 0] = 5; f[s == 8, 1] = 1
    f[s == 9] = 1; f[s == 9, 0] = 6
    f[s == 10] = 0
    f[s == 11] = rng.integers(0, 10, (int(np.count_nonzero(s == 11)), 16))
    for g in range(8):
        if g == 3 or g == 6: continue
        q = rng.permutation(W)[:10]
        for i in range(10): x[:, g, :, int(q[i])] = pal[i]
        L[:, g] = q[f[:, g]]
    m = rng.integers(0, 3, (N, 8, C, 1)); k = np.where(m == 0, 1, np.where(m == 1, 0, k))
    th = rng.choice(np.array([1, 7, 8, 8, 9, 15]), (N, 8, V)); th[..., 0] = np.array([8, 7, 8, 1, 8, 7, 15, 8])
    k[:, 3] = 1; th[:, 3] = 1; k[:, 6] = 0; th[:, 6] = 15
    t[:, 0] = 0; t[:, 6] = 255; t[:, 2, :, ::2] = 255; w[:, 5] = 4095; w[:, 0, ::2] = 0
    deep(rng, x, L, k, o, th, 4); deep(rng, x, L, k, o, th, 7)
    return pack(x, L, k, o, t, w, th)
def setup_inputs_crowd(rng):
    x, L, k, o, t, w, th = parts(rng); lane = np.arange(16)
    pal = [np.full(16, 1), np.full(16, 255), np.where(lane == 15, 1, 255), np.where(lane < 8, 200, 120), np.where(lane < 8, 1, 0), np.full(16, 150)]
    for g in range(8):
        z = rng.permutation(W)[:6]
        for i in range(6): x[:, g, :, int(z[i])] = pal[i]
        if g % 4 == 0:
            odd = rng.integers(0, 16, (N, C, 1)) == np.arange(16); L[:, g] = np.where(odd, z[rng.integers(1, 3, (N, C, 1))], z[0])
        elif g % 4 == 1: L[:, g] = z[rng.integers(0, 6, (N, C, 16))]
        elif g % 4 == 2:
            L[:, g] = z[rng.integers(0, 6, (1, 1, 16))]; L[:, g, :, 0] = z[0]; L[:, g, :, 9] = z[2]
        else: L[:, g] = z[3]
        rest = np.setdiff1d(np.arange(W), z)
        for r in range(N): o[r, g] = rng.permutation(np.concatenate([z, rng.permutation(rest)[:M * C - 6]]))
    k = (rng.random((N, 8, C, 16)) < 0.5).astype(np.int64); th = rng.choice(np.array([1, 8, 14, 15]), (N, 8, V)); th[:, 1, 0] = 14; th[:, 5, 0] = 15; th[:, 0, 0] = 15; th[:, 2, 0] = 1
    return pack(x, L, k, o, t, w, th)
def setup_inputs_ranks(rng):
    x, L, k, o, t, w, th = parts(rng); q = rng.permutation(N)
    for i in (0, 2, 3):
        r = int(q[i]); th[r, :, 0] = 1; k[r] = 0 if i == 3 else 1
        for g in range(8):
            z = rng.permutation(W)[:2]; x[r, g, :, int(z[0])] = 1; x[r, g, :, int(z[1])] = 255
            a = L[r, g]; a[:, 0] = z[0]; a[np.arange(C), rng.integers(1, 16, C)] = z[1]
    k[int(q[2]), 7, C - 1] = 0; k[int(q[3]), 7, C - 1] = 1
    b = int(q[1]); th[b] = 15
    for g in range(8):
        e = rng.permutation(16)[:2]; y = x[b, g]; y[e] = rng.integers(1, 256, (2, 1))
        if g == 2 or g == 7:
            y[int(e[0])] = 2 * (2 * int(rng.integers(0, 64)) + 1); w[b, g] = 0; w[b, g, int(e[0])] = W // 2
    return pack(x, L, k, o, t, w, th)
def check_inputs(d):
    bad = []
    for a, lo, hi in (("dep", 0, 255), ("nam", 0, W - 1), ("mrk", 0, 1), ("own", 0, W - 1), ("pic", 0, 255), ("wt", 0, 4095), ("thr", 1, 15)):
        v = np.asarray(d[a]).astype(np.float64)
        if not (np.min(v) >= lo and np.max(v) <= hi): bad.append("range of " + a)
        elif np.any(v != np.floor(v)): bad.append("whole numbers of " + a)
    s = np.sort(np.stack([gentries(np.asarray(a)) for a in d["own"]]), axis=-1)
    if np.any(s[..., 1:] == s[..., :-1]): bad.append("distinct numbers of own")
    return bad
def reference(dep, nam, mrk, own, pic, wt, thr):
    X = dep.astype(np.float32).astype(np.int32).reshape(N, 8, 16, W)
    L = np.stack([gentries(a) for a in nam]).astype(np.int64).reshape(N, 8, C, 16); K = np.stack([gentries(a) for a in mrk]).astype(np.int64).reshape(N, 8, C, 16)
    O = np.stack([gentries(a) for a in own]).astype(np.int64).reshape(N, 8, C, M)
    T = pic.astype(np.float32).astype(np.int64).reshape(N, 8, 16, C); A = np.zeros((N, 8, C), np.int64); wv = wt.astype(np.int64).reshape(N, 8, 16, 1)
    row = np.arange(16)
    for v in range(V):
        G = np.take_along_axis(X, L.reshape(N, 8, 1, 16 * C), 3).reshape(N, 8, 16, C, 16)
        P = G[..., 0]
        cnt = np.add.reduce((P > 0)[..., None] & (G > P[..., None]), axis=2, dtype=np.int64)
        clash = cnt >= (thr[:, :, v].astype(np.int64)[..., None] + (A & 1))[..., None]
        some = np.any(clash, axis=3); k = np.argmax(clash, axis=3)
        km = np.take_along_axis(K, k[..., None], 3)[..., 0]
        none = ~some; turn = some & (km == 0); cut = some & (km == 1)
        T = np.where(none[:, :, None, :] & (P > 0), P, T)
        h = np.add.reduce(wv * T, axis=2) & (W - 1)
        xk = np.take_along_axis(G, k[:, :, None, :, None], 4)[..., 0]
        n = np.add.reduce(xk, axis=2, dtype=np.int64) & (M - 1)
        na = np.take_along_axis(O, n[..., None], 3)[..., 0]; nb = np.take_along_axis(O, (n ^ (M // 2))[..., None], 3)[..., 0]
        far = np.where(xk > P, xk, 0); near = np.where(xk <= P, xk, 0)
        enter = np.add.reduce((G > 0) & (G < near[..., None]), axis=2, dtype=np.int64) >= E
        j = np.where(np.any(enter, axis=3), np.argmax(enter, axis=3), 16)
        isk = row == k[..., None]; key = np.broadcast_to(4 * row, (N, 8, C, 16))
        key = np.where(none[..., None] & (row == 0), 999, key); key = np.where(turn[..., None] & isk, -1, key); key = np.where(cut[..., None] & isk, 999, key)
        ka = np.where(none, 100, np.where(cut, -1, 999)); kb = np.where(cut, 4 * j - 1, 999)
        order = np.argsort(np.concatenate([key, ka[..., None], kb[..., None]], axis=3), axis=3, kind="stable")[..., :16]
        L = np.take_along_axis(np.concatenate([L, np.where(none, h, na)[..., None], nb[..., None]], axis=3), order, 3)
        K = np.take_along_axis(np.concatenate([np.where(turn[..., None] & isk, 1, K), np.zeros((N, 8, C, 2), np.int64)], axis=3), order, 3)
        A = A + cut
        for r in range(N):
            for g in range(8):
                i = np.flatnonzero(cut[r, g])
                X[r, g][:, na[r, g, i]] = far[r, g][:, i]; X[r, g][:, nb[r, g, i]] = near[r, g][:, i]
        if v < V - 1: L, K, T, A = np.roll(L, 1, axis=0), np.roll(K, 1, axis=0), np.roll(T, 1, axis=0), np.roll(A, 1, axis=0)
    return {"ydep": X.reshape(N, 128, W).astype(np.float32).astype(BF), "ynam": np.stack([gtable(a.reshape(8, -1)) for a in L]).astype(np.float32), "ymrk": np.stack([gtable(a.reshape(8, -1)) for a in K]).astype(np.float32),
            "ypic": T.reshape(N, 128, C).astype(np.float32).astype(BF), "ycut": A.astype(np.float32)}

@@ -1,0 +1,578 @@
+from concourse.mybir import AluOpType, ActivationFunctionType
+OP = AluOpType
+AF = ActivationFunctionType
+
+W, C, NV = 4096, 192, 5
+NH = 2
+MB = 6
+CW = 16 * MB
+BIG = 1048576.0
+CAP = 4096.5
+f32, bf, i32, u16 = "float32", "bfloat16", "int32", "uint16"
+KN = {"SGV": 0, "GES": True, "LATE": 0, "GV": (3, 2), "SLACK": 0.02, "LEAD": 3000.0, "SEED": 0, "JIT": 0.0, "NE": 8,
+      "CY": 1.0, "PCY": 0.5, "HOP": 70.0, "GA": 1.56, "SCA": 3.8, "RT": 2600.0, "FV": 55.0, "FS": 70.0}
+
+SCRATCH = {
+    "tab": ("sbuf", [128, 2 * W + 16], bf),
+    "MS": ("sbuf", [128, NV * NH, 7, 18], f32), "SO": ("sbuf", [128, NV * NH, 7, 18], f32),
+    "TR": ("sbuf", [128, NV * NH, C], bf), "TS": ("sbuf", [128, NV * NH, C], bf),
+    "lnam": ("sbuf", [128, C], i32), "lmrk": ("sbuf", [128, C], i32), "lown": ("sbuf", [128, C], i32),
+    "lwt": ("sbuf", [128, 4], i32), "lthr": ("sbuf", [128, 8], i32),
+    "a3": ("sbuf", [128, 6, 32], f32), "b3": ("sbuf", [128, 6, 32], f32), "tmp": ("sbuf", [128, C], f32),
+    "ones": ("sbuf", [128, 160], f32), "wide": ("sbuf", [128, 160], f32), "wide0": ("sbuf", [128, 160], f32),
+    "wide1": ("sbuf", [128, 160], f32), "nidf": ("sbuf", [128, 128], f32),
+    "idb": ("sbuf", [128, 128], bf), "nidb": ("sbuf", [128, 128], bf), "idbig": ("sbuf", [128, 128], bf),
+    "idm256": ("sbuf", [128, 128], bf), "gm": ("sbuf", [128, 128], f32), "gm1": ("sbuf", [128, 128], f32),
+    "gms": ("sbuf", [128, 128], bf), "whi": ("sbuf", [128, 128], bf), "wlo": ("sbuf", [128, 128], bf),
+    "sel": ("sbuf", [128, 144], bf), "g8t": ("sbuf", [128, 256], f32),
+    "ci": ("sbuf", [128, 12, 8], i32), "cf": ("sbuf", [128, 12, 8], f32),
+    "ij": ("sbuf", [128, C], i32), "jj": ("sbuf", [128, C], f32),
+    "adiag": ("sbuf", [128, CW], f32), "d0r": ("sbuf", [128, CW], f32), "d0u": ("sbuf", [128, CW], f32),
+    "d0m": ("sbuf", [128, 2 * CW], f32), "key": ("sbuf", [128, 2 * CW], f32),
+    "kc": ("sbuf", [128, 6, CW], bf), "dth": ("sbuf", [128, NV, 128], bf),
+    "bc6": ("sbuf", [128, 6], u16), "bc12": ("sbuf", [128, 12], u16), "bcn": ("sbuf", [128, 6], u16),
+}
+PER_HALF = {
+    "G": ([6, 256], bf), "I": ([6, 256], bf), "SG": ([6, 256], bf), "off": ([CW + 2], u16), "offp": ([6], u16),
+    "xoff": ([6], u16), "soff": ([12], u16), "val": ([CW], f32), "R": ([CW], f32),
+    "sc": ([CW], f32), "sh": ([CW], f32), "oa": ([2 * CW], f32), "D": ([2 * CW], f32), "R3": ([2 * CW], f32),
+    "P": ([CW], bf), "xk": ([CW], bf), "gt": ([CW], bf), "B2": ([CW], bf), "Bv": ([CW], bf), "z": ([CW], bf),
+    "e": ([CW], bf), "nl": ([CW], bf), "tb": ([CW], bf),
+    "m1": ([3 * CW + 8], bf), "m2": ([3 * CW + 8], bf), "w1": ([3 * CW + 8], f32), "w2": ([3 * CW], f32), "U": ([CW], f32),
+    "si": ([8, 8], i32), "sf": ([8, 8], f32), "ax": ([6, 16], f32),
+}
+for _h in range(NH):
+    for _k, (_s, _d) in PER_HALF.items():
+        SCRATCH[_k + str(_h)] = ("sbuf", [128] + _s, _d)
+    SCRATCH["pA%d" % _h] = ("psum", [128, 6, 80], f32)
+    SCRATCH["pB%d" % _h] = ("psum", [128, 32, 16], f32)
+    SCRATCH["pC%d" % _h] = ("psum", [128, 512], f32)
+    SCRATCH["pD%d" % _h] = ("psum", [128, 32, 16], f32)
+LOADS = ["dA", "dB", "ln", "lm", "lo", "lp0", "lp1", "lw", "lt"]
+SEMAPHORES = (["v", "s", "p", "g", "sent", "st"] + LOADS
+              + ["a%s%d%d" % (k, v, h) for k in "MT" for v in range(1, NV) for h in range(NH)])
+
+
+def build(T, topo, core, rank):
+    ops = []
+    CY, PCY, GA, SCA, SGV = KN["CY"], KN["PCY"], KN["GA"], KN["SCA"], KN["SGV"]
+
+    def op(e, fs, r, w, ns, banks=(), lock=None, sem=None):
+        ops.append({"e": e, "f": fs if isinstance(fs, list) else [fs], "r": r, "w": w, "ns": ns,
+                    "banks": banks, "lock": lock, "sem": sem})
+
+    def bk(names):
+        return tuple(sorted(set(n[:3] for n in names if n[0] == "p" and n[1] in "ABCD")))
+
+    def V(f, r, w, n):
+        op("v", f, r, w, KN["FV"] + n * CY, bk(r + w))
+
+    def S(f, r, w, n):
+        op("s", f, r, w, KN["FS"] + n * CY, bk(r + w))
+
+    def G(f, r, w, n):
+        op("g", f, r, w, 170 + 2 * n * CY)
+
+    def fill(o, c, w, n):
+        G(lambda q: q.iota(o, [[0, n]], c, 0, allow_small_or_imprecise_dtypes=True), [], w, n)
+
+    def P(mm, r, w, first=True, last=True):
+        fs, ns = [], 0
+        for k, (o, l, x, cost) in enumerate(mm):
+            fs.append(lambda q, o=o, l=l, x=x, a=(first and k == 0), b=(last and k == len(mm) - 1): q.matmul(o, l, x, a, b))
+            ns += cost * PCY
+        op("p", fs, r, w, ns + 20, bk(r + w), None if first and last else ("open" if first else "close" if last else "more"))
+
+    def tt(o, a, b, f):
+        return lambda q: q.tensor_tensor(o, a, b, f)
+
+    def ts(o, a, s1, f1, s2=None, f2=None):
+        if f2 is None:
+            return lambda q: q.tensor_scalar(o, a, s1, None, f1)
+        return lambda q: q.tensor_scalar(o, a, s1, s2, f1, f2)
+
+    def cp(o, a):
+        return lambda q: q.tensor_copy(o, a)
+
+    def ms(o, c):
+        return lambda q: q.memset(o, c)
+
+    def tr(o, a):
+        return lambda q: q.transpose(o, a)
+
+    def act(o, a, f, bias=0.0, scale=1.0):
+        return lambda q: q.activation(o, a, f, bias=bias, scale=scale)
+
+    def scan(o, a, b, f0, f1):
+        return lambda q: q.tensor_tensor_scan(o, a, b, 0.0, f0, f1)
+
+    def load(e, name, o, i, w, ns):
+        op(e, lambda q: q.dma_start(o, i), [], w, ns, sem=name)
+
+    def store(o, i, r, ns):
+        op("y", lambda q: q.dma_start(o, i), r, [], ns, sem="st")
+
+    load("y", "ln", T.lnam[:], T.nam[:], ["lnam"], 2000)
+    load("y", "lm", T.lmrk[:], T.mrk[:], ["lmrk"], 2000)
+    load("y", "dA", T.tab[:, 0:2048], T.dep[:, 0:2048], ["tabA"], 4000)
+    load("y", "dB", T.tab[:, 2048:W], T.dep[:, 2048:W], ["tabB"], 5000)
+    load("y", "lw", T.lwt[:, 0:1], T.wt[:], ["lwt"], 5200)
+    load("y", "lt", T.lthr[0:8, 0:5], T.thr[:], ["lthr"], 5200)
+    load("y", "lo", T.lown[:], T.own[:], ["lown"], 5400)
+    for h in range(NH):
+        load("y", "lp%d" % h, T.TR[:, h, 0:CW], T.pic[:, CW * h:CW * h + CW], ["T0%d" % h], 5400)
+
+    idf, nidf = T.wide[:, 16:144], T.nidf[:]
+    col = lambda k: T.cf[:, k, 0:1]
+    PM, PM1, SCL, H0, H1, WH, WL = range(7)
+    kh, ks, ky, kr, k1, km = (T.kc[:, k, :] for k in range(6))
+    V(ms(T.ones[:], 1.0), [], ["ones"], 160)
+    G(lambda q: q.iota(T.ci[:, 0, 0:1], [[0, 1]], 0, 1), [], ["ci0"], 1)
+    G(lambda q: q.affine_select(T.wide[:], T.ones[:], [[-1, 160]], OP.is_equal, 0.0, 16, 1), ["ones"], ["wide"], 160)
+    V(ts(T.ci[:, 1, 0:1], T.ci[:, 0, 0:1], 16, OP.bitwise_and), ["ci0"], ["ci1"], 1)
+    V(ts(col(H1), T.ci[:, 1, 0:1], 0.0625, OP.mult), ["ci1"], ["H1"], 1)
+    V(ts(col(H0), T.ci[:, 1, 0:1], -0.0625, OP.mult, 1.0, OP.add), ["ci1"], ["H0"], 1)
+    V(ts(T.wide0[:], T.wide[:], col(H0), OP.mult), ["wide", "H0"], ["wide0"], 160)
+    V(ts(T.wide1[:], T.wide[:], col(H1), OP.mult), ["wide", "H1"], ["wide1"], 160)
+    swap = {(0, 0): T.wide0[:, 16:144], (0, 1): T.wide0[:, 0:128], (1, 0): T.wide1[:, 32:160], (1, 1): T.wide1[:, 16:144]}
+    S(act(T.idb[:], idf, AF.Sigmoid, -128.0, 256.0), ["wide"], ["idb"], 1400)
+    S(act(T.nidb[:], idf, AF.Copy, scale=-1.0), ["wide"], ["nidb"], 128)
+    S(act(T.nidf[:], idf, AF.Copy, scale=-1.0), ["wide"], ["nidf"], 128)
+    S(act(T.idbig[:], idf, AF.Copy, scale=-BIG), ["wide"], ["idbig"], 128)
+    S(act(T.idm256[:], idf, AF.Copy, scale=-256.0), ["wide"], ["idm256"], 128)
+    G(lambda q: q.affine_select(T.gm1[:], T.ones[:, 0:128], [[-16, 8], [0, 16]], OP.is_ge, 0.0, 0, 1), ["ones"], ["gm1"], 128)
+    G(lambda q: q.affine_select(T.gm[:], T.gm1[:], [[16, 8], [0, 16]], OP.is_ge, 0.0, 15, -1), ["gm1"], ["gm"], 128)
+    V(ms(T.sel[:], 0.0), [], ["sel"], 72)
+    V(ts(T.sel[:, 15:143:16], T.gm[:, 0::16], -BIG, OP.mult), ["gm", "sel"], ["sel"], 8)
+    S(act(T.gms[:], T.gm[:], AF.Copy, scale=16384.0), ["gm"], ["gms"], 128)
+    V(ts(T.ci[:, 2, 0:1], T.lwt[:, 0:1], 3840, OP.bitwise_and), ["lwt"], ["ci2"], 1)
+    V(ts(T.ci[:, 3, 0:1], T.lwt[:, 0:1], 255, OP.bitwise_and), ["lwt"], ["ci3"], 1)
+    V(cp(col(WH), T.ci[:, 2, 0:1]), ["ci2"], ["WH"], 1)
+    V(cp(col(WL), T.ci[:, 3, 0:1]), ["ci3"], ["WL"], 1)
+    S(act(T.whi[:], T.gm[:], AF.Identity, scale=col(WH)), ["gm", "WH"], ["whi"], 128)
+    S(act(T.wlo[:], T.gm[:], AF.Identity, scale=col(WL)), ["gm", "WL"], ["wlo"], 128)
+    G(lambda q: q.affine_select(T.g8t[0:8, 128:256], T.ones[0:8, 0:128], [[1, 128]], OP.is_ge, 0.0, 0, -16), ["ones"], ["g8u"], 128)
+    G(lambda q: q.affine_select(T.g8t[0:8, 0:128], T.g8t[0:8, 128:256], [[-1, 128]], OP.is_ge, 0.0, 15, 16), ["g8u"], ["g8t"], 128)
+    V(cp(T.cf[0:8, 8, 0:5], T.lthr[0:8, 0:5]), ["lthr"], ["cf8"], 5)
+    P([(T.pC0[:, 480:485], T.g8t[0:8, 0:128], T.cf[0:8, 8, 0:5], 256)], ["g8t", "cf8"], ["pC0thr"])
+    V(ts(T.cf[:, 9, 0:1], T.pC0[:, 480:481], -0.5, OP.add, BIG, OP.mult), ["pC0thr"], ["thr0"], 1)
+    V(ts(T.cf[:, 9, 1:5], T.pC0[:, 481:485], 0.5, OP.add, BIG, OP.mult), ["pC0thr"], ["thrc"], 4)
+    for v in range(NV):
+        S(act(T.dth[:, v, :], idf, AF.Identity, scale=T.cf[:, 9, v:v + 1]), ["wide", "thrc" if v else "thr0"], ["dth%d" % v], 128)
+    G(lambda q: q.iota(T.ij[:, 0:CW], [[0, 6], [1, 16]], 0, 0), [], ["ij"], CW)
+    G(lambda q: q.iota(T.ij[:, CW:C], [[0, 6], [-8, 2], [1, 8]], 8, 0), [], ["ij2"], CW)
+    V(ts(T.ci[:, 4, 0:1], T.ci[:, 0, 0:1], 15, OP.bitwise_and), ["ci0"], ["ci4"], 1)
+    V(cp(col(PM), T.ci[:, 4, 0:1]), ["ci4"], ["PM"], 1)
+    V(ts(col(PM1), T.ci[:, 4, 0:1], 1.0, OP.add), ["ci4"], ["PM1"], 1)
+    V(ts(T.cf[:, 7, 0:1], T.ci[:, 4, 0:1], 15.0, OP.is_equal, 1.0 - 2.0 ** -13, OP.mult), ["ci4"], ["cf7"], 1)
+    V(ts(col(SCL), T.cf[:, 7, 0:1], 2.0 ** -13, OP.add), ["cf7"], ["SCL"], 1)
+    V(ts(T.jj[:, 0:CW], T.ij[:, 0:CW], col(PM), OP.not_equal), ["ij", "PM"], ["jj"], CW)
+    V(ts(T.jj[:, CW:C], T.ij[:, 0:CW], col(PM1), OP.is_equal, 8191.0, OP.mult), ["ij", "PM1"], ["jt"], CW)
+    V(tt(T.adiag[:], T.jj[:, 0:CW], T.jj[:, CW:C], OP.add), ["jj", "jt"], ["adiag"], 2 * CW)
+    for nm, c0, wd in (("d0r", -4096.0, CW), ("d0u", -1.0, CW), ("d0m", 0.0, C)):
+        V(ms(T[nm][:], c0), [], [nm], wd)
+        V(ms(T[nm][:, 0::16], BIG), [nm], [nm], 12)
+    V(ts(T.key[:], T.ij[:], 16384.0, OP.mult, 4096.25, OP.add), ["ij", "ij2"], ["key"], C)
+    fill(kh, 4096, ["kh"], CW)
+    fill(ks, 524288, ["ks"], CW)
+    V(ms(ky, -17.5), [], ["ky"], 48)
+    fill(k1, 1, ["k1"], CW)
+    fill(km, -512, ["km"], CW)
+    G(lambda q: q.iota(kr, [[0, 6], [-4096, 16]], 0, 0, allow_small_or_imprecise_dtypes=True), [], ["kr"], CW)
+    G(lambda q: q.iota(T.ci[:, 5, 0:6], [[1, 6]], 0, 0), [], ["ci5"], 6)
+    V(cp(T.bc6[:], T.ci[:, 5, 0:6]), ["ci5"], ["bc6"], 6)
+    V(cp(T.bc12[:, 0:6], T.ci[:, 5, 0:6]), ["ci5"], ["bc12a"], 6)
+    V(cp(T.bc12[:, 6:12], T.ci[:, 5, 0:6]), ["ci5"], ["bc12b"], 6)
+    V(ts(T.bcn[:], T.ci[:, 5, 0:6], 16.0, OP.mult, CW + 15.0, OP.add), ["ci5"], ["bcn"], 6)
+    for j, nm in enumerate(("tabC", "tabD", "tabF", "tabG")):
+        fill(T.tab[:, W + 1024 * j:W + 1024 * j + 1024], 0, [nm], 1024)
+    fill(T.tab[:, 2 * W:2 * W + 16], -1, ["tabE"], 16)
+    fill(T.SO[:], 0, ["SOinit"], NV * NH * 126)
+    for h in range(NH):
+        H = str(h)
+        fill(T["ax" + H][:], 0, ["ax" + H], CW)
+        V(ms(T.MS[:, h, :, 0], 0.0), [], ["Mx0" + H], 7)
+        V(ms(T.MS[:, h, 6, 0:6], 0.0), ["Mx0" + H], ["Mx0" + H], 6)
+        fill(T["m1" + H][:], 0, ["m1" + H], 3 * CW + 8)
+        fill(T["m2" + H][:], 0, ["m2" + H], 3 * CW + 8)
+
+    def turn(src, bank, slot, r, w, alias=()):
+        for o in range(2):
+            P([(T[bank][:, slot + o:slot + 6:2, :], swap[(o, k)], src(k), 256) for k in range(2)],
+              r + ["wide0", "wide1"], [w + str(o)] + list(alias))
+
+    V(ts(T.tmp[:], T.lmrk[:], -0.25, OP.mult, 0.25, OP.add), ["lmrk"], ["tmp"], C)
+    V(tt(T.a3[:], T.tmp[:], T.lnam[:], OP.add), ["tmp", "lnam"], ["a3"], 2 * C)
+    V(cp(T.b3[:], T.lown[:]), ["lown"], ["b3"], C)
+    for h in range(NH):
+        H = str(h)
+        turn(lambda k: T.a3[:, 3 * h:3 * h + 3, 16 * k:16 * k + 16], "pD" + H, 18, ["a3"], "pD%snew" % H)
+        V(tr(T["R" + H][:], T["pD" + H][:, 18:24, :]), ["pD%snew0" % H, "pD%snew1" % H], ["R" + H], CW)
+        V(cp(T.MS[:, h, 0:6, 1:17], T["R" + H][:]), ["R" + H], ["M0" + H], CW)
+        turn(lambda k: T.b3[:, 3 * h:3 * h + 3, 16 * k:16 * k + 16], "pD" + H, 12, ["b3"], "pD%sT" % H)
+        V(tr(T["U" + H][:], T["pD" + H][:, 12:18, :]), ["pD%sT0" % H, "pD%sT1" % H], ["U" + H], CW)
+        for k in range(2):
+            V(tt(T["oa" + H][:, CW * k:CW * k + CW], T["U" + H][:], T.key[:, CW * k:CW * k + CW], OP.add),
+              ["U" + H, "key"], ["oa%d%s" % (k, H)], 2 * CW)
+
+    nxt = T.cores[(rank + 1) % len(T.cores)]
+    rid, pid, _ = topo.addr(nxt)
+    emask = sum(1 << e for e in topo.engines(core, nxt)[:KN["NE"]])
+    TAB = ["tabA", "tabB"]
+    TABX = ["tabA", "tabB", "tabC", "tabD", "tabF", "tabG"]
+
+    def send(src, dst, sem, r, w):
+        op("g", lambda q: q.remote_dma(dst, src, T.sem[sem], T.sem.sent, pid, rid, emask), r, w, KN["RT"], sem=sem)
+
+    def part(v, h, second):
+        H = str(h)
+        b = lambda n: T[n + H]
+        n_ = lambda *a: [x + H for x in a]
+        k = v * NH + h
+        last = v == NV - 1
+        M, Mx, Tn, SOn = "M%d%s" % (v, H), "Mx%d%s" % (v, H), "T%d%s" % (v, H), "SO%d%s" % (v, H)
+        o, o0, o1 = T.MS[:, k, 0:6, 1:17], T.MS[:, k, 0:6, 0:16], T.MS[:, k, 0:6, 2:18]
+        Gs = ["G%d%s" % (m, H) for m in range(MB)]
+        Pv, Tv = b("P")[:], [T.TR[:, k, 0:CW], T.TR[:, k, CW:C]][:2 if v else 1]
+        pA, pB, pC, pD = b("pA"), b("pB"), b("pC"), b("pD")
+        A_, B_, C_, D_ = "pA" + H, "pB" + H, "pC" + H, "pD" + H
+        As = [A_ + str(x) for x in range(5)]
+        pp, sr, hr = pB[:, 12:18, :], pC[:, 3 * CW:4 * CW], pC[:, 4 * CW:5 * CW]
+        y1, y2 = pB[:, 0:6, :], pB[:, 6:12, :]
+        si = lambda j: b("si")[:, j, 0:6]
+        sf = lambda j: b("sf")[:, j, 0:6]
+
+        def compare(f, after=[]):
+            for j in range(3):
+                a = 16 + 80 * j
+                V(tt(b("I")[:, :, a:a + 80], b("G")[:, :, a:a + 80], pA[:], f), Gs + As + after + n_("~I"), n_("I%d_" % j, "~I"), 480)
+
+        def count(y, x, r0=1, r1=16):
+            return [(pB[:, y:y + 6, r0:r1], T.sel[:, 15 - i:143 - i], x[:, :, 16 * r0 + i:16 * r1:16], max(64, 6 * (r1 - r0))) for i in range(16)]
+
+        def count2(y, name):
+            P(count(y, b("I"), 1, 11), n_("I0_", "I1_") + ["sel", name], [name], first=False, last=False)
+            P(count(y, b("I"), 11, 16), n_("I2_") + ["sel", name], [name], first=False)
+
+        if not second:
+            V(cp(b("offp")[:], T.MS[:, k, 0:6, 1]), [M], n_("offp"), 6)
+            V(cp(b("off")[:, 1:CW + 1], o), [M], n_("off"), CW)
+            S(act(Pv, T.tab[:, 0:W].indirect(b("offp")[:, 0:6]), AF.Copy), TAB + n_("offp"), n_("P", "~G"), CW * GA)
+            for m in range(MB):
+                if m >= MB - KN["GV"][h]:
+                    V(cp(b("G")[:, m, 16:256], T.tab[:, 0:W].indirect(b("off")[:, 16 * m + 2:16 * m + 17])), TAB + n_("off"), [Gs[m]], 240 * GA)
+                    continue
+                S(act(b("G")[:, m, 16:256], T.tab[:, 0:W].indirect(b("off")[:, 16 * m + 2:16 * m + 17]), AF.Copy),
+                  TAB + n_("off", "~G"), [Gs[m]] + n_("~G"), 240 * GA)
+                if m == 0:
+                    S(act(b("z")[:], Pv, AF.Relu, 256.0, -256.0), n_("P", "~G"), n_("z", "~G"), CW)
+            for j in range(5):
+                cj = pA[:, :, 16 * j:16 * j + 16]
+                P([(cj, T.idb[:], Pv, CW), (cj, T.idb[:], b("z")[:], CW)], n_("P", "z") + ["idb"], [As[j]])
+            P([(pp, T.idb[:], Pv, CW)], n_("P") + ["idb"], [B_ + "P"])
+            compare(OP.is_gt)
+            odd = []
+            if v:
+                S(act(sf(4), T.MS[:, k, 6, 0:6], AF.Abs, -2.0, 1.0 / 4096), [Mx], n_("a1"), 6)
+                S(act(b("tb")[:], sf(4).indirect(T.bc6[:, 0:6]), AF.Abs, -1.0), n_("a1") + ["bc6"], n_("tb"), CW * GA)
+                odd = [(y1, T.idbig[:], b("tb")[:], CW)]
+            P([(y1, T.dth[:, v, :], k1, CW), (y1, T.idb[:], kr, CW)] + odd,
+              n_("tb") + ["idbig", "idb", "kr", "k1", "dth%d" % v, B_ + "P"], [B_ + "y1"], last=False)
+            count2(0, B_ + "y1")
+            V(tt(b("val")[:], y1, o, OP.max), [B_ + "y1", M], n_("val"), CW)
+            V(scan(b("R")[:], T.d0r[:], b("val")[:], OP.add, OP.min), n_("val") + ["d0r"], n_("R"), CW)
+            V(ts(si(0), b("R")[:, 15::16], CAP, OP.min, 16384.0, OP.mult), n_("R"), n_("x"), 6)
+            V(ts(si(1), si(0), 12288, OP.bitwise_and), n_("x"), n_("u4"), 6)
+            V(ts(si(2), si(0), 14, OP.arith_shift_right, W - 1, OP.bitwise_and), n_("x"), n_("Lk"), 6)
+            V(tt(sf(0), si(1), si(2), OP.add), n_("u4", "Lk"), n_("xo"), 12)
+            V(cp(b("xoff")[:], sf(0)), n_("xo"), n_("xoff"), 6)
+            S(act(b("xk")[:], T.tab[:].indirect(b("xoff")[:, 0:6]), AF.Copy), TABX + ["tabE"] + n_("xoff"), n_("xk"), CW * GA)
+            if SGV:
+                V(ts(b("SG")[:, :, 16:16 + 16 * SGV], b("G")[:, :, 16:16 + 16 * SGV], 0.0, OP.is_gt), Gs, n_("SGa"), 48 * SGV)
+            cuts = [SGV + 1 + (15 - SGV) * j // 3 for j in range(4)]
+            for j in range(3):
+                r0, r1 = cuts[j], cuts[j + 1]
+                if r1 > r0:
+                    S(act(b("SG")[:, :, 16 * r0:16 * r1], b("G")[:, :, 16 * r0:16 * r1], AF.Sign), Gs, n_("SG%d_" % j), CW * (r1 - r0))
+            P([(pD[:, 0:6, :], T.idb[:], x, CW) for x in Tv + [b("z")[:]]], [Tn, "idb"] + n_("z"), [D_ + "q1"])
+            S(act(b("e")[:], pD[:, 0:6, :], AF.Relu, -256.0), [D_ + "q1"], n_("e"), CW)
+            P([(hr, T.idb[:], kh, CW), (hr, T.whi[:], Pv, CW), (hr, T.wlo[:], Pv, CW), (hr, T.whi[:], b("e")[:], CW), (hr, T.wlo[:], b("e")[:], CW)],
+              n_("P", "e") + ["kh", "whi", "wlo", "idb"], [C_ + "h"])
+            V(scan(b("sh")[:], T.adiag[:], hr, OP.mult, OP.max), [C_ + "h", "adiag"], n_("sh"), CW)
+            V(ts(si(3), b("sh")[:, 15::16], col(SCL), OP.mult), n_("sh") + ["SCL"], n_("h1"), 6)
+            V(ts(si(4), si(3), W - 1, OP.bitwise_and), n_("h1"), n_("h2"), 6)
+            V(ts(T.MS[:, k, 0:6, 17], si(4), 0.25, OP.add), n_("h2") + [M], n_("hs"), 6)
+            P([(pC[:, 1:3 * CW:3], idf, o0, 384), (pC[:, 1:3 * CW:3], nidf, o, 384)], [M, Mx, "wide", "nidf"], [C_ + "dm"])
+            P([(pC[:, 2:3 * CW:3], idf, o, 384)], [M, "wide"], [C_ + "o"])
+            P([(pC[:, 0:3 * CW:3], nidf, o0, 384), (pC[:, 0:3 * CW:3], idf, o1, 384)], [M, Mx, "wide", "nidf"] + n_("hs"), [C_ + "d2"])
+            return
+        V(tt(b("gt")[:], b("xk")[:], pp, OP.is_gt), n_("xk") + [B_ + "P"], n_("gt"), CW)
+        qq = pD[:, 25:31, :]
+        P([(qq, T.idb[:], b("xk")[:], CW), (qq, T.idm256[:], b("gt")[:], CW)], n_("xk", "gt") + ["idb", "idm256"], [D_ + "q"])
+        S(act(b("B2")[:], qq, AF.Relu, -1.0), [D_ + "q"], n_("B2"), CW)
+        for j in range(5):
+            P([(pA[:, :, 16 * j:16 * j + 16], T.idb[:], b("B2")[:], CW)], n_("B2", "~B") + ["idb"], [As[j]] + n_("~B"))
+        S(act(b("Bv")[:], qq, AF.Relu), [D_ + "q"], n_("Bv"), CW)
+        late = KN["LATE"] and h == NH - 1 and v < KN["LATE"]
+        if not late:
+            compare(OP.is_le)
+        P([(sr, T.idb[:], ks, CW), (sr, T.gms[:], b("xk")[:], CW)], n_("xk") + ["idb", "ks", "gms"], [C_ + "s"])
+        V(scan(b("sc")[:], T.adiag[:], sr, OP.mult, OP.max), [C_ + "s", "adiag"], n_("sc"), CW)
+        V(ts(si(5), b("sc")[:, 15::16], col(SCL), OP.mult), n_("sc") + ["SCL"], n_("s1"), 6)
+        V(ts(si(6), si(5), 15 * 16384, OP.bitwise_and), n_("s1"), n_("s2"), 6)
+        S(act(sf(3), sf(0), AF.Sign, 4095.5, -1.0), n_("xo"), n_("cut"), 6)
+        S(act(sf(1), sf(3), AF.Identity, 2048.0, 2048.0), n_("cut"), n_("c4"), 6)
+        V(tt(sf(2), si(6), sf(1), OP.add), n_("s2", "c4"), n_("ms"), 12)
+        V(tt(b("D")[:], sf(2).indirect(T.bc12[:, 0:12]), b("oa")[:], OP.subtract), n_("ms", "oa0", "oa1") + ["bc12a", "bc12b"], n_("D"), 2 * CW * GA)
+        S(act(b("D")[:], b("D")[:], AF.Abs), n_("D"), n_("D"), 2 * CW)
+        V(scan(b("R3")[:], T.d0m[:], b("D")[:], OP.add, OP.min), n_("D") + ["d0m"], n_("R3"), 2 * CW)
+        V(cp(b("soff")[:], b("R3")[:, 15::16]), n_("R3"), n_("soff"), 12)
+        win = T.tab[:, 0:2 * W]
+        V(tt(win.indirect(b("soff")[:, 0:6]), b("xk")[:], b("gt")[:], OP.mult), n_("soff", "xk", "gt") + TABX, TABX, CW * SCA)
+        V(cp(win.indirect(b("soff")[:, 6:12]), b("Bv")[:]), n_("soff", "Bv") + TABX, TABX, CW * SCA)
+        if late:
+            compare(OP.is_le, TAB)
+        V(tt(T.SO[:, k, 6, 0:6], T.MS[:, k, 6, 0:6], sf(1), OP.add), [Mx, "SOinit"] + n_("c4"), [SOn + "a"], 12)
+        TT = [D_ + "T0", D_ + "T1"]
+        S(act(b("nl")[:], b("xk")[:], AF.Relu, scale=-512.0), n_("xk"), n_("nl"), CW)
+        P([(pD[:, 6:12, :], T.idb[:], x, CW) for x in (Pv, b("e")[:], km, b("nl")[:])], n_("P", "e", "nl") + ["idb", "km"], TT[:1])
+        P([(pD[:, 12:18, :], T.idb[:], x, CW) for x in Tv] + [(pD[:, 12:18, :], T.nidb[:], b("nl")[:], CW)], n_("nl") + [Tn, "idb", "nidb"], TT[1:])
+        S(act(T.TS[:, k, :], pD[:, 6:18, :], AF.Relu), TT, ["TS%d" % k], 2 * CW)
+        cs = slice(CW * h, CW * h + CW)
+        if last:
+            V(tt(b("nl")[:], T.TS[:, k, 0:CW], T.TS[:, k, CW:C], OP.add), ["TS%d" % k], n_("nl"), 2 * CW)
+            store(T.ypic[:, cs], b("nl")[:], n_("nl"), 2000)
+            S(act(b("ax")[:, :, 0], T.SO[:, k, 6, 0:6], AF.Copy, scale=1.0 / 4096), [SOn + "a"] + n_("ax"), n_("ax"), 6)
+        else:
+            send(T.TS[:, k, :], T.TR[:, k + NH, :], "aT%d%s" % (v + 1, H), ["TS%d" % k], ["T%d%s" % (v + 1, H)])
+        X3 = 3 * CW
+        m1, m2, w1, w2 = b("m1"), b("m2"), b("w1"), b("w2")
+        ns = m1[:, 5:X3 + 3:3]
+        S(act(ns, b("R")[:], AF.Sigmoid, -5000.0), n_("R", "m1"), n_("ns"), CW)
+        S(act(m1[:, 1:X3:3], sf(0).indirect(T.bc6[:, 0:6]), AF.Relu, -8191.0), n_("xo", "m1") + ["bc6"], n_("nb"), CW * GA)
+        V(scan(w1[:, 0:X3], m1[:, 0:X3], pC[:, 0:X3], OP.mult, OP.add), n_("ns", "nb") + [C_ + "dm", C_ + "d2", C_ + "o"],
+          n_("w", "wa", "wb"), X3)
+        V(tt(sf(5), w1[:, 1:X3:48], T.MS[:, k, 0:6, 1], OP.add), n_("wa") + [M], n_("c5"), 12)
+        V(tt(sf(6), sf(1), si(2), OP.max), n_("c4", "Lk"), n_("c2"), 12)
+        V(tt(sf(7), sf(5), sf(6), OP.max), n_("c5", "c2"), n_("c3"), 12)
+        V(tt(w1[:, 1:X3:3], b("R3")[:].indirect(T.bcn[:, 0:6]), w1[:, 2:X3:3], OP.subtract), n_("R3", "w") + ["bcn"], n_("wa"), CW * GA)
+        V(tt(w1[:, 2:X3:48], b("R3")[:, 15:CW:16], sf(7), OP.min), n_("R3", "c3"), n_("w"), 12)
+        S(act(w1[:, 3:X3 + 3:3], w1[:, 1:X3:3], AF.Copy, scale=-1.0), n_("wa"), n_("wb"), CW)
+        P([(y2, T.idbig[:], ky, CW)] + count(6, b("SG")),
+          n_("SGa", "SG0_", "SG1_", "SG2_", "~B") + ["ky", "idbig", "sel", B_ + "P", B_ + "y1"], [B_ + "y2"], last=False)
+        count2(6, B_ + "y2")
+        V(tt(b("val")[:], y2, ns, OP.max), [B_ + "y2"] + n_("ns"), n_("val"), CW)
+        V(scan(b("U")[:], T.d0u[:], b("val")[:], OP.add, OP.min), n_("val") + ["d0u"], n_("U"), CW)
+        if KN["GES"]:
+            S(act(m2[:, 2:X3:3], b("U")[:], AF.Sigmoid, 128.0, -256.0), n_("U", "m2"), n_("ge"), CW)
+        else:
+            V(ts(m2[:, 2:X3:3], b("U")[:], 0.0, OP.is_le), n_("U", "m2"), n_("ge"), CW)
+        S(act(m2[:, 4:X3 + 2:3], b("U")[:], AF.Sigmoid, 128.0, -256.0), n_("U", "m2"), n_("gf"), CW)
+        V(scan(w2[:], m2[:, 0:X3], w1[:, 0:X3], OP.mult, OP.add), n_("ge", "gf", "w", "wa", "wb"), n_("w2"), X3)
+        S(act(T.SO[:, k, 0:6, 1:17], w2[:, 2:X3:3], AF.Copy), n_("w2") + ["SOinit"], [SOn], CW)
+        if not last:
+            send(T.SO[:, k], T.MS[:, k + NH], "aM%d%s" % (v + 1, H), [SOn, SOn + "a"],
+                 ["M%d%s" % (v + 1, H), "Mx%d%s" % (v + 1, H)])
+            return
+        turn(lambda j: b("ax")[:, j:6:2, :], D_, 0, n_("ax"), D_ + "fc", [D_ + "q1"])
+        V(tr(b("sh")[:], pD[:, 0:6, :]), [D_ + "fc0", D_ + "fc1"], n_("sh"), CW)
+        store(T.ycut[:, cs], b("sh")[0:128:16, :], n_("sh"), 2000)
+        turn(lambda j: T.SO[:, k, j:6:2, 1:17], D_, 6, [SOn], D_ + "fa", [D_ + "T0"])
+        V(tr(b("val")[:], pD[:, 6:12, :]), [D_ + "fa0", D_ + "fa1"], n_("val"), CW)
+        V(cp(T.lnam[:, cs], b("val")[:]), n_("val"), n_("fi") + ["lnam"], CW)
+        V(cp(b("U")[:], T.lnam[:, cs]), n_("fi"), n_("U"), CW)
+        store(T.ynam[:, cs], b("U")[:], n_("U"), 2000)
+        V(tt(b("R")[:], T.lnam[:, cs], b("val")[:], OP.is_equal), n_("fi", "val"), n_("R"), 2 * CW)
+        store(T.ymrk[:, cs], b("R")[:], n_("R"), 2000)
+
+    for v in range(NV):
+        for second in (False, True):
+            for h in range(NH):
+                a = len(ops)
+                part(v, h, second)
+                seen = {}
+                for o in ops[a:]:
+                    nm = o["e"] + "".join(c for c in (o["w"] + ["out"])[0] if not c.isdigit())
+                    seen[nm] = seen.get(nm, 0) + 1
+                    o["k"], o["v"] = "%s%d%d%d" % (nm, seen[nm], second, h), v
+    store(T.ydep[:, 0:2048], T.tab[:, 0:2048], ["tabA"], 4000)
+    store(T.ydep[:, 2048:W], T.tab[:, 2048:W], ["tabB"], 5000)
+    for i, o in enumerate(ops):
+        if "k" not in o:
+            o["k"], o["v"] = "i%d" % i, 0
+    return ops
+
+
+def keys(ops):
+    out = []
+    for o in ops:
+        if o["k"] not in out:
+            out.append(o["k"])
+    return out
+
+
+def order(ops):
+    n = len(ops)
+    lastw, readers, deps, succ = {}, {}, [], [[] for _ in ops]
+    for i, o in enumerate(ops):
+        d = set(lastw[x] for x in o["r"] + o["w"] if x in lastw)
+        for x in o["w"]:
+            d.update(readers.get(x, ()))
+        d.discard(i)
+        deps.append(d)
+        for j in d:
+            succ[j].append(i)
+        for x in o["r"]:
+            readers.setdefault(x, []).append(i)
+        for x in o["w"]:
+            lastw[x] = i
+            readers[x] = []
+    at = dict(zip(keys(ops), PLACE))
+    place = [10 * at[o["k"]] + PERIOD * o["v"] for o in ops]
+    left = [len(d) for d in deps]
+    ready = [i for i in range(n) if left[i] == 0]
+    free = {e: 0.0 for e in "vspgy"}
+    end, start = [0.0] * n, [0.0] * n
+    bank, locked, seq = {}, set(), []
+    while ready:
+        i = min((j for j in ready if ops[j]["e"] != "p" or ops[j]["lock"] == "close" or not any(x in locked for x in ops[j]["banks"])),
+                key=lambda j: (place[j], j))
+        o = ops[i]
+        ready.remove(i)
+        for x in o["banks"]:
+            deps[i].update(j for e, j in bank.get(x, {}).items() if e != o["e"])
+            bank.setdefault(x, {})[o["e"]] = i
+            if o["lock"] == "open":
+                locked.add(x)
+            if o["lock"] == "close":
+                locked.discard(x)
+        start[i] = max([free[o["e"]]] + [end[j] + KN["HOP"] for j in deps[i]])
+        end[i] = start[i] + o["ns"]
+        free[o["e"]] = start[i] + (o["ns"] if o["sem"] is None else (900 if o["e"] == "g" else 60))
+        seq.append(i)
+        for j in succ[i]:
+            left[j] -= 1
+            if left[j] == 0:
+                ready.append(j)
+    return seq, deps, start, max(end)
+
+
+PERIOD = 20000
+PLACE = []
+
+
+def greedy(ops):
+    n = len(ops)
+    HOP = KN["HOP"]
+    lastw, readers, deps, behind = {}, {}, [], []
+    for i, o in enumerate(ops):
+        d, s = set(), set()
+        for x in o["r"] + o["w"]:
+            if x in lastw:
+                (s if x[0] == "~" else d).add(lastw[x])
+        for x in o["w"]:
+            (s if x[0] == "~" else d).update(readers.get(x, ()))
+        if o["e"] == "p":
+            s.update(j for j in d if ops[j]["e"] == "p")
+            d = set(j for j in d if ops[j]["e"] != "p")
+        deps.append(d - {i})
+        behind.append((d | s) - {i})
+        for x in o["r"]:
+            readers.setdefault(x, []).append(i)
+        for x in o["w"]:
+            lastw[x] = i
+            readers[x] = []
+    succ = [[] for _ in ops]
+    for i in range(n):
+        for j in behind[i]:
+            succ[j].append(i)
+    prio = [0.0] * n
+    seed = KN["SEED"]
+    for i in range(n - 1, -1, -1):
+        seed = (seed * 1103515245 + 12345) % 2147483648
+        prio[i] = ops[i]["ns"] + HOP + max([prio[j] for j in succ[i]] or [0.0]) + KN["JIT"] * seed / 2147483648.0
+        if "SO%d0" % (NV - 1) in ops[i]["w"]:
+            prio[i] += KN["LEAD"]
+    left = [len(d) for d in behind]
+    ready = [i for i in range(n) if left[i] == 0]
+    free = {e: 0.0 for e in "vspgy"}
+    end, start = [0.0] * n, [0.0] * n
+    bank, locked, seq = {}, set(), []
+    while ready:
+        best = None
+        for i in ready:
+            o = ops[i]
+            if o["e"] == "p" and o["lock"] not in ("more", "close") and any(x in locked for x in o["banks"]):
+                continue
+            dep = set(deps[i])
+            for x in o["banks"]:
+                dep.update(j for e, j in bank.get(x, {}).items() if e != o["e"])
+            st = max([free[o["e"]]] + [end[j] + HOP for j in dep])
+            key = (st - KN["SLACK"] * prio[i] - BIAS.get(o.get("k"), 0), i)
+            if best is None or key < best[0]:
+                best = (key, i, st, dep)
+        _, i, st, dep = best
+        o = ops[i]
+        ready.remove(i)
+        deps[i], start[i] = dep, st
+        end[i] = st + o["ns"]
+        free[o["e"]] = st + (o["ns"] if o["sem"] is None else (900 if o["e"] == "g" else 60))
+        for x in o["banks"]:
+            bank.setdefault(x, {})[o["e"]] = i
+            if o["lock"] == "open":
+                locked.add(x)
+            if o["lock"] == "close":
+                locked.discard(x)
+        seq.append(i)
+        for j in succ[i]:
+            left[j] -= 1
+            if left[j] == 0:
+                ready.append(j)
+    return seq, deps, start, max(end)
+
+
+PLAN = []
+BIAS = {}
+
+
+def rank_program(g, core, T, topo):
+    rank = T.rank_of(core)
+    if rank is None:
+        return
+    ops = build(T, topo, core, rank)
+    if not PLAN:
+        PLAN.append(greedy(ops))
+    seq, deps, start, _ = PLAN[0]
+    queue = {"v": g.vector, "s": g.scalar, "p": g.tensor, "g": g, "y": g.sync}
+    count = {}
+    known = {e: {} for e in queue}
+    mark = {}
+    sent = 0
+    for i in seq:
+        o = ops[i]
+        e, q = o["e"], queue[o["e"]]
+        for j in sorted(deps[i], key=lambda j: -start[j]):
+            sem, val, seen = mark[j]
+            if known[e].get(sem, 0) < val:
+                q.wait_ge(T.sem[sem], val)
+                known[e][sem] = val
+                for s, x in seen.items():
+                    if known[e].get(s, 0) < x:
+                        known[e][s] = x
+        for f in o["f"]:
+            ins = f(q)
+        if o["sem"] is None:
+            ins.then_inc(T.sem[e], 1)
+            count[e] = count.get(e, 0) + 1
+            mark[i] = (e, count[e], dict(known[e]))
+        elif e == "g":
+            sent += KN["NE"]
+            count[o["sem"]] = KN["NE"]
+            mark[i] = (o["sem"], KN["NE"], {})
+        else:
+            ins.then_inc(T.sem[o["sem"]], 16)
+            count[o["sem"]] = count.get(o["sem"], 0) + 16
+            mark[i] = (o["sem"], count[o["sem"]], dict(known[e]))
+    count["sent"] = sent
+    for s, x in count.items():
+        g.sync.wait_ge(T.sem[s], x)

@@ -6,82 +6,98 @@ W, C, NV = 4096, 192, 5
 NH = 2
 MB = 6
 CW = 16 * MB
+SL = 17 * MB
+NK = (SL + 15) // 16
+SP = 16 * NK
 BIG = 1048576.0
-CAP = 4096.5
+K = 8192.0
+ZT, ZN = -8448.0, -16640.0
+STEP = 16384.0
+TRASH = 2 * W + 16
+TW = TRASH + 512 * MB
 f32, bf, i32, u16 = "float32", "bfloat16", "int32", "uint16"
-KN = {"SGV": 0, "GES": True, "LATE": 0, "GV": (3, 2), "SLACK": 0.02, "LEAD": 3000.0, "SEED": 0, "JIT": 0.0, "NE": 8,
-      "CY": 1.0, "PCY": 0.5, "HOP": 70.0, "GA": 1.56, "SCA": 3.8, "RT": 2600.0, "FV": 55.0, "FS": 70.0}
+KN = {"LQ": (("y", ("d0", "d1", "lo", "lp")), ("s", ("ln", "lm", "lt", "lw"))), "SQ": "yyyyys", "GV": (2, 1), "EG": True,
+      "LEAD": 1500.0, "WIN": 1.0, "DL": 1000.0, "BW": 500.0, "NE": 8, "ENC": "PPPPPPPP", "DEC": "svsv", "TS": True,
+      "C1": ((1, 6, "v"), (6, 11, "v"), (11, 16, "v")), "C2": ((1, 6, "v"), (6, 11, "v"), (11, 16, "s")),
+      "CB": (3, 3), "NP": 4, "SS": False, "NZ": 4, "GE": "ss", "HEAD": "s", "HP": 1, "ZP": False, "SO": "s", "FU": False, "XO": "p",
+      "CY": 0.83, "PCY": 0.44, "PSN": 0.5, "HOP": 215.0, "HS": 80.0, "LP": 150.0, "LS": 0.0, "LG": 2500.0, "DQ": 200.0, "GA": 1.56, "SCA": 3.8, "RT": 1500.0, "RW": 200.0,
+      "ISS": 600.0, "FV": 12.0, "FS": 40.0, "MX": 64,
+      "ALT": ({"CY": 1.1, "PCY": 0.55, "PSN": 1.0, "GA": 1.9, "SCA": 5.0, "RT": 2500.0, "HOP": 330.0, "HS": 120.0, "LG": 5000.0, "FS": 80.0, "FV": 40.0, "WT": 0.65},
+              {"PSN": 0.0, "RT": 1500.0, "HOP": 130.0, "HS": 60.0, "LP": 50.0, "FS": 90.0, "FV": 50.0, "MX": 0, "WT": 1.0}),
+      "BIAS": {"ik10": 5000.0, "iia00": 5000.0, "iones0": 5000.0}, "FB": 5, "FB0": 6, "MOVES": 4, "SEED": 1, "ITER": 4000, "JIT": 1000.0, "TEMP": 100.0}
 
 SCRATCH = {
-    "tab": ("sbuf", [128, 2 * W + 16], bf),
-    "MS": ("sbuf", [128, NV * NH, 7, 18], f32), "SO": ("sbuf", [128, NV * NH, 7, 18], f32),
-    "TR": ("sbuf", [128, NV * NH, C], bf), "TS": ("sbuf", [128, NV * NH, C], bf),
+    "tab": ("sbuf", [128, TW], bf), "raw": ("sbuf", [128, TW // 2], bf), "zr": ("sbuf", [128, 2, 512], bf),
+    "MS": ("sbuf", [128, NV * NH, MB, 20], f32), "SO": ("sbuf", [128, NV * NH, MB, 20], f32),
+    "TR": ("sbuf", [128, NV * NH, CW], bf), "TS": ("sbuf", [128, NV * NH, CW], bf),
     "lnam": ("sbuf", [128, C], i32), "lmrk": ("sbuf", [128, C], i32), "lown": ("sbuf", [128, C], i32),
     "lwt": ("sbuf", [128, 4], i32), "lthr": ("sbuf", [128, 8], i32),
     "a3": ("sbuf", [128, 6, 32], f32), "b3": ("sbuf", [128, 6, 32], f32), "tmp": ("sbuf", [128, C], f32),
     "ones": ("sbuf", [128, 160], f32), "wide": ("sbuf", [128, 160], f32), "wide0": ("sbuf", [128, 160], f32),
-    "wide1": ("sbuf", [128, 160], f32), "nidf": ("sbuf", [128, 128], f32),
-    "idb": ("sbuf", [128, 128], bf), "nidb": ("sbuf", [128, 128], bf), "idbig": ("sbuf", [128, 128], bf),
-    "idm256": ("sbuf", [128, 128], bf), "gm": ("sbuf", [128, 128], f32), "gm1": ("sbuf", [128, 128], f32),
-    "gms": ("sbuf", [128, 128], bf), "whi": ("sbuf", [128, 128], bf), "wlo": ("sbuf", [128, 128], bf),
-    "sel": ("sbuf", [128, 144], bf), "g8t": ("sbuf", [128, 256], f32),
-    "ci": ("sbuf", [128, 12, 8], i32), "cf": ("sbuf", [128, 12, 8], f32),
-    "ij": ("sbuf", [128, C], i32), "jj": ("sbuf", [128, C], f32),
-    "adiag": ("sbuf", [128, CW], f32), "d0r": ("sbuf", [128, CW], f32), "d0u": ("sbuf", [128, CW], f32),
-    "d0m": ("sbuf", [128, 2 * CW], f32), "key": ("sbuf", [128, 2 * CW], f32),
-    "kc": ("sbuf", [128, 6, CW], bf), "dth": ("sbuf", [128, NV, 128], bf),
-    "bc6": ("sbuf", [128, 6], u16), "bc12": ("sbuf", [128, 12], u16), "bcn": ("sbuf", [128, 6], u16),
+    "wide1": ("sbuf", [128, 160], f32), "nidf": ("sbuf", [128, 128], f32), "ids": ("sbuf", [128, 8, 128], bf),
+    "gm": ("sbuf", [128, 128], f32), "ia": ("sbuf", [128, 3, 160], i32),
+    "gmb": ("sbuf", [128, 128], bf), "whi": ("sbuf", [128, 128], bf), "wlo": ("sbuf", [128, 128], bf),
+    "sel": ("sbuf", [128, 2, 144], bf), "g8t": ("sbuf", [128, 256], f32),
+    "ci": ("sbuf", [128, 12, 8], i32), "cf": ("sbuf", [128, 16, 8], f32),
+    "ij": ("sbuf", [128, CW], i32), "jj": ("sbuf", [128, C], f32),
+    "adiag": ("sbuf", [128, CW], f32), "d0r": ("sbuf", [128, SL], f32), "d0u": ("sbuf", [128, SL], f32),
+    "key": ("sbuf", [128, SP], f32), "kc": ("sbuf", [128, 5, SP], bf), "kk": ("sbuf", [128, 512], bf),
+    "dth": ("sbuf", [128, NV, 128], bf), "out": ("sbuf", [128, 3, C], f32), "ls": ("sbuf", [128, 4, 8], u16),
 }
 PER_HALF = {
-    "G": ([6, 256], bf), "I": ([6, 256], bf), "SG": ([6, 256], bf), "off": ([CW + 2], u16), "offp": ([6], u16),
-    "xoff": ([6], u16), "soff": ([12], u16), "val": ([CW], f32), "R": ([CW], f32),
-    "sc": ([CW], f32), "sh": ([CW], f32), "oa": ([2 * CW], f32), "D": ([2 * CW], f32), "R3": ([2 * CW], f32),
-    "P": ([CW], bf), "xk": ([CW], bf), "gt": ([CW], bf), "B2": ([CW], bf), "Bv": ([CW], bf), "z": ([CW], bf),
-    "e": ([CW], bf), "nl": ([CW], bf), "tb": ([CW], bf),
-    "m1": ([3 * CW + 8], bf), "m2": ([3 * CW + 8], bf), "w1": ([3 * CW + 8], f32), "w2": ([3 * CW], f32), "U": ([CW], f32),
-    "si": ([8, 8], i32), "sf": ([8, 8], f32), "ax": ([6, 16], f32),
+    "G": ([MB, 256], bf), "I": ([MB, 256], bf), "off": ([CW + 2], u16), "Pe": ([CW], bf), "le": ([CW], bf), "offp": ([MB], u16),
+    "xoff": ([MB], u16), "soff": ([2 * MB], u16), "val": ([SL], f32), "R": ([SL], f32), "U": ([SL], f32),
+    "sc": ([CW], f32), "sh": ([CW], f32), "E": ([2, MB, 18], f32), "D": ([3, SL], f32), "Rn": ([2 * SL], f32), "Rh": ([SL], f32),
+    "P": ([CW], bf), "xk": ([CW], bf), "t": ([CW], bf), "FB": ([2 * CW], bf), "FC": ([2 * CW], bf), "Tc": ([CW], bf),
+    "p1": ([CW], bf), "sg": ([SL], bf), "nl": ([CW], bf), "tb": ([SP], bf), "keep": ([SP], f32),
+    "m1": ([3 * SP + 4], bf), "m2": ([3 * SP], bf), "w1": ([3 * SP + 4], f32), "w2": ([3 * SL], f32),
+    "si": ([8, 8], i32), "sf": ([8, 8], f32), "ax": ([MB, 16], f32),
 }
 for _h in range(NH):
     for _k, (_s, _d) in PER_HALF.items():
         SCRATCH[_k + str(_h)] = ("sbuf", [128] + _s, _d)
-    SCRATCH["pA%d" % _h] = ("psum", [128, 6, 80], f32)
-    SCRATCH["pB%d" % _h] = ("psum", [128, 32, 16], f32)
+    SCRATCH["pA%d" % _h] = ("psum", [128, 32, 16], f32)
+    SCRATCH["pB%d" % _h] = ("psum", [128, 30, 17], f32)
     SCRATCH["pC%d" % _h] = ("psum", [128, 512], f32)
-    SCRATCH["pD%d" % _h] = ("psum", [128, 32, 16], f32)
-LOADS = ["dA", "dB", "ln", "lm", "lo", "lp0", "lp1", "lw", "lt"]
+    SCRATCH["pE%d" % _h] = ("psum", [128, 32, 16], f32)
+ND = 2
+LOADS = ["d%d" % j for j in range(ND)] + ["ln", "lm", "lo", "lp", "lw", "lt"]
 SEMAPHORES = (["v", "s", "p", "g", "sent", "st"] + LOADS
               + ["a%s%d%d" % (k, v, h) for k in "MT" for v in range(1, NV) for h in range(NH)])
 
 
 def build(T, topo, core, rank):
     ops = []
-    CY, PCY, GA, SCA, SGV = KN["CY"], KN["PCY"], KN["GA"], KN["SCA"], KN["SGV"]
+    GA, SCA = "GA", "SCA"
 
-    def op(e, fs, r, w, ns, banks=(), lock=None, sem=None):
-        ops.append({"e": e, "f": fs if isinstance(fs, list) else [fs], "r": r, "w": w, "ns": ns,
-                    "banks": banks, "lock": lock, "sem": sem})
+    def op(e, fs, r, w, c, banks=(), lock=None, sem=None):
+        ops.append({"e": e, "f": fs if isinstance(fs, list) else [fs], "r": r, "w": w, "c": c,
+                    "banks": banks, "lock": lock, "sem": sem, "k": "i%s%d" % ((w + ["st"])[0], sum(o["w"][:1] == w[:1] for o in ops))})
 
     def bk(names):
-        return tuple(sorted(set(n[:3] for n in names if n[0] == "p" and n[1] in "ABCD")))
+        return tuple(sorted(set(n[:3] for n in names if n[0] == "p" and n[1] in "ABCE")))
 
-    def V(f, r, w, n):
-        op("v", f, r, w, KN["FV"] + n * CY, bk(r + w))
+    def V(f, r, w, n, rate="c"):
+        op("v", f, r, w, (rate, n), bk(r + w))
 
-    def S(f, r, w, n):
-        op("s", f, r, w, KN["FS"] + n * CY, bk(r + w))
+    def S(f, r, w, n, rate="c"):
+        op("s", f, r, w, ("q" if bk(r) else rate, n), bk(r + w))
 
     def G(f, r, w, n):
-        op("g", f, r, w, 170 + 2 * n * CY)
+        op("g", f, r, w, ("g", n))
+
+    def iota(o, pattern, base, cm, w, n):
+        G(lambda q: q.iota(o, pattern, base, cm, allow_small_or_imprecise_dtypes=True), [], w, n)
 
     def fill(o, c, w, n):
-        G(lambda q: q.iota(o, [[0, n]], c, 0, allow_small_or_imprecise_dtypes=True), [], w, n)
+        iota(o, [[0, n]], c, 0, w, n)
 
     def P(mm, r, w, first=True, last=True):
         fs, ns = [], 0
         for k, (o, l, x, cost) in enumerate(mm):
             fs.append(lambda q, o=o, l=l, x=x, a=(first and k == 0), b=(last and k == len(mm) - 1): q.matmul(o, l, x, a, b))
-            ns += cost * PCY
-        op("p", fs, r, w, ns + 20, bk(r + w), None if first and last else ("open" if first else "close" if last else "more"))
+            ns += max(64, cost)
+        op("p", fs, r, w, ("p", ns), bk(r + w), None if first and last else ("open" if first else "close" if last else "more"))
 
     def tt(o, a, b, f):
         return lambda q: q.tensor_tensor(o, a, b, f)
@@ -106,123 +122,173 @@ def build(T, topo, core, rank):
     def scan(o, a, b, f0, f1):
         return lambda q: q.tensor_tensor_scan(o, a, b, 0.0, f0, f1)
 
-    def load(e, name, o, i, w, ns):
-        op(e, lambda q: q.dma_start(o, i), [], w, ns, sem=name)
+    def load(e, name, o, i, w, by):
+        op(e, lambda q: q.dma_start(o, i), [], w + ["~load" + e], ("d", by), sem=name)
 
-    def store(o, i, r, ns):
-        op("y", lambda q: q.dma_start(o, i), r, [], ns, sem="st")
+    def store(o, i, r, by, e="y"):
+        op(e, lambda q: q.dma_start(o, i), r, [], ("d", by), sem="st")
 
-    load("y", "ln", T.lnam[:], T.nam[:], ["lnam"], 2000)
-    load("y", "lm", T.lmrk[:], T.mrk[:], ["lmrk"], 2000)
-    load("y", "dA", T.tab[:, 0:2048], T.dep[:, 0:2048], ["tabA"], 4000)
-    load("y", "dB", T.tab[:, 2048:W], T.dep[:, 2048:W], ["tabB"], 5000)
-    load("y", "lw", T.lwt[:, 0:1], T.wt[:], ["lwt"], 5200)
-    load("y", "lt", T.lthr[0:8, 0:5], T.thr[:], ["lthr"], 5200)
-    load("y", "lo", T.lown[:], T.own[:], ["lown"], 5400)
-    for h in range(NH):
-        load("y", "lp%d" % h, T.TR[:, h, 0:CW], T.pic[:, CW * h:CW * h + CW], ["T0%d" % h], 5400)
+    DW = W // ND
+    loads = {"ln": (T.lnam[:], T.nam[:], ["lnam"], 4 * C), "lm": (T.lmrk[:], T.mrk[:], ["lmrk"], 4 * C),
+             "lt": (T.lthr[0:8, 0:5], T.thr[:], ["lthr"], 4), "lp": (T.TR[:, 0:NH, :], T.pic[:], ["T00", "T01"], 2 * C),
+             "lw": (T.lwt[:, 0:1], T.wt[:], ["lwt"], 4), "lo": (T.lown[:], T.own[:], ["lown"], 4 * C)}
+    for j in range(ND):
+        loads["d%d" % j] = (T.raw[:, DW * j:DW * j + DW], T.dep[:, DW * j:DW * j + DW], ["raw%d" % j], 2 * DW)
+    for e, names in KN["LQ"]:
+        for name in names:
+            load(e, name, *loads[name])
 
     idf, nidf = T.wide[:, 16:144], T.nidf[:]
     col = lambda k: T.cf[:, k, 0:1]
     PM, PM1, SCL, H0, H1, WH, WL = range(7)
-    kh, ks, ky, kr, k1, km = (T.kc[:, k, :] for k in range(6))
+    kh, ks, ky, kz, k1 = range(5)
+    kc = lambda k, n=CW: T.kc[:, k, 0:n]
+    scales = {"id": 1.0, "nid": -1.0, "id2k": 2 * K, "ida": 255.0 / 256, "nk": -K, "big": BIG, "nbig": -BIG}
+    if not KN["FU"]:
+        del scales["nk"]
+        scales.update({"idc": 256 * K, "idd": -255 * K})
+    I = {n: T.ids[:, j, :] for j, n in enumerate(scales)}
     V(ms(T.ones[:], 1.0), [], ["ones"], 160)
-    G(lambda q: q.iota(T.ci[:, 0, 0:1], [[0, 1]], 0, 1), [], ["ci0"], 1)
-    G(lambda q: q.affine_select(T.wide[:], T.ones[:], [[-1, 160]], OP.is_equal, 0.0, 16, 1), ["ones"], ["wide"], 160)
-    V(ts(T.ci[:, 1, 0:1], T.ci[:, 0, 0:1], 16, OP.bitwise_and), ["ci0"], ["ci1"], 1)
+    G(lambda q: q.iota(T.ia[:, 0, :], [[-1, 160]], 16, 1), [], ["ia0"], 160)
+    V(ts(T.wide[:], T.ia[:, 0, :], 0.0, OP.is_equal), ["ia0"], ["wide"], 160)
+    V(ms(T.kk[:], K), [], ["kk"], 256)
+    V(ms(T.tab[:, 1:2 * W:2], ZT), [], ["tabZ"], W // 2)
+    fill(T.tab[:, 2 * W:TRASH], int(ZN), ["tabN"], 16)
+    V(ts(T.ci[:, 1, 0:1], T.ia[:, 0, 16:17], 16, OP.bitwise_and), ["ia0"], ["ci1"], 1)
     V(ts(col(H1), T.ci[:, 1, 0:1], 0.0625, OP.mult), ["ci1"], ["H1"], 1)
     V(ts(col(H0), T.ci[:, 1, 0:1], -0.0625, OP.mult, 1.0, OP.add), ["ci1"], ["H0"], 1)
-    V(ts(T.wide0[:], T.wide[:], col(H0), OP.mult), ["wide", "H0"], ["wide0"], 160)
-    V(ts(T.wide1[:], T.wide[:], col(H1), OP.mult), ["wide", "H1"], ["wide1"], 160)
+    S(act(T.wide0[:], T.wide[:], AF.Identity, scale=col(H0)), ["wide", "H0"], ["wide0"], 160)
+    S(act(T.wide1[:], T.wide[:], AF.Identity, scale=col(H1)), ["wide", "H1"], ["wide1"], 160)
     swap = {(0, 0): T.wide0[:, 16:144], (0, 1): T.wide0[:, 0:128], (1, 0): T.wide1[:, 32:160], (1, 1): T.wide1[:, 16:144]}
-    S(act(T.idb[:], idf, AF.Sigmoid, -128.0, 256.0), ["wide"], ["idb"], 1400)
-    S(act(T.nidb[:], idf, AF.Copy, scale=-1.0), ["wide"], ["nidb"], 128)
+    for n, c in scales.items():
+        S(act(I[n], idf, AF.Copy, scale=c), ["wide"], [n], 128)
     S(act(T.nidf[:], idf, AF.Copy, scale=-1.0), ["wide"], ["nidf"], 128)
-    S(act(T.idbig[:], idf, AF.Copy, scale=-BIG), ["wide"], ["idbig"], 128)
-    S(act(T.idm256[:], idf, AF.Copy, scale=-256.0), ["wide"], ["idm256"], 128)
-    G(lambda q: q.affine_select(T.gm1[:], T.ones[:, 0:128], [[-16, 8], [0, 16]], OP.is_ge, 0.0, 0, 1), ["ones"], ["gm1"], 128)
-    G(lambda q: q.affine_select(T.gm[:], T.gm1[:], [[16, 8], [0, 16]], OP.is_ge, 0.0, 15, -1), ["gm1"], ["gm"], 128)
-    V(ms(T.sel[:], 0.0), [], ["sel"], 72)
-    V(ts(T.sel[:, 15:143:16], T.gm[:, 0::16], -BIG, OP.mult), ["gm", "sel"], ["sel"], 8)
-    S(act(T.gms[:], T.gm[:], AF.Copy, scale=16384.0), ["gm"], ["gms"], 128)
+    G(lambda q: q.iota(T.ia[:, 1, 0:128], [[-16, 8], [0, 16]], 0, 1), [], ["ia1"], 128)
+    V(ts(T.ia[:, 1, 0:128], T.ia[:, 1, 0:128], -16, OP.bitwise_and), ["ia1"], ["ia1"], 128)
+    V(ts(T.gm[:], T.ia[:, 1, 0:128], 0.0, OP.is_equal), ["ia1"], ["gm"], 128)
+    fill(T.sel[:], 0, ["sel"], 288)
+    S(act(kc(k1, SL), T.ones[:, 0:SL], AF.Sigmoid, scale=256.0), ["ones"], ["k1", "~first"], 1650)
+    V(ts(T.sel[:, 0, 15:143:16], T.gm[:, 0::16], -BIG, OP.mult), ["gm", "sel"], ["sel0"], 8)
+    V(ts(T.sel[:, 1, 15:143:16], T.gm[:, 0::16], -BIG / K, OP.mult), ["gm", "sel"], ["sel1"], 8)
+    S(act(T.gmb[:], T.gm[:], AF.Copy), ["gm"], ["gmb"], 128)
     V(ts(T.ci[:, 2, 0:1], T.lwt[:, 0:1], 3840, OP.bitwise_and), ["lwt"], ["ci2"], 1)
-    V(ts(T.ci[:, 3, 0:1], T.lwt[:, 0:1], 255, OP.bitwise_and), ["lwt"], ["ci3"], 1)
-    V(cp(col(WH), T.ci[:, 2, 0:1]), ["ci2"], ["WH"], 1)
-    V(cp(col(WL), T.ci[:, 3, 0:1]), ["ci3"], ["WL"], 1)
-    S(act(T.whi[:], T.gm[:], AF.Identity, scale=col(WH)), ["gm", "WH"], ["whi"], 128)
-    S(act(T.wlo[:], T.gm[:], AF.Identity, scale=col(WL)), ["gm", "WL"], ["wlo"], 128)
-    G(lambda q: q.affine_select(T.g8t[0:8, 128:256], T.ones[0:8, 0:128], [[1, 128]], OP.is_ge, 0.0, 0, -16), ["ones"], ["g8u"], 128)
-    G(lambda q: q.affine_select(T.g8t[0:8, 0:128], T.g8t[0:8, 128:256], [[-1, 128]], OP.is_ge, 0.0, 15, 16), ["g8u"], ["g8t"], 128)
+    V(ts(T.ci[:, 2, 1:2], T.lwt[:, 0:1], 255, OP.bitwise_and), ["lwt"], ["ci3"], 1)
+    V(cp(T.cf[:, WH, 0:2], T.ci[:, 2, 0:2]), ["ci2", "ci3"], ["WH"], 1)
+    S(act(T.whi[:], T.gm[:], AF.Identity, scale=T.cf[:, WH, 0:1]), ["gm", "WH"], ["whi"], 128)
+    S(act(T.wlo[:], T.gm[:], AF.Identity, scale=T.cf[:, WH, 1:2]), ["gm", "WH"], ["wlo"], 128)
+    G(lambda q: q.iota(T.ia[0:8, 2, 0:128], [[1, 128]], 0, -16), [], ["ia2"], 128)
+    V(ts(T.ia[0:8, 2, 0:128], T.ia[0:8, 2, 0:128], -16, OP.bitwise_and), ["ia2"], ["ia2"], 128)
+    V(ts(T.g8t[0:8, 0:128], T.ia[0:8, 2, 0:128], 0.0, OP.is_equal), ["ia2"], ["g8t"], 128)
     V(cp(T.cf[0:8, 8, 0:5], T.lthr[0:8, 0:5]), ["lthr"], ["cf8"], 5)
-    P([(T.pC0[:, 480:485], T.g8t[0:8, 0:128], T.cf[0:8, 8, 0:5], 256)], ["g8t", "cf8"], ["pC0thr"])
-    V(ts(T.cf[:, 9, 0:1], T.pC0[:, 480:481], -0.5, OP.add, BIG, OP.mult), ["pC0thr"], ["thr0"], 1)
-    V(ts(T.cf[:, 9, 1:5], T.pC0[:, 481:485], 0.5, OP.add, BIG, OP.mult), ["pC0thr"], ["thrc"], 4)
+    P([(T.pB1[:, 29, 0:5], T.g8t[0:8, 0:128], T.cf[0:8, 8, 0:5], 256)], ["g8t", "cf8"], ["pB1thr"])
+    V(ts(T.cf[:, 9, 0:5], T.pB1[:, 29, 0:5], -0.5, OP.add, BIG, OP.mult), ["pB1thr"], ["thr"], 5)
+    V(ts(T.cf[:, 9, 2:5:2], T.pB1[:, 29, 2:5:2], 0.5, OP.add, BIG, OP.mult), ["pB1thr", "thr"], ["thr"], 2)
     for v in range(NV):
-        S(act(T.dth[:, v, :], idf, AF.Identity, scale=T.cf[:, 9, v:v + 1]), ["wide", "thrc" if v else "thr0"], ["dth%d" % v], 128)
-    G(lambda q: q.iota(T.ij[:, 0:CW], [[0, 6], [1, 16]], 0, 0), [], ["ij"], CW)
-    G(lambda q: q.iota(T.ij[:, CW:C], [[0, 6], [-8, 2], [1, 8]], 8, 0), [], ["ij2"], CW)
-    V(ts(T.ci[:, 4, 0:1], T.ci[:, 0, 0:1], 15, OP.bitwise_and), ["ci0"], ["ci4"], 1)
+        S(act(T.dth[:, v, :], idf, AF.Identity, scale=T.cf[:, 9, v:v + 1]), ["wide", "thr"], ["dth%d" % v], 128)
+    G(lambda q: q.iota(T.ij[:], [[0, MB], [1, 16]], 0, 0), [], ["ij"], CW)
+    V(ts(T.ci[:, 4, 0:1], T.ia[:, 0, 16:17], 15, OP.bitwise_and), ["ia0"], ["ci4"], 1)
     V(cp(col(PM), T.ci[:, 4, 0:1]), ["ci4"], ["PM"], 1)
     V(ts(col(PM1), T.ci[:, 4, 0:1], 1.0, OP.add), ["ci4"], ["PM1"], 1)
-    V(ts(T.cf[:, 7, 0:1], T.ci[:, 4, 0:1], 15.0, OP.is_equal, 1.0 - 2.0 ** -13, OP.mult), ["ci4"], ["cf7"], 1)
-    V(ts(col(SCL), T.cf[:, 7, 0:1], 2.0 ** -13, OP.add), ["cf7"], ["SCL"], 1)
-    V(ts(T.jj[:, 0:CW], T.ij[:, 0:CW], col(PM), OP.not_equal), ["ij", "PM"], ["jj"], CW)
-    V(ts(T.jj[:, CW:C], T.ij[:, 0:CW], col(PM1), OP.is_equal, 8191.0, OP.mult), ["ij", "PM1"], ["jt"], CW)
+    V(ts(col(SCL), T.ci[:, 4, 0:1], 15.0, OP.is_equal, 2.0 ** -13, OP.max), ["ci4"], ["SCL"], 1)
+    V(ts(T.jj[:, 0:CW], T.ij[:], col(PM), OP.not_equal), ["ij", "PM"], ["jj"], CW)
+    V(ts(T.jj[:, CW:C], T.ij[:], col(PM1), OP.is_equal, 8191.0, OP.mult), ["ij", "PM1"], ["jt"], CW)
     V(tt(T.adiag[:], T.jj[:, 0:CW], T.jj[:, CW:C], OP.add), ["jj", "jt"], ["adiag"], 2 * CW)
-    for nm, c0, wd in (("d0r", -4096.0, CW), ("d0u", -1.0, CW), ("d0m", 0.0, C)):
-        V(ms(T[nm][:], c0), [], [nm], wd)
-        V(ms(T[nm][:, 0::16], BIG), [nm], [nm], 12)
-    V(ts(T.key[:], T.ij[:], 16384.0, OP.mult, 4096.25, OP.add), ["ij", "ij2"], ["key"], C)
-    fill(kh, 4096, ["kh"], CW)
-    fill(ks, 524288, ["ks"], CW)
-    V(ms(ky, -17.5), [], ["ky"], 48)
-    fill(k1, 1, ["k1"], CW)
-    fill(km, -512, ["km"], CW)
-    G(lambda q: q.iota(kr, [[0, 6], [-4096, 16]], 0, 0, allow_small_or_imprecise_dtypes=True), [], ["kr"], CW)
-    G(lambda q: q.iota(T.ci[:, 5, 0:6], [[1, 6]], 0, 0), [], ["ci5"], 6)
-    V(cp(T.bc6[:], T.ci[:, 5, 0:6]), ["ci5"], ["bc6"], 6)
-    V(cp(T.bc12[:, 0:6], T.ci[:, 5, 0:6]), ["ci5"], ["bc12a"], 6)
-    V(cp(T.bc12[:, 6:12], T.ci[:, 5, 0:6]), ["ci5"], ["bc12b"], 6)
-    V(ts(T.bcn[:], T.ci[:, 5, 0:6], 16.0, OP.mult, CW + 15.0, OP.add), ["ci5"], ["bcn"], 6)
-    for j, nm in enumerate(("tabC", "tabD", "tabF", "tabG")):
-        fill(T.tab[:, W + 1024 * j:W + 1024 * j + 1024], 0, [nm], 1024)
-    fill(T.tab[:, 2 * W:2 * W + 16], -1, ["tabE"], 16)
-    fill(T.SO[:], 0, ["SOinit"], NV * NH * 126)
+    for H in map(str, range(NH)):
+        fill(T["m1" + H][:, 1:3 * SL:3], 0, ["m1" + H], SL)
+        V(ms(T["m1" + H][:, 1:3 * SL:51], 1.0), ["m1" + H], ["m1" + H], MB)
+    for nm, c0 in (("d0r", -int(STEP)), ("d0u", -1)):
+        fill(T[nm][:], c0, [nm], SL)
+        V(ms(T[nm][:, 0::17], BIG), [nm], [nm], MB)
+    fill(T.key[:, SL:SP], 0, ["kez"], SP - SL)
+    iota(T.key[:, 0:SL], [[0, MB], [1, 17]], -1, 0, ["key"], SL)
+    fill(kc(kh), 4096, ["kh"], CW)
+    fill(kc(ks), 524288, ["ks"], CW)
+    V(ms(kc(ky, SL), 1.75), [], ["ky"], SL // 2)
+    fill(kc(kz), int(-ZN), ["kz"], CW)
+    cf = lambda k: T.cf[:, k, 0:NK]
+    iota(cf(10), [[16, NK]], 0, 0, ["l0"], NK)
+    V(ts(cf(11), cf(10), col(PM), OP.add), ["l0", "PM"], ["lj"], NK)
+    V(ts(T.ci[:, 5, 0:NK], cf(11), -8.0, OP.add, 1.0 / 17, OP.mult), ["lj"], ["lb"], NK)
+    V(ts(cf(12), T.ci[:, 5, 0:NK], 17.0, OP.mult), ["lb"], ["l17"], NK)
+    V(tt(cf(13), cf(12), cf(11), OP.is_equal), ["l17", "lj"], ["le"], NK)
+    V(ts(cf(14), cf(13), float(MB), OP.mult), ["le"], ["lf"], NK)
+    V(tt(cf(15), cf(14), T.ci[:, 5, 0:NK], OP.max), ["lf", "lb"], ["lg"], NK)
+    Lk, Lb, Le, Lf = (T.ls[:, j, 0:NK] for j in range(4))
+    V(ts(Lk, cf(15), float(MB), OP.min), ["lg"], ["Lk"], NK)
+    V(ts(Lb, T.ci[:, 5, 0:NK], MB - 1.0, OP.min), ["lb"], ["Lb"], NK)
+    V(ts(Le, Lb, 17.0, OP.mult, 16.0, OP.add), ["Lb"], ["Le"], NK)
+    V(ts(Lf, Lb, 17.0, OP.mult, SL + 16.0, OP.add), ["Lb"], ["Lf"], NK)
     for h in range(NH):
         H = str(h)
+        fill(T.MS[:, h], 0, ["M0" + H, "Mx0" + H], 20 * MB)
+        fill(T["m1" + H][:, 0:1], 0, ["m0" + H], 1)
+        fill(T["w1" + H][:], 0, ["w" + H], 3 * SP + 4)
+        if KN["ZP"]:
+            fill(T["w2" + H][:, 0:SL + 1:SL], 0, ["w2z" + H], 2)
+        else:
+            fill(T["m2" + H][:], 0, ["m2" + H], 3 * SP)
+        fill(T["E" + H][:, :, :, 17], 0, ["Ez" + H], 2 * MB)
+        iota(T["E" + H][:, :, :, 0], [[256, 2 * MB]], TRASH, 2, ["Et" + H], 2 * MB)
+        G(lambda q, H=H: q.iota(T["si" + H][:, 6, MB:MB + 1], [[0, 1]], -1, 0), [], ["sk" + H], 1)
         fill(T["ax" + H][:], 0, ["ax" + H], CW)
-        V(ms(T.MS[:, h, :, 0], 0.0), [], ["Mx0" + H], 7)
-        V(ms(T.MS[:, h, 6, 0:6], 0.0), ["Mx0" + H], ["Mx0" + H], 6)
-        fill(T["m1" + H][:], 0, ["m1" + H], 3 * CW + 8)
-        fill(T["m2" + H][:], 0, ["m2" + H], 3 * CW + 8)
+    for v in range(NV):
+        fill(T.SO[:, NH * v:NH * v + NH], 0, ["SOi%d" % v], NH * 20 * MB)
 
-    def turn(src, bank, slot, r, w, alias=()):
+    TAB = ["tab%d" % j for j in range(8)]
+    for j, how in enumerate(KN["ENC"]):
+        x, xn = T.raw[:, 512 * j:512 * j + 512], "raw%d" % (512 * j // DW)
+        o = T.tab[:, 1024 * j:1024 * j + 1024:2]
+        bank = ("pA0", "pE0", "pA1", "pE1")[j % 4]
+        if how == "P":
+            S(act(T[bank][:], x, AF.Identity, -K, 2 * K), [xn], [bank], 512)
+            V(tt(o, x, T[bank][:], OP.min), [xn, bank, "tabZ"], [TAB[j]], 512)
+        elif how == "V":
+            P([(T[bank][:], I["id2k"], x, 512), (T[bank][:], I["nid"], T.kk[:], 512)], [xn, "id2k", "nid", "kk"], [bank])
+            V(tt(o, x, T[bank][:], OP.min), [xn, bank, "tabZ"], [TAB[j]], 512)
+        else:
+            z, zn = T.zr[:, j % 2, :], "zr%d" % (j % 2)
+            if how == "S":
+                S(act(z, x, AF.Relu, K, -2 * K), [xn], [zn], 512)
+            else:
+                V(ts(z, x, 0.0, OP.is_equal, K, OP.mult), [xn], [zn], 256)
+            P([(T[bank][:], I["id"], x, 512), (T[bank][:], I["nid"], z, 512)], [xn, zn, "id", "nid"], [bank])
+            S(act(o, T[bank][:], AF.Copy), [bank, "tabZ"], [TAB[j]], 512)
+    TAB = TAB + ["tabZ"]
+
+    def turn(src, bank, slot, r, w):
         for o in range(2):
-            P([(T[bank][:, slot + o:slot + 6:2, :], swap[(o, k)], src(k), 256) for k in range(2)],
-              r + ["wide0", "wide1"], [w + str(o)] + list(alias))
+            P([(T[bank][:, slot + o:slot + MB:2, :], swap[(o, k)], src(k), 256) for k in range(2)],
+              r + ["wide0", "wide1"], [w])
 
-    V(ts(T.tmp[:], T.lmrk[:], -0.25, OP.mult, 0.25, OP.add), ["lmrk"], ["tmp"], C)
+    V(ts(T.tmp[:], T.lmrk[:], -0.1875, OP.mult, 0.1875, OP.add), ["lmrk"], ["tmp"], C)
     V(tt(T.a3[:], T.tmp[:], T.lnam[:], OP.add), ["tmp", "lnam"], ["a3"], 2 * C)
     V(cp(T.b3[:], T.lown[:]), ["lown"], ["b3"], C)
     for h in range(NH):
         H = str(h)
-        turn(lambda k: T.a3[:, 3 * h:3 * h + 3, 16 * k:16 * k + 16], "pD" + H, 18, ["a3"], "pD%snew" % H)
-        V(tr(T["R" + H][:], T["pD" + H][:, 18:24, :]), ["pD%snew0" % H, "pD%snew1" % H], ["R" + H], CW)
-        V(cp(T.MS[:, h, 0:6, 1:17], T["R" + H][:]), ["R" + H], ["M0" + H], CW)
-        turn(lambda k: T.b3[:, 3 * h:3 * h + 3, 16 * k:16 * k + 16], "pD" + H, 12, ["b3"], "pD%sT" % H)
-        V(tr(T["U" + H][:], T["pD" + H][:, 12:18, :]), ["pD%sT0" % H, "pD%sT1" % H], ["U" + H], CW)
-        for k in range(2):
-            V(tt(T["oa" + H][:, CW * k:CW * k + CW], T["U" + H][:], T.key[:, CW * k:CW * k + CW], OP.add),
-              ["U" + H, "key"], ["oa%d%s" % (k, H)], 2 * CW)
+        E, D = T["E" + H], T["D" + H]
+        turn(lambda k: T.a3[:, 3 * h:3 * h + 3, 16 * k:16 * k + 16], "pE" + H, 0, ["a3"], "pE" + H)
+        V(tr(T["sc" + H][:], T["pE" + H][:, 0:MB, :]), ["pE" + H], ["sc" + H], CW)
+        S(act(T.MS[:, h, 0:MB, 1:17], T["sc" + H][:], AF.Copy, scale=2.0), ["sc" + H], ["M0" + H], CW)
+        turn(lambda k: T.b3[:, 3 * h:3 * h + 3, 16 * k:16 * k + 16], "pE" + H, 0, ["b3"], "pE" + H)
+        V(tr(T["sh" + H][:], T["pE" + H][:, 0:MB, :]), ["pE" + H], ["sh" + H], CW)
+        S(act(E[:, 0, :, 1:17], T["sh" + H][:], AF.Identity, 0.375, 2.0), ["sh" + H], ["E" + H], CW)
+        S(act(E[:, 1, :, 1:9], E[:, 0, :, 9:17], AF.Copy), ["E" + H], ["Ea" + H], CW // 2)
+        S(act(E[:, 1, :, 9:17], E[:, 0, :, 1:9], AF.Copy), ["E" + H], ["Eb" + H], CW // 2)
+        S(act(T["sf" + H][:, 7, 0:MB], E[:, 0, :, 1], AF.Identity, 1.0), ["E" + H], ["c1" + H], MB)
+        for j in range(2):
+            pd, pn = T["pB" + H][:, (2 + j) * MB:(3 + j) * MB, :], "pB%sd%d" % (H, j)
+            P([(pd, idf, E[:, j, :, 0:17], 4 * SL), (pd, nidf, E[:, j, :, 1:18], 4 * SL)],
+              ["E" + H, "Ea" + H, "Eb" + H, "Ez" + H, "Et" + H, "wide", "nidf"], [pn])
+            for i in (0, 2)[:2 - j]:
+                S(act(D[:, j + i, :], pd, AF.Copy), [pn], ["D%d%s" % (j + i, H)], SL)
 
     nxt = T.cores[(rank + 1) % len(T.cores)]
     rid, pid, _ = topo.addr(nxt)
     emask = sum(1 << e for e in topo.engines(core, nxt)[:KN["NE"]])
-    TAB = ["tabA", "tabB"]
-    TABX = ["tabA", "tabB", "tabC", "tabD", "tabF", "tabG"]
+    RAW = ["raw%d" % j for j in range(ND)]
 
-    def send(src, dst, sem, r, w):
-        op("g", lambda q: q.remote_dma(dst, src, T.sem[sem], T.sem.sent, pid, rid, emask), r, w, KN["RT"], sem=sem)
+    def send(src, dst, sem, r, w, by):
+        op("g", lambda q: q.remote_dma(dst, src, T.sem[sem], T.sem.sent, pid, rid, emask), r, w, ("r", by), sem=sem)
 
     def part(v, h, second):
         H = str(h)
@@ -231,234 +297,241 @@ def build(T, topo, core, rank):
         k = v * NH + h
         last = v == NV - 1
         M, Mx, Tn, SOn = "M%d%s" % (v, H), "Mx%d%s" % (v, H), "T%d%s" % (v, H), "SO%d%s" % (v, H)
-        o, o0, o1 = T.MS[:, k, 0:6, 1:17], T.MS[:, k, 0:6, 0:16], T.MS[:, k, 0:6, 2:18]
-        Gs = ["G%d%s" % (m, H) for m in range(MB)]
-        Pv, Tv = b("P")[:], [T.TR[:, k, 0:CW], T.TR[:, k, CW:C]][:2 if v else 1]
-        pA, pB, pC, pD = b("pA"), b("pB"), b("pC"), b("pD")
-        A_, B_, C_, D_ = "pA" + H, "pB" + H, "pC" + H, "pD" + H
-        As = [A_ + str(x) for x in range(5)]
-        pp, sr, hr = pB[:, 12:18, :], pC[:, 3 * CW:4 * CW], pC[:, 4 * CW:5 * CW]
-        y1, y2 = pB[:, 0:6, :], pB[:, 6:12, :]
-        si = lambda j: b("si")[:, j, 0:6]
-        sf = lambda j: b("sf")[:, j, 0:6]
+        o0, o, o1 = T.MS[:, k, 0:MB, 0:17], T.MS[:, k, 0:MB, 1:18], T.MS[:, k, 0:MB, 2:19]
+        Gs = ["G%d_%s" % (m, H) for m in range(MB)]
+        Pv, Pe, Tv, xk = b("P")[:], b("Pe")[:], T.TR[:, k, :], b("xk")[:]
+        pA, pB, pC, pE = b("pA"), b("pB"), b("pC"), b("pE")
+        A_, B_, C_, E_ = "pA" + H, "pB" + H, "pC" + H, "pE" + H
+        X3 = 3 * SL
+        c1, c2 = pC[:, 512 - CW:512], pC[:, 512 - 2 * CW:512 - CW]
+        y1, y2 = pB[:, 0:MB, :], pB[:, MB:2 * MB, :]
+        si = lambda j: b("si")[:, j, 0:MB]
+        sf = lambda j: b("sf")[:, j, 0:MB]
+        m1, m2, w1, w2 = b("m1"), b("m2"), b("w1"), b("w2")
+        ns = m1[:, 3:X3 + 1:3]
 
-        def compare(f, after=[]):
-            for j in range(3):
-                a = 16 + 80 * j
-                V(tt(b("I")[:, :, a:a + 80], b("G")[:, :, a:a + 80], pA[:], f), Gs + As + after + n_("~I"), n_("I%d_" % j, "~I"), 480)
+        def compare(pieces, x, xr, ix, f, sign):
+            n = max([r1 - r0 for r0, r1, e in pieces if e == "v"] or [0])
+            if n:
+                P([(pA[:, j:n * MB:n, :], I[ix[0]], x, CW) for j in range(n)], xr + [ix[0]], [A_])
+            used = 0
+            for r0, r1, e in pieces:
+                E_ = "pE%d" % ((h + used) % NH)
+                pE, used = T[E_], used + (e == "s")
+                d, Gp, Ip = r1 - r0, b("G")[:, :, 16 * r0:16 * r1], b("I")[:, :, 16 * r0:16 * r1]
+                In = n_(*["I%d_%d_" % (r0, m) for m in range(MB)])
+                if e == "v":
+                    assert d == n
+                    cb = KN["CB"][second]
+                    for m0 in range(0, MB, cb):
+                        m1_ = m0 + cb
+                        V(tt(b("I")[:, m0:m1_, 16 * r0:16 * r1], b("G")[:, m0:m1_, 16 * r0:16 * r1], pA[:, n * m0:n * m1_, :], f),
+                          Gs[m0:m1_] + [A_], In[m0:m1_], d * 16 * cb)
+                else:
+                    mx, mg = [(pE[:, j:d * MB:d, :], I[ix[1]], x, CW) for j in range(d)], [(pE[:, 0:d * MB, :], I[ix[2]], Gp, d * CW)]
+                    if sign[0]:
+                        P(mx, xr + [ix[1]], [E_], last=False)
+                        P(mg, Gs + [ix[2], E_], [E_], first=False)
+                    elif KN["EG"]:
+                        P(mg, Gs + [ix[2]], [E_], last=False)
+                        P(mx, xr + [ix[1], E_], [E_], first=False)
+                    else:
+                        P(mx + mg, xr + Gs + list(ix[1:]), [E_])
+                    S(act(Ip, pE[:, 0:d * MB, :], AF.Sigmoid, *sign), [E_], In, d * CW)
 
-        def count(y, x, r0=1, r1=16):
-            return [(pB[:, y:y + 6, r0:r1], T.sel[:, 15 - i:143 - i], x[:, :, 16 * r0 + i:16 * r1:16], max(64, 6 * (r1 - r0))) for i in range(16)]
+        def count(y, x, j, r0=1, r1=16):
+            return [(pB[:, y:y + MB, r0 + 1:r1 + 1], T.sel[:, j, 15 - i:143 - i], x[:, :, 16 * r0 + i:16 * r1:16], MB * (r1 - r0)) for i in range(16)]
 
-        def count2(y, name):
-            P(count(y, b("I"), 1, 11), n_("I0_", "I1_") + ["sel", name], [name], first=False, last=False)
-            P(count(y, b("I"), 11, 16), n_("I2_") + ["sel", name], [name], first=False)
+        def counts(y, name, pieces):
+            mm, step = count(y, b("I"), 0), 16 // KN["NP"]
+            for j in range(0, 16, step):
+                P(mm[j:j + step], n_(*["I%d_%d_" % (r0, m) for r0, r1, e in pieces for m in range(MB)]) + ["sel0", name], [name],
+                  first=False, last=j + step == 16)
 
         if not second:
-            V(cp(b("offp")[:], T.MS[:, k, 0:6, 1]), [M], n_("offp"), 6)
-            V(cp(b("off")[:, 1:CW + 1], o), [M], n_("off"), CW)
-            S(act(Pv, T.tab[:, 0:W].indirect(b("offp")[:, 0:6]), AF.Copy), TAB + n_("offp"), n_("P", "~G"), CW * GA)
+            V(cp(b("offp")[:], T.MS[:, k, 0:MB, 1]), [M], n_("offp"), MB)
+            win = T.tab[:, 0:2 * W]
+            S(act(Pv, win.indirect(b("offp")[:, 0:MB]), AF.Abs), TAB + n_("offp"), n_("P"), CW, GA)
+            V(cp(b("off")[:, 1:CW + 1], T.MS[:, k, 0:MB, 1:17]), [M], n_("off"), CW)
             for m in range(MB):
-                if m >= MB - KN["GV"][h]:
-                    V(cp(b("G")[:, m, 16:256], T.tab[:, 0:W].indirect(b("off")[:, 16 * m + 2:16 * m + 17])), TAB + n_("off"), [Gs[m]], 240 * GA)
-                    continue
-                S(act(b("G")[:, m, 16:256], T.tab[:, 0:W].indirect(b("off")[:, 16 * m + 2:16 * m + 17]), AF.Copy),
-                  TAB + n_("off", "~G"), [Gs[m]] + n_("~G"), 240 * GA)
-                if m == 0:
-                    S(act(b("z")[:], Pv, AF.Relu, 256.0, -256.0), n_("P", "~G"), n_("z", "~G"), CW)
-            for j in range(5):
-                cj = pA[:, :, 16 * j:16 * j + 16]
-                P([(cj, T.idb[:], Pv, CW), (cj, T.idb[:], b("z")[:], CW)], n_("P", "z") + ["idb"], [As[j]])
-            P([(pp, T.idb[:], Pv, CW)], n_("P") + ["idb"], [B_ + "P"])
-            compare(OP.is_gt)
+                src = win.indirect(b("off")[:, 16 * m + 2:16 * m + 17])
+                if m < KN["GV"][h]:
+                    V(cp(b("G")[:, m, 16:256], src), TAB + n_("off"), [Gs[m]], 240, GA)
+                else:
+                    S(act(b("G")[:, m, 16:256], src, AF.Copy), TAB + n_("off"), [Gs[m]], 240, GA)
+            S(act(Pe, win.indirect(b("offp")[:, 0:MB]), AF.Copy), TAB + n_("offp"), n_("Pe"), CW, GA)
+            compare(KN["C1"], Pv, n_("P"), ("id", "nid", "id"), OP.is_gt, (-128.0, 256.0))
             odd = []
             if v:
-                S(act(sf(4), T.MS[:, k, 6, 0:6], AF.Abs, -2.0, 1.0 / 4096), [Mx], n_("a1"), 6)
-                S(act(b("tb")[:], sf(4).indirect(T.bc6[:, 0:6]), AF.Abs, -1.0), n_("a1") + ["bc6"], n_("tb"), CW * GA)
-                odd = [(y1, T.idbig[:], b("tb")[:], CW)]
-            P([(y1, T.dth[:, v, :], k1, CW), (y1, T.idb[:], kr, CW)] + odd,
-              n_("tb") + ["idbig", "idb", "kr", "k1", "dth%d" % v, B_ + "P"], [B_ + "y1"], last=False)
-            count2(0, B_ + "y1")
-            V(tt(b("val")[:], y1, o, OP.max), [B_ + "y1", M], n_("val"), CW)
-            V(scan(b("R")[:], T.d0r[:], b("val")[:], OP.add, OP.min), n_("val") + ["d0r"], n_("R"), CW)
-            V(ts(si(0), b("R")[:, 15::16], CAP, OP.min, 16384.0, OP.mult), n_("R"), n_("x"), 6)
-            V(ts(si(1), si(0), 12288, OP.bitwise_and), n_("x"), n_("u4"), 6)
-            V(ts(si(2), si(0), 14, OP.arith_shift_right, W - 1, OP.bitwise_and), n_("x"), n_("Lk"), 6)
-            V(tt(sf(0), si(1), si(2), OP.add), n_("u4", "Lk"), n_("xo"), 12)
-            V(cp(b("xoff")[:], sf(0)), n_("xo"), n_("xoff"), 6)
-            S(act(b("xk")[:], T.tab[:].indirect(b("xoff")[:, 0:6]), AF.Copy), TABX + ["tabE"] + n_("xoff"), n_("xk"), CW * GA)
-            if SGV:
-                V(ts(b("SG")[:, :, 16:16 + 16 * SGV], b("G")[:, :, 16:16 + 16 * SGV], 0.0, OP.is_gt), Gs, n_("SGa"), 48 * SGV)
-            cuts = [SGV + 1 + (15 - SGV) * j // 3 for j in range(4)]
-            for j in range(3):
-                r0, r1 = cuts[j], cuts[j + 1]
-                if r1 > r0:
-                    S(act(b("SG")[:, :, 16 * r0:16 * r1], b("G")[:, :, 16 * r0:16 * r1], AF.Sign), Gs, n_("SG%d_" % j), CW * (r1 - r0))
-            P([(pD[:, 0:6, :], T.idb[:], x, CW) for x in Tv + [b("z")[:]]], [Tn, "idb"] + n_("z"), [D_ + "q1"])
-            S(act(b("e")[:], pD[:, 0:6, :], AF.Relu, -256.0), [D_ + "q1"], n_("e"), CW)
-            P([(hr, T.idb[:], kh, CW), (hr, T.whi[:], Pv, CW), (hr, T.wlo[:], Pv, CW), (hr, T.whi[:], b("e")[:], CW), (hr, T.wlo[:], b("e")[:], CW)],
-              n_("P", "e") + ["kh", "whi", "wlo", "idb"], [C_ + "h"])
-            V(scan(b("sh")[:], T.adiag[:], hr, OP.mult, OP.max), [C_ + "h", "adiag"], n_("sh"), CW)
-            V(ts(si(3), b("sh")[:, 15::16], col(SCL), OP.mult), n_("sh") + ["SCL"], n_("h1"), 6)
-            V(ts(si(4), si(3), W - 1, OP.bitwise_and), n_("h1"), n_("h2"), 6)
-            V(ts(T.MS[:, k, 0:6, 17], si(4), 0.25, OP.add), n_("h2") + [M], n_("hs"), 6)
-            P([(pC[:, 1:3 * CW:3], idf, o0, 384), (pC[:, 1:3 * CW:3], nidf, o, 384)], [M, Mx, "wide", "nidf"], [C_ + "dm"])
-            P([(pC[:, 2:3 * CW:3], idf, o, 384)], [M, "wide"], [C_ + "o"])
-            P([(pC[:, 0:3 * CW:3], nidf, o0, 384), (pC[:, 0:3 * CW:3], idf, o1, 384)], [M, Mx, "wide", "nidf"] + n_("hs"), [C_ + "d2"])
+                S(act(sf(4), T.MS[:, k, :, 19], AF.Abs, -2.0, 1.0 / 4096), [Mx], n_("a1"), MB)
+                S(act(b("tb")[:], sf(4).indirect(Lb), AF.Abs, -1.0), n_("a1") + ["Lb"], n_("tb"), SP, GA)
+                odd = [(y1, I["big" if v % 2 else "nbig"], b("tb")[:, 0:SL], SL)]
+            P([(y1, T.dth[:, v, :], kc(k1, SL), SL)] + odd, n_("tb") + ["big", "nbig", "k1", "dth%d" % v], [B_ + "y1"], last=False)
+            counts(0, B_ + "y1", KN["C1"])
+            V(tt(b("val")[:], y1, o0, OP.max), [B_ + "y1", M, Mx], n_("val"), SL)
+            V(scan(b("R")[:], T.d0r[:], b("val")[:], OP.add, OP.min), n_("val") + ["d0r"], n_("R"), SL)
+            V(ts(si(0), b("R")[:, 16::17], 2 * W + 0.75, OP.min, 0.25, OP.add), n_("R"), n_("x"), MB)
+            V(ts(si(1), si(0), int(STEP) - 1, OP.bitwise_and), n_("x"), n_("xo"), MB)
+            V(cp(b("xoff")[:], si(1)), n_("xo"), n_("xoff"), MB)
+            xs = T.tab[:, 0:TRASH].indirect(b("xoff")[:, 0:MB])
+            if KN["FU"]:
+                V(tt(b("le")[:], xs, Pe, OP.is_le), TAB + ["tabN"] + n_("xoff", "Pe"), n_("le"), CW, GA)
+                V(tt(b("t")[:], xs, b("le")[:], OP.mult), TAB + ["tabN"] + n_("xoff", "le"), n_("t"), CW, GA)
+            S(act(xk, xs, AF.Copy), TAB + ["tabN"] + n_("xoff"), n_("xk"), CW, GA)
+            P([(c2, I["id"], Tv, CW), (c2, I["nid"], Pv, CW), (c2, I["id"], T.kk[:, 0:CW], CW)], [Tn, "id", "nid", "kk"] + n_("P"), [C_ + "2"])
+            V(tt(b("Tc")[:], Pv, c2, OP.min), n_("P") + [C_ + "2"], n_("Tc"), CW)
+            P([(c1, I["id"], kc(kh), CW), (c1, T.whi[:], b("Tc")[:], CW), (c1, T.wlo[:], b("Tc")[:], CW)],
+              n_("Tc") + ["kh", "whi", "wlo", "id"], [C_ + "1"])
+            V(scan(b("sh")[:], T.adiag[:], c1, OP.mult, OP.max), [C_ + "1", "adiag"], n_("sh"), CW)
+            V(ts(si(3), b("sh")[:, 15::16], col(SCL), OP.mult), n_("sh") + ["SCL"], n_("h1"), MB)
+            V(ts(si(4), si(3), W - 1, OP.bitwise_and), n_("h1"), n_("h2"), MB)
+            if KN["HP"]:
+                V(ts(sf(5), si(4), 2.0, OP.mult, 0.375, OP.add), n_("h2"), n_("hr"), MB)
+                if v:
+                    V(ms(T.MS[:, k, 0:MB, 17], 0.0), [M], n_("hs"), MB)
+            else:
+                V(ts(T.MS[:, k, 0:MB, 17], si(4), 2.0, OP.mult, 0.375, OP.add), n_("h2") + [M], n_("hr"), MB)
+                S(act(T.MS[:, k, 0:MB, 18], T.MS[:, k, 0:MB, 17], AF.Copy), n_("hr"), n_("hs"), MB)
+            S(act(ns, b("R")[:], AF.Sigmoid, -20000.0), n_("R", "m1"), n_("ns"), SL)
+            S(act(m1[:, 2:3 * SP + 1:3], b("R")[:].indirect(Le), AF.Sigmoid, 20000.0, -1.0), n_("R", "m1") + ["Le"], n_("nb"), SP, GA)
+            if KN["XO"] == "s":
+                S(act(pC[:, 3:X3 + 1:3], o, AF.Copy), [M] + n_("hs"), [C_ + "o", C_ + "h"], SL)
+            else:
+                P([(pC[:, 3:X3 + 1:3], idf, o, 4 * SL)], [M, "wide"] + n_("hs"), [C_ + "o", C_ + "h"])
+            P([(pC[:, 1:X3 + 1:3], idf, o0, 4 * SL), (pC[:, 1:X3 + 1:3], nidf, o1, 4 * SL)], [M, "wide", "nidf"] + n_("hs"), [C_ + "d2"])
+            P([(pC[:, 2:X3 + 1:3], nidf, o, 4 * SL), (pC[:, 2:X3 + 1:3], idf, o1, 4 * SL)], [M, "wide", "nidf"] + n_("hs"), [C_ + "dm"])
+            for j, nm, f in ((46, "d2", OP.subtract), (47, "dm", OP.add))[:2 * KN["HP"]]:
+                V(tt(pC[:, j:X3:51], pC[:, j:X3:51], sf(5), f), n_("hr") + [C_ + nm], [C_ + nm], MB)
             return
-        V(tt(b("gt")[:], b("xk")[:], pp, OP.is_gt), n_("xk") + [B_ + "P"], n_("gt"), CW)
-        qq = pD[:, 25:31, :]
-        P([(qq, T.idb[:], b("xk")[:], CW), (qq, T.idm256[:], b("gt")[:], CW)], n_("xk", "gt") + ["idb", "idm256"], [D_ + "q"])
-        S(act(b("B2")[:], qq, AF.Relu, -1.0), [D_ + "q"], n_("B2"), CW)
-        for j in range(5):
-            P([(pA[:, :, 16 * j:16 * j + 16], T.idb[:], b("B2")[:], CW)], n_("B2", "~B") + ["idb"], [As[j]] + n_("~B"))
-        S(act(b("Bv")[:], qq, AF.Relu), [D_ + "q"], n_("Bv"), CW)
-        late = KN["LATE"] and h == NH - 1 and v < KN["LATE"]
-        if not late:
-            compare(OP.is_le)
-        P([(sr, T.idb[:], ks, CW), (sr, T.gms[:], b("xk")[:], CW)], n_("xk") + ["idb", "ks", "gms"], [C_ + "s"])
-        V(scan(b("sc")[:], T.adiag[:], sr, OP.mult, OP.max), [C_ + "s", "adiag"], n_("sc"), CW)
-        V(ts(si(5), b("sc")[:, 15::16], col(SCL), OP.mult), n_("sc") + ["SCL"], n_("s1"), 6)
-        V(ts(si(6), si(5), 15 * 16384, OP.bitwise_and), n_("s1"), n_("s2"), 6)
-        S(act(sf(3), sf(0), AF.Sign, 4095.5, -1.0), n_("xo"), n_("cut"), 6)
-        S(act(sf(1), sf(3), AF.Identity, 2048.0, 2048.0), n_("cut"), n_("c4"), 6)
-        V(tt(sf(2), si(6), sf(1), OP.add), n_("s2", "c4"), n_("ms"), 12)
-        V(tt(b("D")[:], sf(2).indirect(T.bc12[:, 0:12]), b("oa")[:], OP.subtract), n_("ms", "oa0", "oa1") + ["bc12a", "bc12b"], n_("D"), 2 * CW * GA)
-        S(act(b("D")[:], b("D")[:], AF.Abs), n_("D"), n_("D"), 2 * CW)
-        V(scan(b("R3")[:], T.d0m[:], b("D")[:], OP.add, OP.min), n_("D") + ["d0m"], n_("R3"), 2 * CW)
-        V(cp(b("soff")[:], b("R3")[:, 15::16]), n_("R3"), n_("soff"), 12)
-        win = T.tab[:, 0:2 * W]
-        V(tt(win.indirect(b("soff")[:, 0:6]), b("xk")[:], b("gt")[:], OP.mult), n_("soff", "xk", "gt") + TABX, TABX, CW * SCA)
-        V(cp(win.indirect(b("soff")[:, 6:12]), b("Bv")[:]), n_("soff", "Bv") + TABX, TABX, CW * SCA)
-        if late:
-            compare(OP.is_le, TAB)
-        V(tt(T.SO[:, k, 6, 0:6], T.MS[:, k, 6, 0:6], sf(1), OP.add), [Mx, "SOinit"] + n_("c4"), [SOn + "a"], 12)
-        TT = [D_ + "T0", D_ + "T1"]
-        S(act(b("nl")[:], b("xk")[:], AF.Relu, scale=-512.0), n_("xk"), n_("nl"), CW)
-        P([(pD[:, 6:12, :], T.idb[:], x, CW) for x in (Pv, b("e")[:], km, b("nl")[:])], n_("P", "e", "nl") + ["idb", "km"], TT[:1])
-        P([(pD[:, 12:18, :], T.idb[:], x, CW) for x in Tv] + [(pD[:, 12:18, :], T.nidb[:], b("nl")[:], CW)], n_("nl") + [Tn, "idb", "nidb"], TT[1:])
-        S(act(T.TS[:, k, :], pD[:, 6:18, :], AF.Relu), TT, ["TS%d" % k], 2 * CW)
+        u, le, Bv = b("t")[:], b("le")[:], b("FB")[:, CW:2 * CW]
+        if KN["FU"]:
+            compare(KN["C2"], u, n_("t"), ("ida", "ida", "nid"), OP.is_lt, (0.0, 65536.0))
+        else:
+            P([(pA[:, 0:MB, :], I["idc"], Pe, CW), (pA[:, 0:MB, :], I["idd"], xk, CW)], n_("xk", "Pe") + ["idc", "idd"], [A_])
+            V(tt(u, xk, pA[:, 0:MB, :], OP.min), n_("xk") + [A_], n_("t"), CW)
+            V(ts(Bv, u, -K, OP.max), n_("t"), n_("B"), CW // 2)
+            compare(KN["C2"], Bv, n_("B"), ("ida", "ida", "nid"), OP.is_lt, (0.0, 65536.0))
+        P([(c2, I["id"], kc(ks), CW), (c2, T.gmb[:], xk, CW)], n_("xk") + ["id", "ks", "gmb"], [C_ + "2"])
+        V(scan(b("sc")[:], T.adiag[:], c2, OP.mult, OP.max), [C_ + "2", "adiag"], n_("sc"), CW)
+        V(ts(si(5), b("sc")[:, 15::16], col(SCL), OP.mult), n_("sc") + ["SCL"], n_("s1"), MB)
+        V(ts(si(6), si(5), 4096 + 15, OP.bitwise_and), n_("s1"), n_("s2"), MB)
+        V(tt(b("keep")[:], b("si")[:, 6, 0:MB + 1].indirect(Lk), T.key[:], OP.not_equal), n_("s2", "sk") + ["Lk", "key", "kez"], n_("keep"), SP, GA)
+        for j in range(2):
+            V(scan(b("Rn")[:, SL * j:SL * j + SL], b("keep")[:, 0:SL], b("D")[:, j, :], OP.mult, OP.add), n_("keep", "D%d" % j), n_("Rn%d" % j), SL)
+        if KN["FU"]:
+            P([(c1, I["id"], xk, CW), (c1, I["nid"], u, CW), (c1, I["nk"], le, CW)][:2 if last else 3],
+              n_("xk", "t", "le") + ["id", "nid", "nk"], [C_ + "1"])
+        else:
+            P([(c1, I["id"], xk, CW), (c1, I["nid"], Bv, CW)], n_("xk", "B") + ["id", "nid"], [C_ + "1"])
+        if last:
+            V(ts(b("soff")[:], b("Rn")[:, 16::17], 0.5, OP.mult), n_("Rn0", "Rn1"), n_("soff"), 2 * MB)
+            S(act(b("FC")[:, 0:CW], c1, AF.Relu, 0.0 if KN["FU"] else -K), [C_ + "1"], n_("F"), CW)
+            S(act(b("FC")[:, CW:2 * CW], u, AF.Relu), n_("t"), n_("Bp"), CW)
+            V(cp(T.raw[:].indirect(b("soff")[:]), b("FC")[:]), n_("soff", "F", "Bp") + RAW, RAW, 2 * CW, SCA)
+        else:
+            V(cp(b("soff")[:], b("Rn")[:, 16::17]), n_("Rn0", "Rn1"), n_("soff"), 2 * MB)
+            S(act(b("FB")[:, 0:CW], c1, AF.Identity, 0.0 if KN["FU"] else -K), [C_ + "1"], n_("F"), CW)
+            if KN["FU"]:
+                P([(c2, I["nid"], u, CW), (c2, I["nk"], le, CW)], n_("t", "le") + ["nid", "nk"], [C_ + "2"])
+                S(act(Bv, c2, AF.Identity, -K, -1.0), [C_ + "2"], n_("B"), CW)
+            if KN["SS"]:
+                for j in (1, 0):
+                    V(cp(T.tab[:].indirect(b("soff")[:, MB * j:MB * j + MB]), b("FB")[:, CW * j:CW * j + CW]),
+                      n_("soff", "FB"[j]) + TAB + ["tabN"], TAB + ["tabN"], CW, SCA)
+            else:
+                V(cp(T.tab[:].indirect(b("soff")[:]), b("FB")[:]), n_("soff", "F", "B") + TAB + ["tabN"], TAB + ["tabN"], 2 * CW, SCA)
+        V(tt(T.SO[:, k, :, 19], T.MS[:, k, :, 19], si(6), OP.add), [Mx, "SOi%d" % v] + n_("s2"), [SOn + "a"], 2 * MB)
+        if KN["TS"]:
+            S(act(b("nl")[:], xk, AF.Relu, ZT, -1.0), n_("xk"), n_("nl"), CW)
+            P([(c1, I["id"], b("Tc")[:], CW), (c1, I["nid"], xk, CW)], n_("Tc", "xk") + ["id", "nid"], [C_ + "1"])
+            S(act(b("p1")[:], c1, AF.Relu, ZN), [C_ + "1"], n_("p1"), CW)
+            P([(c2, I["id"], Tv, CW), (c2, I["nid"], b("nl")[:], CW)], n_("nl") + [Tn, "id", "nid"], [C_ + "2"])
+            V(tt(T.TS[:, k, :], b("p1")[:], c2, OP.max), n_("p1") + [C_ + "2"], ["TS%d" % k], CW)
+        else:
+            P([(c2, I["id"], kc(kz), CW), (c2, I["id"], xk, CW)], n_("xk") + ["id", "kz"], [C_ + "2"])
+            V(tt(b("p1")[:], Tv, c2, OP.min), [Tn, C_ + "2"], n_("p1"), CW)
+            P([(c1, I["nid"], kc(kz), CW), (c1, I["id"], b("Tc")[:], CW), (c1, I["nid"], xk, CW)], n_("Tc", "xk") + ["id", "nid", "kz"], [C_ + "1"])
+            V(tt(T.TS[:, k, :], b("p1")[:], c1, OP.max), n_("p1") + [C_ + "1"], ["TS%d" % k], CW)
         cs = slice(CW * h, CW * h + CW)
         if last:
-            V(tt(b("nl")[:], T.TS[:, k, 0:CW], T.TS[:, k, CW:C], OP.add), ["TS%d" % k], n_("nl"), 2 * CW)
-            store(T.ypic[:, cs], b("nl")[:], n_("nl"), 2000)
-            S(act(b("ax")[:, :, 0], T.SO[:, k, 6, 0:6], AF.Copy, scale=1.0 / 4096), [SOn + "a"] + n_("ax"), n_("ax"), 6)
+            V(ts(si(7), T.SO[:, k, :, 19], -1.0 / 4096, OP.mult, float(NV), OP.add), [SOn + "a"], n_("A"), MB)
+            V(cp(b("ax")[:, :, 0], si(7)), n_("A", "ax"), n_("ax"), MB)
         else:
-            send(T.TS[:, k, :], T.TR[:, k + NH, :], "aT%d%s" % (v + 1, H), ["TS%d" % k], ["T%d%s" % (v + 1, H)])
-        X3 = 3 * CW
-        m1, m2, w1, w2 = b("m1"), b("m2"), b("w1"), b("w2")
-        ns = m1[:, 5:X3 + 3:3]
-        S(act(ns, b("R")[:], AF.Sigmoid, -5000.0), n_("R", "m1"), n_("ns"), CW)
-        S(act(m1[:, 1:X3:3], sf(0).indirect(T.bc6[:, 0:6]), AF.Relu, -8191.0), n_("xo", "m1") + ["bc6"], n_("nb"), CW * GA)
-        V(scan(w1[:, 0:X3], m1[:, 0:X3], pC[:, 0:X3], OP.mult, OP.add), n_("ns", "nb") + [C_ + "dm", C_ + "d2", C_ + "o"],
+            send(T.TS[:, k, :], T.TR[:, k + NH, :], "aT%d%s" % (v + 1, H), ["TS%d" % k], ["T%d%s" % (v + 1, H)], 2 * CW)
+        V(tt(b("D")[:, 2, 0:SL:17], si(1), sf(7), OP.subtract), n_("xo", "c1", "D2"), n_("D2"), 2 * MB)
+        V(scan(b("Rh")[:], b("keep")[:, 0:SL], b("D")[:, 2, :], OP.mult, OP.add), n_("keep", "D2"), n_("Rh"), SL)
+        if KN["HEAD"] == "s":
+            S(act(pC[:, 0:X3:51], b("Rh")[:, 16::17], AF.Copy), n_("Rh") + [C_ + "o"], [C_ + "h"], MB)
+        else:
+            V(cp(pC[:, 0:X3:51], b("Rh")[:, 16::17]), n_("Rh") + [C_ + "o"], [C_ + "h"], MB)
+        V(scan(w1[:, 0:X3 + 1], m1[:, 0:X3 + 1], pC[:, 0:X3 + 1], OP.mult, OP.add), n_("ns", "nb", "m0", "m1") + [C_ + "dm", C_ + "d2", C_ + "o", C_ + "h"],
           n_("w", "wa", "wb"), X3)
-        V(tt(sf(5), w1[:, 1:X3:48], T.MS[:, k, 0:6, 1], OP.add), n_("wa") + [M], n_("c5"), 12)
-        V(tt(sf(6), sf(1), si(2), OP.max), n_("c4", "Lk"), n_("c2"), 12)
-        V(tt(sf(7), sf(5), sf(6), OP.max), n_("c5", "c2"), n_("c3"), 12)
-        V(tt(w1[:, 1:X3:3], b("R3")[:].indirect(T.bcn[:, 0:6]), w1[:, 2:X3:3], OP.subtract), n_("R3", "w") + ["bcn"], n_("wa"), CW * GA)
-        V(tt(w1[:, 2:X3:48], b("R3")[:, 15:CW:16], sf(7), OP.min), n_("R3", "c3"), n_("w"), 12)
-        S(act(w1[:, 3:X3 + 3:3], w1[:, 1:X3:3], AF.Copy, scale=-1.0), n_("wa"), n_("wb"), CW)
-        P([(y2, T.idbig[:], ky, CW)] + count(6, b("SG")),
-          n_("SGa", "SG0_", "SG1_", "SG2_", "~B") + ["ky", "idbig", "sel", B_ + "P", B_ + "y1"], [B_ + "y2"], last=False)
-        count2(6, B_ + "y2")
-        V(tt(b("val")[:], y2, ns, OP.max), [B_ + "y2"] + n_("ns"), n_("val"), CW)
-        V(scan(b("U")[:], T.d0u[:], b("val")[:], OP.add, OP.min), n_("val") + ["d0u"], n_("U"), CW)
-        if KN["GES"]:
-            S(act(m2[:, 2:X3:3], b("U")[:], AF.Sigmoid, 128.0, -256.0), n_("U", "m2"), n_("ge"), CW)
+        V(tt(w1[:, 2:3 * SP + 1:3], b("Rn")[:].indirect(Lf), w1[:, 3:3 * SP + 1:3], OP.subtract), n_("Rn0", "Rn1", "w") + ["Lf"], n_("wa"), SP, GA)
+        if not KN["ZP"]:
+            S(act(w1[:, 4:X3 + 4:3], w1[:, 2:X3 + 1:3], AF.Copy, scale=-1.0), n_("wa"), n_("wb"), SL)
+        nz = [(y2, I["big"], kc(ky, SL), SL)] + count(MB, b("G"), 1)
+        cuts = [len(nz) * j // KN["NZ"] for j in range(KN["NZ"] + 1)]
+        for j in range(KN["NZ"]):
+            P(nz[cuts[j]:cuts[j + 1]], Gs + ["ky", "big", "sel1", B_ + "y1", B_ + "y2"], [B_ + "y2"], first=j == 0, last=False)
+        counts(MB, B_ + "y2", KN["C2"])
+        V(tt(b("val")[:], y2, ns, OP.max), [B_ + "y2"] + n_("ns"), n_("val"), SL)
+        V(scan(b("U")[:], T.d0u[:], b("val")[:], OP.add, OP.min), n_("val") + ["d0u"], n_("U"), SL)
+        if KN["ZP"]:
+            gz, zo, Z = pC[:, 0:SL - 1], pC[:, 128:128 + SL], w2[:, 0:SL + 1]
+            if KN["GE"][0] == "s":
+                S(act(gz, b("U")[:, 1:SL], AF.Sigmoid, 128.0, -256.0), n_("U", "w"), [C_ + "o", C_ + "d2", C_ + "dm", C_ + "h"], SL)
+            else:
+                V(ts(gz, b("U")[:, 1:SL], 0.0, OP.is_le), n_("U", "w"), [C_ + "o", C_ + "d2", C_ + "dm", C_ + "h"], SL)
+            V(tt(w2[:, 1:SL], w1[:, 2:X3 - 2:3], gz, OP.mult), n_("wa", "w2z") + [C_ + "o"], n_("w2"), SL)
+            P([(zo, idf, w1[:, 3:X3 + 1:3], 4 * SL), (zo, idf, w2[:, 1:SL + 1], 4 * SL), (zo, nidf, w2[:, 0:SL], 4 * SL)],
+              n_("w", "w2", "w2z") + ["wide", "nidf"], [C_ + "d2", C_ + "dm", C_ + "h"])
+            S(act(T.SO[:, k, 0:MB, 1:18], zo, AF.Copy, scale=0.5 if last else 1.0), [C_ + "d2", "SOi%d" % v], [SOn], SL)
         else:
-            V(ts(m2[:, 2:X3:3], b("U")[:], 0.0, OP.is_le), n_("U", "m2"), n_("ge"), CW)
-        S(act(m2[:, 4:X3 + 2:3], b("U")[:], AF.Sigmoid, 128.0, -256.0), n_("U", "m2"), n_("gf"), CW)
-        V(scan(w2[:], m2[:, 0:X3], w1[:, 0:X3], OP.mult, OP.add), n_("ge", "gf", "w", "wa", "wb"), n_("w2"), X3)
-        S(act(T.SO[:, k, 0:6, 1:17], w2[:, 2:X3:3], AF.Copy), n_("w2") + ["SOinit"], [SOn], CW)
+            for e, nm, dst, src in ((KN["GE"][0], "ge", m2[:, 2:X3 - 3:3], b("U")[:, 1:SL]), (KN["GE"][1], "gf", m2[:, 1:X3:3], b("U")[:])):
+                if e == "s":
+                    S(act(dst, src, AF.Sigmoid, 128.0, -256.0), n_("U", "m2"), n_(nm), SL)
+                else:
+                    V(ts(dst, src, 0.0, OP.is_le), n_("U", "m2"), n_(nm), SL)
+            V(scan(w2[:], m2[:, 0:X3], w1[:, 1:X3 + 1], OP.mult, OP.add), n_("ge", "gf", "w", "wa", "wb"), n_("w2"), X3)
+            if KN["SO"] == "s":
+                S(act(T.SO[:, k, 0:MB, 1:18], w2[:, 2:X3:3], AF.Copy, scale=0.5 if last else 1.0), n_("w2") + ["SOi%d" % v], [SOn], SL)
+            else:
+                V(ts(T.SO[:, k, 0:MB, 1:18], w2[:, 2:X3:3], 0.5 if last else 1.0, OP.mult), n_("w2") + ["SOi%d" % v], [SOn], SL)
         if not last:
             send(T.SO[:, k], T.MS[:, k + NH], "aM%d%s" % (v + 1, H), [SOn, SOn + "a"],
-                 ["M%d%s" % (v + 1, H), "Mx%d%s" % (v + 1, H)])
+                 ["M%d%s" % (v + 1, H), "Mx%d%s" % (v + 1, H)], 80 * MB)
             return
-        turn(lambda j: b("ax")[:, j:6:2, :], D_, 0, n_("ax"), D_ + "fc", [D_ + "q1"])
-        V(tr(b("sh")[:], pD[:, 0:6, :]), [D_ + "fc0", D_ + "fc1"], n_("sh"), CW)
-        store(T.ycut[:, cs], b("sh")[0:128:16, :], n_("sh"), 2000)
-        turn(lambda j: T.SO[:, k, j:6:2, 1:17], D_, 6, [SOn], D_ + "fa", [D_ + "T0"])
-        V(tr(b("val")[:], pD[:, 6:12, :]), [D_ + "fa0", D_ + "fa1"], n_("val"), CW)
-        V(cp(T.lnam[:, cs], b("val")[:]), n_("val"), n_("fi") + ["lnam"], CW)
-        V(cp(b("U")[:], T.lnam[:, cs]), n_("fi"), n_("U"), CW)
-        store(T.ynam[:, cs], b("U")[:], n_("U"), 2000)
-        V(tt(b("R")[:], T.lnam[:, cs], b("val")[:], OP.is_equal), n_("fi", "val"), n_("R"), 2 * CW)
-        store(T.ymrk[:, cs], b("R")[:], n_("R"), 2000)
+        turn(lambda j: b("ax")[:, j:MB:2, :], A_, 0, n_("ax"), A_)
+        V(tr(T.out[:, 0, cs], pA[:, 0:MB, :]), [A_], n_("oc"), CW)
+        turn(lambda j: T.SO[:, k, j:MB:2, 1:17], E_, 0, [SOn], E_)
+        V(tr(b("sc")[:], pE[:, 0:MB, :]), [E_], n_("sc"), CW)
+        V(cp(T.lnam[:, cs], b("sc")[:]), n_("sc"), n_("fi") + ["lnam"], CW)
+        V(cp(T.out[:, 1, cs], T.lnam[:, cs]), n_("fi"), n_("on"), CW)
+        V(tt(T.out[:, 2, cs], T.lnam[:, cs], b("sc")[:], OP.is_equal), n_("fi", "sc"), n_("om"), 2 * CW)
 
     for v in range(NV):
+        if v == NV - 1:
+            for j, e in enumerate(KN["DEC"]):
+                n = W // len(KN["DEC"])
+                o, x = T.raw[:, n * j:n * j + n], T.tab[:, 2 * n * j:2 * n * (j + 1):2]
+                if e == "v":
+                    V(ts(o, x, 0.0, OP.max), TAB, [RAW[n * j // DW]], n // 2)
+                else:
+                    S(act(o, x, AF.Relu), TAB, [RAW[n * j // DW]], n)
         for second in (False, True):
             for h in range(NH):
                 a = len(ops)
                 part(v, h, second)
-                seen = {}
-                for o in ops[a:]:
-                    nm = o["e"] + "".join(c for c in (o["w"] + ["out"])[0] if not c.isdigit())
-                    seen[nm] = seen.get(nm, 0) + 1
-                    o["k"], o["v"] = "%s%d%d%d" % (nm, seen[nm], second, h), v
-    store(T.ydep[:, 0:2048], T.tab[:, 0:2048], ["tabA"], 4000)
-    store(T.ydep[:, 2048:W], T.tab[:, 2048:W], ["tabB"], 5000)
-    for i, o in enumerate(ops):
-        if "k" not in o:
-            o["k"], o["v"] = "i%d" % i, 0
+                for j, o in enumerate(ops[a:]):
+                    o["k"] = "%s%d%d%s%d" % ("amz"[(v > 0) + (v == NV - 1)], h, second, o["e"], j)
+    for j in range(ND):
+        store(T.ydep[:, DW * j:DW * j + DW], T.raw[:, DW * j:DW * j + DW], [RAW[j]], 2 * DW, KN["SQ"][j])
+    k = NH * (NV - 1)
+    store(T.ypic[:], T.TS[:, k:k + NH, :], ["TS%d" % (k + h) for h in range(NH)], 2 * C, KN["SQ"][ND])
+    store(T.ycut[:], T.out[0:128:16, 0, :], ["oc0", "oc1"], C // 4, KN["SQ"][ND + 1])
+    store(T.ynam[:], T.out[:, 1, :], ["on0", "on1"], 4 * C, KN["SQ"][ND + 2])
+    store(T.ymrk[:], T.out[:, 2, :], ["om0", "om1"], 4 * C, KN["SQ"][ND + 3])
     return ops
-
-
-def keys(ops):
-    out = []
-    for o in ops:
-        if o["k"] not in out:
-            out.append(o["k"])
-    return out
-
-
-def order(ops):
-    n = len(ops)
-    lastw, readers, deps, succ = {}, {}, [], [[] for _ in ops]
-    for i, o in enumerate(ops):
-        d = set(lastw[x] for x in o["r"] + o["w"] if x in lastw)
-        for x in o["w"]:
-            d.update(readers.get(x, ()))
-        d.discard(i)
-        deps.append(d)
-        for j in d:
-            succ[j].append(i)
-        for x in o["r"]:
-            readers.setdefault(x, []).append(i)
-        for x in o["w"]:
-            lastw[x] = i
-            readers[x] = []
-    at = dict(zip(keys(ops), PLACE))
-    place = [10 * at[o["k"]] + PERIOD * o["v"] for o in ops]
-    left = [len(d) for d in deps]
-    ready = [i for i in range(n) if left[i] == 0]
-    free = {e: 0.0 for e in "vspgy"}
-    end, start = [0.0] * n, [0.0] * n
-    bank, locked, seq = {}, set(), []
-    while ready:
-        i = min((j for j in ready if ops[j]["e"] != "p" or ops[j]["lock"] == "close" or not any(x in locked for x in ops[j]["banks"])),
-                key=lambda j: (place[j], j))
-        o = ops[i]
-        ready.remove(i)
-        for x in o["banks"]:
-            deps[i].update(j for e, j in bank.get(x, {}).items() if e != o["e"])
-            bank.setdefault(x, {})[o["e"]] = i
-            if o["lock"] == "open":
-                locked.add(x)
-            if o["lock"] == "close":
-                locked.discard(x)
-        start[i] = max([free[o["e"]]] + [end[j] + KN["HOP"] for j in deps[i]])
-        end[i] = start[i] + o["ns"]
-        free[o["e"]] = start[i] + (o["ns"] if o["sem"] is None else (900 if o["e"] == "g" else 60))
-        seq.append(i)
-        for j in succ[i]:
-            left[j] -= 1
-            if left[j] == 0:
-                ready.append(j)
-    return seq, deps, start, max(end)
-
-
-PERIOD = 20000
-PLACE = []
 
 
 def greedy(ops):
@@ -486,53 +559,194 @@ def greedy(ops):
     for i in range(n):
         for j in behind[i]:
             succ[j].append(i)
+    eng = [o["e"] for o in ops]
+    banks = [o["banks"] for o in ops]
+    fresh = [o["e"] == "p" and o["lock"] not in ("more", "close") and o["banks"] for o in ops]
+    isdma = [o["sem"] is not None and o["e"] != "g" for o in ops]
+    deps = [sorted(d) for d in deps]
+
+    def times(m):
+        ns = [dur(o, m) for o in ops]
+        ex = [m["LG"] if o["c"][0] == "g" else m["LP"] if o["e"] == "p" else m["LS"] if o["e"] == "s" else 0.0 for o in ops]
+        return (ns, [ns[i] if o["sem"] is None else (m["ISS"] if o["e"] == "g" else m["DQ"]) for i, o in enumerate(ops)],
+                [x + m["HS"] for x in ex], [x + m["HOP"] for x in ex])
+
+    models = [dict(KN, **x) for x in KN["ALT"]]
+    tabs = [times(m) for m in models]
+    ns, hold, near, far = times(KN)
+    DL, WIN = KN["DL"], KN["WIN"]
     prio = [0.0] * n
-    seed = KN["SEED"]
     for i in range(n - 1, -1, -1):
-        seed = (seed * 1103515245 + 12345) % 2147483648
-        prio[i] = ops[i]["ns"] + HOP + max([prio[j] for j in succ[i]] or [0.0]) + KN["JIT"] * seed / 2147483648.0
+        prio[i] = ns[i] + HOP + max([prio[j] for j in succ[i]] or [0.0])
         if "SO%d0" % (NV - 1) in ops[i]["w"]:
             prio[i] += KN["LEAD"]
-    left = [len(d) for d in behind]
-    ready = [i for i in range(n) if left[i] == 0]
-    free = {e: 0.0 for e in "vspgy"}
-    end, start = [0.0] * n, [0.0] * n
-    bank, locked, seq = {}, set(), []
-    while ready:
-        best = None
-        for i in ready:
-            o = ops[i]
-            if o["e"] == "p" and o["lock"] not in ("more", "close") and any(x in locked for x in o["banks"]):
-                continue
-            dep = set(deps[i])
-            for x in o["banks"]:
-                dep.update(j for e, j in bank.get(x, {}).items() if e != o["e"])
-            st = max([free[o["e"]]] + [end[j] + HOP for j in dep])
-            key = (st - KN["SLACK"] * prio[i] - BIAS.get(o.get("k"), 0), i)
-            if best is None or key < best[0]:
-                best = (key, i, st, dep)
-        _, i, st, dep = best
-        o = ops[i]
-        ready.remove(i)
-        deps[i], start[i] = dep, st
-        end[i] = st + o["ns"]
-        free[o["e"]] = st + (o["ns"] if o["sem"] is None else (900 if o["e"] == "g" else 60))
-        for x in o["banks"]:
-            bank.setdefault(x, {})[o["e"]] = i
-            if o["lock"] == "open":
-                locked.add(x)
-            if o["lock"] == "close":
-                locked.discard(x)
-        seq.append(i)
-        for j in succ[i]:
-            left[j] -= 1
-            if left[j] == 0:
-                ready.append(j)
-    return seq, deps, start, max(end)
+
+    after = [[] for _ in ops]
+    for i in range(n):
+        for j in deps[i]:
+            after[j].append(i)
+    stale = [o["e"] == "p" and o["lock"] not in ("more", "open") and o["banks"] for o in ops]
+
+    def back(pr):
+        left = [len(d) for d in succ]
+        ready = [i for i in range(n) if left[i] == 0]
+        free = {e: 0.0 for e in "vspgy"}
+        end, rt = [0.0] * n, [ns[i] - hold[i] for i in range(n)]
+        bank, locked = {}, set()
+        while ready:
+            cand, t1, i1 = [], 1e18, -1
+            for i in ready:
+                e = eng[i]
+                st = rt[i] if rt[i] > free[e] else free[e]
+                if banks[i]:
+                    if stale[i] and locked and any(x in locked for x in banks[i]):
+                        continue
+                    for x in banks[i]:
+                        for f, j in bank.get(x, ()):
+                            if f != e and end[j] + far[i] > st:
+                                st = end[j] + far[i]
+                cand.append((st, i))
+                t = st + WIN * hold[i]
+                if t < t1:
+                    t1, i1 = t, i
+            e, best, i = eng[i1], -1e18, -1
+            for s, j in cand:
+                if eng[j] == e and (s < t1 or j == i1) and pr[j] > best:
+                    best, i, st = pr[j], j, s
+            ready.remove(i)
+            for x in banks[i]:
+                bank[x] = [(f, j) for f, j in bank.get(x, ()) if f != e] + [(e, i)]
+                if ops[i]["lock"] == "close":
+                    locked.add(x)
+                if ops[i]["lock"] == "open":
+                    locked.discard(x)
+            end[i] = free[e] = st + hold[i]
+            for j in behind[i]:
+                left[j] -= 1
+                if left[j] == 0:
+                    rt[j] = max([end[x] + (near[j] if eng[x] == eng[j] else far[j]) for x in after[j]] or [0.0]) + ns[j] - hold[j]
+                    ready.append(j)
+        return end
+
+    def place(pr):
+        left = [len(d) for d in behind]
+        ready = [i for i in range(n) if left[i] == 0]
+        free = {e: 0.0 for e in "vspgy"}
+        end, start, rt, full = [0.0] * n, [0.0] * n, [0.0] * n, [None] * n
+        bank, locked, seq, dma = {}, set(), [], 0.0
+        while ready:
+            cand, t1, i1 = [], 1e18, -1
+            for i in ready:
+                e = eng[i]
+                st = rt[i] if rt[i] > free[e] else free[e]
+                if banks[i]:
+                    if fresh[i] and locked and any(x in locked for x in banks[i]):
+                        continue
+                    for x in banks[i]:
+                        for f, j in bank.get(x, ()):
+                            if f != e and end[j] + far[j] > st:
+                                st = end[j] + far[j]
+                cand.append((st, i))
+                t = st + WIN * hold[i]
+                if t < t1:
+                    t1, i1 = t, i
+            e, best, i = eng[i1], -1e18, -1
+            for s, j in cand:
+                if eng[j] == e and (s < t1 or j == i1) and pr[j] > best:
+                    best, i, st = pr[j], j, s
+            ready.remove(i)
+            dep = deps[i]
+            for x in banks[i]:
+                old = bank.get(x, ())
+                dep = dep + [j for f, j in old if f != e]
+                bank[x] = [(f, j) for f, j in old if f != e] + [(e, i)]
+                if ops[i]["lock"] == "open":
+                    locked.add(x)
+                if ops[i]["lock"] == "close":
+                    locked.discard(x)
+            full[i], start[i] = dep, st
+            end[i] = st + ns[i]
+            if isdma[i]:
+                end[i] = dma = max(st + DL, dma) + ns[i] - DL
+            free[e] = st + hold[i]
+            seq.append(i)
+            for j in succ[i]:
+                left[j] -= 1
+                if left[j] == 0:
+                    rt[j] = max([end[x] + (near[x] if eng[x] == eng[j] else far[x]) for x in deps[j]] or [0.0])
+                    ready.append(j)
+        return seq, full, start, max(end)
+
+    def retime(plan, m, tab):
+        free, end, dma = {e: 0.0 for e in "vspgy"}, [0.0] * n, 0.0
+        for i in plan[0]:
+            st = free[eng[i]]
+            for j in plan[1][i]:
+                t = end[j] + tab[2 if eng[j] == eng[i] else 3][j]
+                if t > st:
+                    st = t
+            end[i] = st + tab[0][i]
+            if isdma[i]:
+                end[i] = dma = max(st + DL, dma) + tab[0][i] - DL
+            free[eng[i]] = st + tab[1][i]
+        return max(end)
+
+    def score(plan):
+        return (plan[3] + sum(retime(plan, m, t) * m["WT"] for m, t in zip(models, tabs))) / (1 + len(models))
+
+    names = sorted(set(o["k"] for o in ops))
+    names += [x for x in names if x[0] == "m"] * 2
+    where = {}
+    for i, o in enumerate(ops):
+        where.setdefault(o["k"], []).append(i)
+    pr = [prio[i] + KN["BIAS"].get(ops[i]["k"], 0.0) for i in range(n)]
+    best = place(pr)
+    cost = top = score(best)
+    base, rnd = best[3], [KN["SEED"]]
+    now = best
+
+    def draw(k):
+        rnd[0] = (rnd[0] * 1103515245 + 12345) % 2147483648
+        return (rnd[0] >> 8) % k
+
+    for it in range(KN["ITER"]):
+        if it % KN["FB"] == 0 or it < KN["FB0"]:
+            trial = back([now[2][i] + ns[i] for i in range(n)])
+        else:
+            trial = list(pr)
+            for _ in range(1 + draw(KN["MOVES"])):
+                d = KN["JIT"] * (draw(2001) - 1000) / 1000.0
+                for i in where[names[draw(len(names))]]:
+                    trial[i] += d
+        plan = place(trial)
+        if plan[3] > base + 1500 and it >= KN["FB0"]:
+            continue
+        c = score(plan)
+        if c <= cost + KN["TEMP"] * (1 - it / KN["ITER"]) or it < KN["FB0"]:
+            pr, cost, base, now = trial, c, plan[3], plan
+            if c < top:
+                best, top = plan, c
+    return best + (top, ops)
+
+
+def dur(o, m):
+    kind, x = o["c"]
+    if kind in ("GA", "SCA"):
+        return (50 if o["e"] == "v" else 65) + x * m[kind] * m["CY"]
+    if kind == "c":
+        return m["FV" if o["e"] == "v" else "FS"] + max(m["MX"], x) * m["CY"]
+    if kind == "q":
+        return m["FS"] + (max(m["MX"], x) + x * m["PSN"]) * m["CY"]
+    if kind == "g":
+        return 150 + 2 * x * m["CY"]
+    if kind == "p":
+        return x * m["PCY"]
+    if kind == "r":
+        return m["RT"] + 128 * x / m["RW"]
+    return m["DL"] + 128 * x / m["BW"]
 
 
 PLAN = []
-BIAS = {}
 
 
 def rank_program(g, core, T, topo):
@@ -542,7 +756,7 @@ def rank_program(g, core, T, topo):
     ops = build(T, topo, core, rank)
     if not PLAN:
         PLAN.append(greedy(ops))
-    seq, deps, start, _ = PLAN[0]
+    seq, deps, start = PLAN[0][:3]
     queue = {"v": g.vector, "s": g.scalar, "p": g.tensor, "g": g, "y": g.sync}
     count = {}
     known = {e: {} for e in queue}

from concourse.mybir import AluOpType, ActivationFunctionType
OP = AluOpType
AF = ActivationFunctionType

W, C, NV = 4096, 192, 5
NH = 2
MB = 6
CW = 16 * MB
SL = 17 * MB
NK = (SL + 15) // 16
SP = 16 * NK
BIG = 1048576.0
K = 8192.0
ZT, ZN = -8448.0, -16640.0
STEP = 16384.0
TRASH = 2 * W + 16
TW = TRASH + 512 * MB
f32, bf, i32, u16 = "float32", "bfloat16", "int32", "uint16"
KN = {"LQ": (("y", ("d0", "d1", "lo", "lp")), ("s", ("ln", "lm", "lt", "lw"))), "SQ": "yyyyys", "GV": (2, 1), "EG": True,
      "LEAD": 1500.0, "WIN": 1.0, "DL": 1000.0, "BW": 500.0, "NE": 8, "ENC": "PPPPPPPP", "DEC": "svsv", "TS": True,
      "C1": ((1, 6, "v"), (6, 11, "v"), (11, 16, "v")), "C2": ((1, 6, "v"), (6, 11, "v"), (11, 16, "s")),
      "CB": (3, 3), "NP": 4, "SS": False, "NZ": 4, "GE": "ss", "HEAD": "s", "HP": 1, "ZP": False, "SO": "s", "FU": False, "XO": "p",
      "CY": 0.83, "PCY": 0.44, "PSN": 0.5, "HOP": 215.0, "HS": 80.0, "LP": 150.0, "LS": 0.0, "LG": 2500.0, "DQ": 200.0, "GA": 1.56, "SCA": 3.8, "RT": 1500.0, "RW": 200.0,
      "ISS": 600.0, "FV": 12.0, "FS": 40.0, "MX": 64,
      "ALT": ({"CY": 1.1, "PCY": 0.55, "PSN": 1.0, "GA": 1.9, "SCA": 5.0, "RT": 2500.0, "HOP": 330.0, "HS": 120.0, "LG": 5000.0, "FS": 80.0, "FV": 40.0, "WT": 0.65},
              {"PSN": 0.0, "RT": 1500.0, "HOP": 130.0, "HS": 60.0, "LP": 50.0, "FS": 90.0, "FV": 50.0, "MX": 0, "WT": 1.0}),
      "BIAS": {"ik10": 5000.0, "iia00": 5000.0, "iones0": 5000.0}, "FB": 5, "FB0": 6, "MOVES": 4, "SEED": 1, "ITER": 4000, "JIT": 1000.0, "TEMP": 100.0}

SCRATCH = {
    "tab": ("sbuf", [128, TW], bf), "raw": ("sbuf", [128, TW // 2], bf), "zr": ("sbuf", [128, 2, 512], bf),
    "MS": ("sbuf", [128, NV * NH, MB, 20], f32), "SO": ("sbuf", [128, NV * NH, MB, 20], f32),
    "TR": ("sbuf", [128, NV * NH, CW], bf), "TS": ("sbuf", [128, NV * NH, CW], bf),
    "lnam": ("sbuf", [128, C], i32), "lmrk": ("sbuf", [128, C], i32), "lown": ("sbuf", [128, C], i32),
    "lwt": ("sbuf", [128, 4], i32), "lthr": ("sbuf", [128, 8], i32),
    "a3": ("sbuf", [128, 6, 32], f32), "b3": ("sbuf", [128, 6, 32], f32), "tmp": ("sbuf", [128, C], f32),
    "ones": ("sbuf", [128, 160], f32), "wide": ("sbuf", [128, 160], f32), "wide0": ("sbuf", [128, 160], f32),
    "wide1": ("sbuf", [128, 160], f32), "nidf": ("sbuf", [128, 128], f32), "ids": ("sbuf", [128, 8, 128], bf),
    "gm": ("sbuf", [128, 128], f32), "ia": ("sbuf", [128, 3, 160], i32),
    "gmb": ("sbuf", [128, 128], bf), "whi": ("sbuf", [128, 128], bf), "wlo": ("sbuf", [128, 128], bf),
    "sel": ("sbuf", [128, 2, 144], bf), "g8t": ("sbuf", [128, 256], f32),
    "ci": ("sbuf", [128, 12, 8], i32), "cf": ("sbuf", [128, 16, 8], f32),
    "ij": ("sbuf", [128, CW], i32), "jj": ("sbuf", [128, C], f32),
    "adiag": ("sbuf", [128, CW], f32), "d0r": ("sbuf", [128, SL], f32), "d0u": ("sbuf", [128, SL], f32),
    "key": ("sbuf", [128, SP], f32), "kc": ("sbuf", [128, 5, SP], bf), "kk": ("sbuf", [128, 512], bf),
    "dth": ("sbuf", [128, NV, 128], bf), "out": ("sbuf", [128, 3, C], f32), "ls": ("sbuf", [128, 4, 8], u16),
}
PER_HALF = {
    "G": ([MB, 256], bf), "I": ([MB, 256], bf), "off": ([CW + 2], u16), "Pe": ([CW], bf), "le": ([CW], bf), "offp": ([MB], u16),
    "xoff": ([MB], u16), "soff": ([2 * MB], u16), "val": ([SL], f32), "R": ([SL], f32), "U": ([SL], f32),
    "sc": ([CW], f32), "sh": ([CW], f32), "E": ([2, MB, 18], f32), "D": ([3, SL], f32), "Rn": ([2 * SL], f32), "Rh": ([SL], f32),
    "P": ([CW], bf), "xk": ([CW], bf), "t": ([CW], bf), "FB": ([2 * CW], bf), "FC": ([2 * CW], bf), "Tc": ([CW], bf),
    "p1": ([CW], bf), "sg": ([SL], bf), "nl": ([CW], bf), "tb": ([SP], bf), "keep": ([SP], f32),
    "m1": ([3 * SP + 4], bf), "m2": ([3 * SP], bf), "w1": ([3 * SP + 4], f32), "w2": ([3 * SL], f32),
    "si": ([8, 8], i32), "sf": ([8, 8], f32), "ax": ([MB, 16], f32),
}
for _h in range(NH):
    for _k, (_s, _d) in PER_HALF.items():
        SCRATCH[_k + str(_h)] = ("sbuf", [128] + _s, _d)
    SCRATCH["pA%d" % _h] = ("psum", [128, 32, 16], f32)
    SCRATCH["pB%d" % _h] = ("psum", [128, 30, 17], f32)
    SCRATCH["pC%d" % _h] = ("psum", [128, 512], f32)
    SCRATCH["pE%d" % _h] = ("psum", [128, 32, 16], f32)
ND = 2
LOADS = ["d%d" % j for j in range(ND)] + ["ln", "lm", "lo", "lp", "lw", "lt"]
SEMAPHORES = (["v", "s", "p", "g", "sent", "st"] + LOADS
              + ["a%s%d%d" % (k, v, h) for k in "MT" for v in range(1, NV) for h in range(NH)])


def build(T, topo, core, rank):
    ops = []
    GA, SCA = "GA", "SCA"

    def op(e, fs, r, w, c, banks=(), lock=None, sem=None):
        ops.append({"e": e, "f": fs if isinstance(fs, list) else [fs], "r": r, "w": w, "c": c,
                    "banks": banks, "lock": lock, "sem": sem, "k": "i%s%d" % ((w + ["st"])[0], sum(o["w"][:1] == w[:1] for o in ops))})

    def bk(names):
        return tuple(sorted(set(n[:3] for n in names if n[0] == "p" and n[1] in "ABCE")))

    def V(f, r, w, n, rate="c"):
        op("v", f, r, w, (rate, n), bk(r + w))

    def S(f, r, w, n, rate="c"):
        op("s", f, r, w, ("q" if bk(r) else rate, n), bk(r + w))

    def G(f, r, w, n):
        op("g", f, r, w, ("g", n))

    def iota(o, pattern, base, cm, w, n):
        G(lambda q: q.iota(o, pattern, base, cm, allow_small_or_imprecise_dtypes=True), [], w, n)

    def fill(o, c, w, n):
        iota(o, [[0, n]], c, 0, w, n)

    def P(mm, r, w, first=True, last=True):
        fs, ns = [], 0
        for k, (o, l, x, cost) in enumerate(mm):
            fs.append(lambda q, o=o, l=l, x=x, a=(first and k == 0), b=(last and k == len(mm) - 1): q.matmul(o, l, x, a, b))
            ns += max(64, cost)
        op("p", fs, r, w, ("p", ns), bk(r + w), None if first and last else ("open" if first else "close" if last else "more"))

    def tt(o, a, b, f):
        return lambda q: q.tensor_tensor(o, a, b, f)

    def ts(o, a, s1, f1, s2=None, f2=None):
        if f2 is None:
            return lambda q: q.tensor_scalar(o, a, s1, None, f1)
        return lambda q: q.tensor_scalar(o, a, s1, s2, f1, f2)

    def cp(o, a):
        return lambda q: q.tensor_copy(o, a)

    def ms(o, c):
        return lambda q: q.memset(o, c)

    def tr(o, a):
        return lambda q: q.transpose(o, a)

    def act(o, a, f, bias=0.0, scale=1.0):
        return lambda q: q.activation(o, a, f, bias=bias, scale=scale)

    def scan(o, a, b, f0, f1):
        return lambda q: q.tensor_tensor_scan(o, a, b, 0.0, f0, f1)

    def load(e, name, o, i, w, by):
        op(e, lambda q: q.dma_start(o, i), [], w + ["~load" + e], ("d", by), sem=name)

    def store(o, i, r, by, e="y"):
        op(e, lambda q: q.dma_start(o, i), r, [], ("d", by), sem="st")

    DW = W // ND
    loads = {"ln": (T.lnam[:], T.nam[:], ["lnam"], 4 * C), "lm": (T.lmrk[:], T.mrk[:], ["lmrk"], 4 * C),
             "lt": (T.lthr[0:8, 0:5], T.thr[:], ["lthr"], 4), "lp": (T.TR[:, 0:NH, :], T.pic[:], ["T00", "T01"], 2 * C),
             "lw": (T.lwt[:, 0:1], T.wt[:], ["lwt"], 4), "lo": (T.lown[:], T.own[:], ["lown"], 4 * C)}
    for j in range(ND):
        loads["d%d" % j] = (T.raw[:, DW * j:DW * j + DW], T.dep[:, DW * j:DW * j + DW], ["raw%d" % j], 2 * DW)
    for e, names in KN["LQ"]:
        for name in names:
            load(e, name, *loads[name])

    idf, nidf = T.wide[:, 16:144], T.nidf[:]
    col = lambda k: T.cf[:, k, 0:1]
    PM, PM1, SCL, H0, H1, WH, WL = range(7)
    kh, ks, ky, kz, k1 = range(5)
    kc = lambda k, n=CW: T.kc[:, k, 0:n]
    scales = {"id": 1.0, "nid": -1.0, "id2k": 2 * K, "ida": 255.0 / 256, "nk": -K, "big": BIG, "nbig": -BIG}
    if not KN["FU"]:
        del scales["nk"]
        scales.update({"idc": 256 * K, "idd": -255 * K})
    I = {n: T.ids[:, j, :] for j, n in enumerate(scales)}
    V(ms(T.ones[:], 1.0), [], ["ones"], 160)
    G(lambda q: q.iota(T.ia[:, 0, :], [[-1, 160]], 16, 1), [], ["ia0"], 160)
    V(ts(T.wide[:], T.ia[:, 0, :], 0.0, OP.is_equal), ["ia0"], ["wide"], 160)
    V(ms(T.kk[:], K), [], ["kk"], 256)
    V(ms(T.tab[:, 1:2 * W:2], ZT), [], ["tabZ"], W // 2)
    fill(T.tab[:, 2 * W:TRASH], int(ZN), ["tabN"], 16)
    V(ts(T.ci[:, 1, 0:1], T.ia[:, 0, 16:17], 16, OP.bitwise_and), ["ia0"], ["ci1"], 1)
    V(ts(col(H1), T.ci[:, 1, 0:1], 0.0625, OP.mult), ["ci1"], ["H1"], 1)
    V(ts(col(H0), T.ci[:, 1, 0:1], -0.0625, OP.mult, 1.0, OP.add), ["ci1"], ["H0"], 1)
    S(act(T.wide0[:], T.wide[:], AF.Identity, scale=col(H0)), ["wide", "H0"], ["wide0"], 160)
    S(act(T.wide1[:], T.wide[:], AF.Identity, scale=col(H1)), ["wide", "H1"], ["wide1"], 160)
    swap = {(0, 0): T.wide0[:, 16:144], (0, 1): T.wide0[:, 0:128], (1, 0): T.wide1[:, 32:160], (1, 1): T.wide1[:, 16:144]}
    for n, c in scales.items():
        S(act(I[n], idf, AF.Copy, scale=c), ["wide"], [n], 128)
    S(act(T.nidf[:], idf, AF.Copy, scale=-1.0), ["wide"], ["nidf"], 128)
    G(lambda q: q.iota(T.ia[:, 1, 0:128], [[-16, 8], [0, 16]], 0, 1), [], ["ia1"], 128)
    V(ts(T.ia[:, 1, 0:128], T.ia[:, 1, 0:128], -16, OP.bitwise_and), ["ia1"], ["ia1"], 128)
    V(ts(T.gm[:], T.ia[:, 1, 0:128], 0.0, OP.is_equal), ["ia1"], ["gm"], 128)
    fill(T.sel[:], 0, ["sel"], 288)
    S(act(kc(k1, SL), T.ones[:, 0:SL], AF.Sigmoid, scale=256.0), ["ones"], ["k1", "~first"], 1650)
    V(ts(T.sel[:, 0, 15:143:16], T.gm[:, 0::16], -BIG, OP.mult), ["gm", "sel"], ["sel0"], 8)
    V(ts(T.sel[:, 1, 15:143:16], T.gm[:, 0::16], -BIG / K, OP.mult), ["gm", "sel"], ["sel1"], 8)
    S(act(T.gmb[:], T.gm[:], AF.Copy), ["gm"], ["gmb"], 128)
    V(ts(T.ci[:, 2, 0:1], T.lwt[:, 0:1], 3840, OP.bitwise_and), ["lwt"], ["ci2"], 1)
    V(ts(T.ci[:, 2, 1:2], T.lwt[:, 0:1], 255, OP.bitwise_and), ["lwt"], ["ci3"], 1)
    V(cp(T.cf[:, WH, 0:2], T.ci[:, 2, 0:2]), ["ci2", "ci3"], ["WH"], 1)
    S(act(T.whi[:], T.gm[:], AF.Identity, scale=T.cf[:, WH, 0:1]), ["gm", "WH"], ["whi"], 128)
    S(act(T.wlo[:], T.gm[:], AF.Identity, scale=T.cf[:, WH, 1:2]), ["gm", "WH"], ["wlo"], 128)
    G(lambda q: q.iota(T.ia[0:8, 2, 0:128], [[1, 128]], 0, -16), [], ["ia2"], 128)
    V(ts(T.ia[0:8, 2, 0:128], T.ia[0:8, 2, 0:128], -16, OP.bitwise_and), ["ia2"], ["ia2"], 128)
    V(ts(T.g8t[0:8, 0:128], T.ia[0:8, 2, 0:128], 0.0, OP.is_equal), ["ia2"], ["g8t"], 128)
    V(cp(T.cf[0:8, 8, 0:5], T.lthr[0:8, 0:5]), ["lthr"], ["cf8"], 5)
    P([(T.pB1[:, 29, 0:5], T.g8t[0:8, 0:128], T.cf[0:8, 8, 0:5], 256)], ["g8t", "cf8"], ["pB1thr"])
    V(ts(T.cf[:, 9, 0:5], T.pB1[:, 29, 0:5], -0.5, OP.add, BIG, OP.mult), ["pB1thr"], ["thr"], 5)
    V(ts(T.cf[:, 9, 2:5:2], T.pB1[:, 29, 2:5:2], 0.5, OP.add, BIG, OP.mult), ["pB1thr", "thr"], ["thr"], 2)
    for v in range(NV):
        S(act(T.dth[:, v, :], idf, AF.Identity, scale=T.cf[:, 9, v:v + 1]), ["wide", "thr"], ["dth%d" % v], 128)
    G(lambda q: q.iota(T.ij[:], [[0, MB], [1, 16]], 0, 0), [], ["ij"], CW)
    V(ts(T.ci[:, 4, 0:1], T.ia[:, 0, 16:17], 15, OP.bitwise_and), ["ia0"], ["ci4"], 1)
    V(cp(col(PM), T.ci[:, 4, 0:1]), ["ci4"], ["PM"], 1)
    V(ts(col(PM1), T.ci[:, 4, 0:1], 1.0, OP.add), ["ci4"], ["PM1"], 1)
    V(ts(col(SCL), T.ci[:, 4, 0:1], 15.0, OP.is_equal, 2.0 ** -13, OP.max), ["ci4"], ["SCL"], 1)
    V(ts(T.jj[:, 0:CW], T.ij[:], col(PM), OP.not_equal), ["ij", "PM"], ["jj"], CW)
    V(ts(T.jj[:, CW:C], T.ij[:], col(PM1), OP.is_equal, 8191.0, OP.mult), ["ij", "PM1"], ["jt"], CW)
    V(tt(T.adiag[:], T.jj[:, 0:CW], T.jj[:, CW:C], OP.add), ["jj", "jt"], ["adiag"], 2 * CW)
    for H in map(str, range(NH)):
        fill(T["m1" + H][:, 1:3 * SL:3], 0, ["m1" + H], SL)
        V(ms(T["m1" + H][:, 1:3 * SL:51], 1.0), ["m1" + H], ["m1" + H], MB)
    for nm, c0 in (("d0r", -int(STEP)), ("d0u", -1)):
        fill(T[nm][:], c0, [nm], SL)
        V(ms(T[nm][:, 0::17], BIG), [nm], [nm], MB)
    fill(T.key[:, SL:SP], 0, ["kez"], SP - SL)
    iota(T.key[:, 0:SL], [[0, MB], [1, 17]], -1, 0, ["key"], SL)
    fill(kc(kh), 4096, ["kh"], CW)
    fill(kc(ks), 524288, ["ks"], CW)
    V(ms(kc(ky, SL), 1.75), [], ["ky"], SL // 2)
    fill(kc(kz), int(-ZN), ["kz"], CW)
    cf = lambda k: T.cf[:, k, 0:NK]
    iota(cf(10), [[16, NK]], 0, 0, ["l0"], NK)
    V(ts(cf(11), cf(10), col(PM), OP.add), ["l0", "PM"], ["lj"], NK)
    V(ts(T.ci[:, 5, 0:NK], cf(11), -8.0, OP.add, 1.0 / 17, OP.mult), ["lj"], ["lb"], NK)
    V(ts(cf(12), T.ci[:, 5, 0:NK], 17.0, OP.mult), ["lb"], ["l17"], NK)
    V(tt(cf(13), cf(12), cf(11), OP.is_equal), ["l17", "lj"], ["le"], NK)
    V(ts(cf(14), cf(13), float(MB), OP.mult), ["le"], ["lf"], NK)
    V(tt(cf(15), cf(14), T.ci[:, 5, 0:NK], OP.max), ["lf", "lb"], ["lg"], NK)
    Lk, Lb, Le, Lf = (T.ls[:, j, 0:NK] for j in range(4))
    V(ts(Lk, cf(15), float(MB), OP.min), ["lg"], ["Lk"], NK)
    V(ts(Lb, T.ci[:, 5, 0:NK], MB - 1.0, OP.min), ["lb"], ["Lb"], NK)
    V(ts(Le, Lb, 17.0, OP.mult, 16.0, OP.add), ["Lb"], ["Le"], NK)
    V(ts(Lf, Lb, 17.0, OP.mult, SL + 16.0, OP.add), ["Lb"], ["Lf"], NK)
    for h in range(NH):
        H = str(h)
        fill(T.MS[:, h], 0, ["M0" + H, "Mx0" + H], 20 * MB)
        fill(T["m1" + H][:, 0:1], 0, ["m0" + H], 1)
        fill(T["w1" + H][:], 0, ["w" + H], 3 * SP + 4)
        if KN["ZP"]:
            fill(T["w2" + H][:, 0:SL + 1:SL], 0, ["w2z" + H], 2)
        else:
            fill(T["m2" + H][:], 0, ["m2" + H], 3 * SP)
        fill(T["E" + H][:, :, :, 17], 0, ["Ez" + H], 2 * MB)
        iota(T["E" + H][:, :, :, 0], [[256, 2 * MB]], TRASH, 2, ["Et" + H], 2 * MB)
        G(lambda q, H=H: q.iota(T["si" + H][:, 6, MB:MB + 1], [[0, 1]], -1, 0), [], ["sk" + H], 1)
        fill(T["ax" + H][:], 0, ["ax" + H], CW)
    for v in range(NV):
        fill(T.SO[:, NH * v:NH * v + NH], 0, ["SOi%d" % v], NH * 20 * MB)

    TAB = ["tab%d" % j for j in range(8)]
    for j, how in enumerate(KN["ENC"]):
        x, xn = T.raw[:, 512 * j:512 * j + 512], "raw%d" % (512 * j // DW)
        o = T.tab[:, 1024 * j:1024 * j + 1024:2]
        bank = ("pA0", "pE0", "pA1", "pE1")[j % 4]
        if how == "P":
            S(act(T[bank][:], x, AF.Identity, -K, 2 * K), [xn], [bank], 512)
            V(tt(o, x, T[bank][:], OP.min), [xn, bank, "tabZ"], [TAB[j]], 512)
        elif how == "V":
            P([(T[bank][:], I["id2k"], x, 512), (T[bank][:], I["nid"], T.kk[:], 512)], [xn, "id2k", "nid", "kk"], [bank])
            V(tt(o, x, T[bank][:], OP.min), [xn, bank, "tabZ"], [TAB[j]], 512)
        else:
            z, zn = T.zr[:, j % 2, :], "zr%d" % (j % 2)
            if how == "S":
                S(act(z, x, AF.Relu, K, -2 * K), [xn], [zn], 512)
            else:
                V(ts(z, x, 0.0, OP.is_equal, K, OP.mult), [xn], [zn], 256)
            P([(T[bank][:], I["id"], x, 512), (T[bank][:], I["nid"], z, 512)], [xn, zn, "id", "nid"], [bank])
            S(act(o, T[bank][:], AF.Copy), [bank, "tabZ"], [TAB[j]], 512)
    TAB = TAB + ["tabZ"]

    def turn(src, bank, slot, r, w):
        for o in range(2):
            P([(T[bank][:, slot + o:slot + MB:2, :], swap[(o, k)], src(k), 256) for k in range(2)],
              r + ["wide0", "wide1"], [w])

    V(ts(T.tmp[:], T.lmrk[:], -0.1875, OP.mult, 0.1875, OP.add), ["lmrk"], ["tmp"], C)
    V(tt(T.a3[:], T.tmp[:], T.lnam[:], OP.add), ["tmp", "lnam"], ["a3"], 2 * C)
    V(cp(T.b3[:], T.lown[:]), ["lown"], ["b3"], C)
    for h in range(NH):
        H = str(h)
        E, D = T["E" + H], T["D" + H]
        turn(lambda k: T.a3[:, 3 * h:3 * h + 3, 16 * k:16 * k + 16], "pE" + H, 0, ["a3"], "pE" + H)
        V(tr(T["sc" + H][:], T["pE" + H][:, 0:MB, :]), ["pE" + H], ["sc" + H], CW)
        S(act(T.MS[:, h, 0:MB, 1:17], T["sc" + H][:], AF.Copy, scale=2.0), ["sc" + H], ["M0" + H], CW)
        turn(lambda k: T.b3[:, 3 * h:3 * h + 3, 16 * k:16 * k + 16], "pE" + H, 0, ["b3"], "pE" + H)
        V(tr(T["sh" + H][:], T["pE" + H][:, 0:MB, :]), ["pE" + H], ["sh" + H], CW)
        S(act(E[:, 0, :, 1:17], T["sh" + H][:], AF.Identity, 0.375, 2.0), ["sh" + H], ["E" + H], CW)
        S(act(E[:, 1, :, 1:9], E[:, 0, :, 9:17], AF.Copy), ["E" + H], ["Ea" + H], CW // 2)
        S(act(E[:, 1, :, 9:17], E[:, 0, :, 1:9], AF.Copy), ["E" + H], ["Eb" + H], CW // 2)
        S(act(T["sf" + H][:, 7, 0:MB], E[:, 0, :, 1], AF.Identity, 1.0), ["E" + H], ["c1" + H], MB)
        for j in range(2):
            pd, pn = T["pB" + H][:, (2 + j) * MB:(3 + j) * MB, :], "pB%sd%d" % (H, j)
            P([(pd, idf, E[:, j, :, 0:17], 4 * SL), (pd, nidf, E[:, j, :, 1:18], 4 * SL)],
              ["E" + H, "Ea" + H, "Eb" + H, "Ez" + H, "Et" + H, "wide", "nidf"], [pn])
            for i in (0, 2)[:2 - j]:
                S(act(D[:, j + i, :], pd, AF.Copy), [pn], ["D%d%s" % (j + i, H)], SL)

    nxt = T.cores[(rank + 1) % len(T.cores)]
    rid, pid, _ = topo.addr(nxt)
    emask = sum(1 << e for e in topo.engines(core, nxt)[:KN["NE"]])
    RAW = ["raw%d" % j for j in range(ND)]

    def send(src, dst, sem, r, w, by):
        op("g", lambda q: q.remote_dma(dst, src, T.sem[sem], T.sem.sent, pid, rid, emask), r, w, ("r", by), sem=sem)

    def part(v, h, second):
        H = str(h)
        b = lambda n: T[n + H]
        n_ = lambda *a: [x + H for x in a]
        k = v * NH + h
        last = v == NV - 1
        M, Mx, Tn, SOn = "M%d%s" % (v, H), "Mx%d%s" % (v, H), "T%d%s" % (v, H), "SO%d%s" % (v, H)
        o0, o, o1 = T.MS[:, k, 0:MB, 0:17], T.MS[:, k, 0:MB, 1:18], T.MS[:, k, 0:MB, 2:19]
        Gs = ["G%d_%s" % (m, H) for m in range(MB)]
        Pv, Pe, Tv, xk = b("P")[:], b("Pe")[:], T.TR[:, k, :], b("xk")[:]
        pA, pB, pC, pE = b("pA"), b("pB"), b("pC"), b("pE")
        A_, B_, C_, E_ = "pA" + H, "pB" + H, "pC" + H, "pE" + H
        X3 = 3 * SL
        c1, c2 = pC[:, 512 - CW:512], pC[:, 512 - 2 * CW:512 - CW]
        y1, y2 = pB[:, 0:MB, :], pB[:, MB:2 * MB, :]
        si = lambda j: b("si")[:, j, 0:MB]
        sf = lambda j: b("sf")[:, j, 0:MB]
        m1, m2, w1, w2 = b("m1"), b("m2"), b("w1"), b("w2")
        ns = m1[:, 3:X3 + 1:3]

        def compare(pieces, x, xr, ix, f, sign):
            n = max([r1 - r0 for r0, r1, e in pieces if e == "v"] or [0])
            if n:
                P([(pA[:, j:n * MB:n, :], I[ix[0]], x, CW) for j in range(n)], xr + [ix[0]], [A_])
            used = 0
            for r0, r1, e in pieces:
                E_ = "pE%d" % ((h + used) % NH)
                pE, used = T[E_], used + (e == "s")
                d, Gp, Ip = r1 - r0, b("G")[:, :, 16 * r0:16 * r1], b("I")[:, :, 16 * r0:16 * r1]
                In = n_(*["I%d_%d_" % (r0, m) for m in range(MB)])
                if e == "v":
                    assert d == n
                    cb = KN["CB"][second]
                    for m0 in range(0, MB, cb):
                        m1_ = m0 + cb
                        V(tt(b("I")[:, m0:m1_, 16 * r0:16 * r1], b("G")[:, m0:m1_, 16 * r0:16 * r1], pA[:, n * m0:n * m1_, :], f),
                          Gs[m0:m1_] + [A_], In[m0:m1_], d * 16 * cb)
                else:
                    mx, mg = [(pE[:, j:d * MB:d, :], I[ix[1]], x, CW) for j in range(d)], [(pE[:, 0:d * MB, :], I[ix[2]], Gp, d * CW)]
                    if sign[0]:
                        P(mx, xr + [ix[1]], [E_], last=False)
                        P(mg, Gs + [ix[2], E_], [E_], first=False)
                    elif KN["EG"]:
                        P(mg, Gs + [ix[2]], [E_], last=False)
                        P(mx, xr + [ix[1], E_], [E_], first=False)
                    else:
                        P(mx + mg, xr + Gs + list(ix[1:]), [E_])
                    S(act(Ip, pE[:, 0:d * MB, :], AF.Sigmoid, *sign), [E_], In, d * CW)

        def count(y, x, j, r0=1, r1=16):
            return [(pB[:, y:y + MB, r0 + 1:r1 + 1], T.sel[:, j, 15 - i:143 - i], x[:, :, 16 * r0 + i:16 * r1:16], MB * (r1 - r0)) for i in range(16)]

        def counts(y, name, pieces):
            mm, step = count(y, b("I"), 0), 16 // KN["NP"]
            for j in range(0, 16, step):
                P(mm[j:j + step], n_(*["I%d_%d_" % (r0, m) for r0, r1, e in pieces for m in range(MB)]) + ["sel0", name], [name],
                  first=False, last=j + step == 16)

        if not second:
            V(cp(b("offp")[:], T.MS[:, k, 0:MB, 1]), [M], n_("offp"), MB)
            win = T.tab[:, 0:2 * W]
            S(act(Pv, win.indirect(b("offp")[:, 0:MB]), AF.Abs), TAB + n_("offp"), n_("P"), CW, GA)
            V(cp(b("off")[:, 1:CW + 1], T.MS[:, k, 0:MB, 1:17]), [M], n_("off"), CW)
            for m in range(MB):
                src = win.indirect(b("off")[:, 16 * m + 2:16 * m + 17])
                if m < KN["GV"][h]:
                    V(cp(b("G")[:, m, 16:256], src), TAB + n_("off"), [Gs[m]], 240, GA)
                else:
                    S(act(b("G")[:, m, 16:256], src, AF.Copy), TAB + n_("off"), [Gs[m]], 240, GA)
            S(act(Pe, win.indirect(b("offp")[:, 0:MB]), AF.Copy), TAB + n_("offp"), n_("Pe"), CW, GA)
            compare(KN["C1"], Pv, n_("P"), ("id", "nid", "id"), OP.is_gt, (-128.0, 256.0))
            odd = []
            if v:
                S(act(sf(4), T.MS[:, k, :, 19], AF.Abs, -2.0, 1.0 / 4096), [Mx], n_("a1"), MB)
                S(act(b("tb")[:], sf(4).indirect(Lb), AF.Abs, -1.0), n_("a1") + ["Lb"], n_("tb"), SP, GA)
                odd = [(y1, I["big" if v % 2 else "nbig"], b("tb")[:, 0:SL], SL)]
            P([(y1, T.dth[:, v, :], kc(k1, SL), SL)] + odd, n_("tb") + ["big", "nbig", "k1", "dth%d" % v], [B_ + "y1"], last=False)
            counts(0, B_ + "y1", KN["C1"])
            V(tt(b("val")[:], y1, o0, OP.max), [B_ + "y1", M, Mx], n_("val"), SL)
            V(scan(b("R")[:], T.d0r[:], b("val")[:], OP.add, OP.min), n_("val") + ["d0r"], n_("R"), SL)
            V(ts(si(0), b("R")[:, 16::17], 2 * W + 0.75, OP.min, 0.25, OP.add), n_("R"), n_("x"), MB)
            V(ts(si(1), si(0), int(STEP) - 1, OP.bitwise_and), n_("x"), n_("xo"), MB)
            V(cp(b("xoff")[:], si(1)), n_("xo"), n_("xoff"), MB)
            xs = T.tab[:, 0:TRASH].indirect(b("xoff")[:, 0:MB])
            if KN["FU"]:
                V(tt(b("le")[:], xs, Pe, OP.is_le), TAB + ["tabN"] + n_("xoff", "Pe"), n_("le"), CW, GA)
                V(tt(b("t")[:], xs, b("le")[:], OP.mult), TAB + ["tabN"] + n_("xoff", "le"), n_("t"), CW, GA)
            S(act(xk, xs, AF.Copy), TAB + ["tabN"] + n_("xoff"), n_("xk"), CW, GA)
            P([(c2, I["id"], Tv, CW), (c2, I["nid"], Pv, CW), (c2, I["id"], T.kk[:, 0:CW], CW)], [Tn, "id", "nid", "kk"] + n_("P"), [C_ + "2"])
            V(tt(b("Tc")[:], Pv, c2, OP.min), n_("P") + [C_ + "2"], n_("Tc"), CW)
            P([(c1, I["id"], kc(kh), CW), (c1, T.whi[:], b("Tc")[:], CW), (c1, T.wlo[:], b("Tc")[:], CW)],
              n_("Tc") + ["kh", "whi", "wlo", "id"], [C_ + "1"])
            V(scan(b("sh")[:], T.adiag[:], c1, OP.mult, OP.max), [C_ + "1", "adiag"], n_("sh"), CW)
            V(ts(si(3), b("sh")[:, 15::16], col(SCL), OP.mult), n_("sh") + ["SCL"], n_("h1"), MB)
            V(ts(si(4), si(3), W - 1, OP.bitwise_and), n_("h1"), n_("h2"), MB)
            if KN["HP"]:
                V(ts(sf(5), si(4), 2.0, OP.mult, 0.375, OP.add), n_("h2"), n_("hr"), MB)
                if v:
                    V(ms(T.MS[:, k, 0:MB, 17], 0.0), [M], n_("hs"), MB)
            else:
                V(ts(T.MS[:, k, 0:MB, 17], si(4), 2.0, OP.mult, 0.375, OP.add), n_("h2") + [M], n_("hr"), MB)
                S(act(T.MS[:, k, 0:MB, 18], T.MS[:, k, 0:MB, 17], AF.Copy), n_("hr"), n_("hs"), MB)
            S(act(ns, b("R")[:], AF.Sigmoid, -20000.0), n_("R", "m1"), n_("ns"), SL)
            S(act(m1[:, 2:3 * SP + 1:3], b("R")[:].indirect(Le), AF.Sigmoid, 20000.0, -1.0), n_("R", "m1") + ["Le"], n_("nb"), SP, GA)
            if KN["XO"] == "s":
                S(act(pC[:, 3:X3 + 1:3], o, AF.Copy), [M] + n_("hs"), [C_ + "o", C_ + "h"], SL)
            else:
                P([(pC[:, 3:X3 + 1:3], idf, o, 4 * SL)], [M, "wide"] + n_("hs"), [C_ + "o", C_ + "h"])
            P([(pC[:, 1:X3 + 1:3], idf, o0, 4 * SL), (pC[:, 1:X3 + 1:3], nidf, o1, 4 * SL)], [M, "wide", "nidf"] + n_("hs"), [C_ + "d2"])
            P([(pC[:, 2:X3 + 1:3], nidf, o, 4 * SL), (pC[:, 2:X3 + 1:3], idf, o1, 4 * SL)], [M, "wide", "nidf"] + n_("hs"), [C_ + "dm"])
            for j, nm, f in ((46, "d2", OP.subtract), (47, "dm", OP.add))[:2 * KN["HP"]]:
                V(tt(pC[:, j:X3:51], pC[:, j:X3:51], sf(5), f), n_("hr") + [C_ + nm], [C_ + nm], MB)
            return
        u, le, Bv = b("t")[:], b("le")[:], b("FB")[:, CW:2 * CW]
        if KN["FU"]:
            compare(KN["C2"], u, n_("t"), ("ida", "ida", "nid"), OP.is_lt, (0.0, 65536.0))
        else:
            P([(pA[:, 0:MB, :], I["idc"], Pe, CW), (pA[:, 0:MB, :], I["idd"], xk, CW)], n_("xk", "Pe") + ["idc", "idd"], [A_])
            V(tt(u, xk, pA[:, 0:MB, :], OP.min), n_("xk") + [A_], n_("t"), CW)
            V(ts(Bv, u, -K, OP.max), n_("t"), n_("B"), CW // 2)
            compare(KN["C2"], Bv, n_("B"), ("ida", "ida", "nid"), OP.is_lt, (0.0, 65536.0))
        P([(c2, I["id"], kc(ks), CW), (c2, T.gmb[:], xk, CW)], n_("xk") + ["id", "ks", "gmb"], [C_ + "2"])
        V(scan(b("sc")[:], T.adiag[:], c2, OP.mult, OP.max), [C_ + "2", "adiag"], n_("sc"), CW)
        V(ts(si(5), b("sc")[:, 15::16], col(SCL), OP.mult), n_("sc") + ["SCL"], n_("s1"), MB)
        V(ts(si(6), si(5), 4096 + 15, OP.bitwise_and), n_("s1"), n_("s2"), MB)
        V(tt(b("keep")[:], b("si")[:, 6, 0:MB + 1].indirect(Lk), T.key[:], OP.not_equal), n_("s2", "sk") + ["Lk", "key", "kez"], n_("keep"), SP, GA)
        for j in range(2):
            V(scan(b("Rn")[:, SL * j:SL * j + SL], b("keep")[:, 0:SL], b("D")[:, j, :], OP.mult, OP.add), n_("keep", "D%d" % j), n_("Rn%d" % j), SL)
        if KN["FU"]:
            P([(c1, I["id"], xk, CW), (c1, I["nid"], u, CW), (c1, I["nk"], le, CW)][:2 if last else 3],
              n_("xk", "t", "le") + ["id", "nid", "nk"], [C_ + "1"])
        else:
            P([(c1, I["id"], xk, CW), (c1, I["nid"], Bv, CW)], n_("xk", "B") + ["id", "nid"], [C_ + "1"])
        if last:
            V(ts(b("soff")[:], b("Rn")[:, 16::17], 0.5, OP.mult), n_("Rn0", "Rn1"), n_("soff"), 2 * MB)
            S(act(b("FC")[:, 0:CW], c1, AF.Relu, 0.0 if KN["FU"] else -K), [C_ + "1"], n_("F"), CW)
            S(act(b("FC")[:, CW:2 * CW], u, AF.Relu), n_("t"), n_("Bp"), CW)
            V(cp(T.raw[:].indirect(b("soff")[:]), b("FC")[:]), n_("soff", "F", "Bp") + RAW, RAW, 2 * CW, SCA)
        else:
            V(cp(b("soff")[:], b("Rn")[:, 16::17]), n_("Rn0", "Rn1"), n_("soff"), 2 * MB)
            S(act(b("FB")[:, 0:CW], c1, AF.Identity, 0.0 if KN["FU"] else -K), [C_ + "1"], n_("F"), CW)
            if KN["FU"]:
                P([(c2, I["nid"], u, CW), (c2, I["nk"], le, CW)], n_("t", "le") + ["nid", "nk"], [C_ + "2"])
                S(act(Bv, c2, AF.Identity, -K, -1.0), [C_ + "2"], n_("B"), CW)
            if KN["SS"]:
                for j in (1, 0):
                    V(cp(T.tab[:].indirect(b("soff")[:, MB * j:MB * j + MB]), b("FB")[:, CW * j:CW * j + CW]),
                      n_("soff", "FB"[j]) + TAB + ["tabN"], TAB + ["tabN"], CW, SCA)
            else:
                V(cp(T.tab[:].indirect(b("soff")[:]), b("FB")[:]), n_("soff", "F", "B") + TAB + ["tabN"], TAB + ["tabN"], 2 * CW, SCA)
        V(tt(T.SO[:, k, :, 19], T.MS[:, k, :, 19], si(6), OP.add), [Mx, "SOi%d" % v] + n_("s2"), [SOn + "a"], 2 * MB)
        if KN["TS"]:
            S(act(b("nl")[:], xk, AF.Relu, ZT, -1.0), n_("xk"), n_("nl"), CW)
            P([(c1, I["id"], b("Tc")[:], CW), (c1, I["nid"], xk, CW)], n_("Tc", "xk") + ["id", "nid"], [C_ + "1"])
            S(act(b("p1")[:], c1, AF.Relu, ZN), [C_ + "1"], n_("p1"), CW)
            P([(c2, I["id"], Tv, CW), (c2, I["nid"], b("nl")[:], CW)], n_("nl") + [Tn, "id", "nid"], [C_ + "2"])
            V(tt(T.TS[:, k, :], b("p1")[:], c2, OP.max), n_("p1") + [C_ + "2"], ["TS%d" % k], CW)
        else:
            P([(c2, I["id"], kc(kz), CW), (c2, I["id"], xk, CW)], n_("xk") + ["id", "kz"], [C_ + "2"])
            V(tt(b("p1")[:], Tv, c2, OP.min), [Tn, C_ + "2"], n_("p1"), CW)
            P([(c1, I["nid"], kc(kz), CW), (c1, I["id"], b("Tc")[:], CW), (c1, I["nid"], xk, CW)], n_("Tc", "xk") + ["id", "nid", "kz"], [C_ + "1"])
            V(tt(T.TS[:, k, :], b("p1")[:], c1, OP.max), n_("p1") + [C_ + "1"], ["TS%d" % k], CW)
        cs = slice(CW * h, CW * h + CW)
        if last:
            V(ts(si(7), T.SO[:, k, :, 19], -1.0 / 4096, OP.mult, float(NV), OP.add), [SOn + "a"], n_("A"), MB)
            V(cp(b("ax")[:, :, 0], si(7)), n_("A", "ax"), n_("ax"), MB)
        else:
            send(T.TS[:, k, :], T.TR[:, k + NH, :], "aT%d%s" % (v + 1, H), ["TS%d" % k], ["T%d%s" % (v + 1, H)], 2 * CW)
        V(tt(b("D")[:, 2, 0:SL:17], si(1), sf(7), OP.subtract), n_("xo", "c1", "D2"), n_("D2"), 2 * MB)
        V(scan(b("Rh")[:], b("keep")[:, 0:SL], b("D")[:, 2, :], OP.mult, OP.add), n_("keep", "D2"), n_("Rh"), SL)
        if KN["HEAD"] == "s":
            S(act(pC[:, 0:X3:51], b("Rh")[:, 16::17], AF.Copy), n_("Rh") + [C_ + "o"], [C_ + "h"], MB)
        else:
            V(cp(pC[:, 0:X3:51], b("Rh")[:, 16::17]), n_("Rh") + [C_ + "o"], [C_ + "h"], MB)
        V(scan(w1[:, 0:X3 + 1], m1[:, 0:X3 + 1], pC[:, 0:X3 + 1], OP.mult, OP.add), n_("ns", "nb", "m0", "m1") + [C_ + "dm", C_ + "d2", C_ + "o", C_ + "h"],
          n_("w", "wa", "wb"), X3)
        V(tt(w1[:, 2:3 * SP + 1:3], b("Rn")[:].indirect(Lf), w1[:, 3:3 * SP + 1:3], OP.subtract), n_("Rn0", "Rn1", "w") + ["Lf"], n_("wa"), SP, GA)
        if not KN["ZP"]:
            S(act(w1[:, 4:X3 + 4:3], w1[:, 2:X3 + 1:3], AF.Copy, scale=-1.0), n_("wa"), n_("wb"), SL)
        nz = [(y2, I["big"], kc(ky, SL), SL)] + count(MB, b("G"), 1)
        cuts = [len(nz) * j // KN["NZ"] for j in range(KN["NZ"] + 1)]
        for j in range(KN["NZ"]):
            P(nz[cuts[j]:cuts[j + 1]], Gs + ["ky", "big", "sel1", B_ + "y1", B_ + "y2"], [B_ + "y2"], first=j == 0, last=False)
        counts(MB, B_ + "y2", KN["C2"])
        V(tt(b("val")[:], y2, ns, OP.max), [B_ + "y2"] + n_("ns"), n_("val"), SL)
        V(scan(b("U")[:], T.d0u[:], b("val")[:], OP.add, OP.min), n_("val") + ["d0u"], n_("U"), SL)
        if KN["ZP"]:
            gz, zo, Z = pC[:, 0:SL - 1], pC[:, 128:128 + SL], w2[:, 0:SL + 1]
            if KN["GE"][0] == "s":
                S(act(gz, b("U")[:, 1:SL], AF.Sigmoid, 128.0, -256.0), n_("U", "w"), [C_ + "o", C_ + "d2", C_ + "dm", C_ + "h"], SL)
            else:
                V(ts(gz, b("U")[:, 1:SL], 0.0, OP.is_le), n_("U", "w"), [C_ + "o", C_ + "d2", C_ + "dm", C_ + "h"], SL)
            V(tt(w2[:, 1:SL], w1[:, 2:X3 - 2:3], gz, OP.mult), n_("wa", "w2z") + [C_ + "o"], n_("w2"), SL)
            P([(zo, idf, w1[:, 3:X3 + 1:3], 4 * SL), (zo, idf, w2[:, 1:SL + 1], 4 * SL), (zo, nidf, w2[:, 0:SL], 4 * SL)],
              n_("w", "w2", "w2z") + ["wide", "nidf"], [C_ + "d2", C_ + "dm", C_ + "h"])
            S(act(T.SO[:, k, 0:MB, 1:18], zo, AF.Copy, scale=0.5 if last else 1.0), [C_ + "d2", "SOi%d" % v], [SOn], SL)
        else:
            for e, nm, dst, src in ((KN["GE"][0], "ge", m2[:, 2:X3 - 3:3], b("U")[:, 1:SL]), (KN["GE"][1], "gf", m2[:, 1:X3:3], b("U")[:])):
                if e == "s":
                    S(act(dst, src, AF.Sigmoid, 128.0, -256.0), n_("U", "m2"), n_(nm), SL)
                else:
                    V(ts(dst, src, 0.0, OP.is_le), n_("U", "m2"), n_(nm), SL)
            V(scan(w2[:], m2[:, 0:X3], w1[:, 1:X3 + 1], OP.mult, OP.add), n_("ge", "gf", "w", "wa", "wb"), n_("w2"), X3)
            if KN["SO"] == "s":
                S(act(T.SO[:, k, 0:MB, 1:18], w2[:, 2:X3:3], AF.Copy, scale=0.5 if last else 1.0), n_("w2") + ["SOi%d" % v], [SOn], SL)
            else:
                V(ts(T.SO[:, k, 0:MB, 1:18], w2[:, 2:X3:3], 0.5 if last else 1.0, OP.mult), n_("w2") + ["SOi%d" % v], [SOn], SL)
        if not last:
            send(T.SO[:, k], T.MS[:, k + NH], "aM%d%s" % (v + 1, H), [SOn, SOn + "a"],
                 ["M%d%s" % (v + 1, H), "Mx%d%s" % (v + 1, H)], 80 * MB)
            return
        turn(lambda j: b("ax")[:, j:MB:2, :], A_, 0, n_("ax"), A_)
        V(tr(T.out[:, 0, cs], pA[:, 0:MB, :]), [A_], n_("oc"), CW)
        turn(lambda j: T.SO[:, k, j:MB:2, 1:17], E_, 0, [SOn], E_)
        V(tr(b("sc")[:], pE[:, 0:MB, :]), [E_], n_("sc"), CW)
        V(cp(T.lnam[:, cs], b("sc")[:]), n_("sc"), n_("fi") + ["lnam"], CW)
        V(cp(T.out[:, 1, cs], T.lnam[:, cs]), n_("fi"), n_("on"), CW)
        V(tt(T.out[:, 2, cs], T.lnam[:, cs], b("sc")[:], OP.is_equal), n_("fi", "sc"), n_("om"), 2 * CW)

    for v in range(NV):
        if v == NV - 1:
            for j, e in enumerate(KN["DEC"]):
                n = W // len(KN["DEC"])
                o, x = T.raw[:, n * j:n * j + n], T.tab[:, 2 * n * j:2 * n * (j + 1):2]
                if e == "v":
                    V(ts(o, x, 0.0, OP.max), TAB, [RAW[n * j // DW]], n // 2)
                else:
                    S(act(o, x, AF.Relu), TAB, [RAW[n * j // DW]], n)
        for second in (False, True):
            for h in range(NH):
                a = len(ops)
                part(v, h, second)
                for j, o in enumerate(ops[a:]):
                    o["k"] = "%s%d%d%s%d" % ("amz"[(v > 0) + (v == NV - 1)], h, second, o["e"], j)
    for j in range(ND):
        store(T.ydep[:, DW * j:DW * j + DW], T.raw[:, DW * j:DW * j + DW], [RAW[j]], 2 * DW, KN["SQ"][j])
    k = NH * (NV - 1)
    store(T.ypic[:], T.TS[:, k:k + NH, :], ["TS%d" % (k + h) for h in range(NH)], 2 * C, KN["SQ"][ND])
    store(T.ycut[:], T.out[0:128:16, 0, :], ["oc0", "oc1"], C // 4, KN["SQ"][ND + 1])
    store(T.ynam[:], T.out[:, 1, :], ["on0", "on1"], 4 * C, KN["SQ"][ND + 2])
    store(T.ymrk[:], T.out[:, 2, :], ["om0", "om1"], 4 * C, KN["SQ"][ND + 3])
    return ops


def greedy(ops):
    n = len(ops)
    HOP = KN["HOP"]
    lastw, readers, deps, behind = {}, {}, [], []
    for i, o in enumerate(ops):
        d, s = set(), set()
        for x in o["r"] + o["w"]:
            if x in lastw:
                (s if x[0] == "~" else d).add(lastw[x])
        for x in o["w"]:
            (s if x[0] == "~" else d).update(readers.get(x, ()))
        if o["e"] == "p":
            s.update(j for j in d if ops[j]["e"] == "p")
            d = set(j for j in d if ops[j]["e"] != "p")
        deps.append(d - {i})
        behind.append((d | s) - {i})
        for x in o["r"]:
            readers.setdefault(x, []).append(i)
        for x in o["w"]:
            lastw[x] = i
            readers[x] = []
    succ = [[] for _ in ops]
    for i in range(n):
        for j in behind[i]:
            succ[j].append(i)
    eng = [o["e"] for o in ops]
    banks = [o["banks"] for o in ops]
    fresh = [o["e"] == "p" and o["lock"] not in ("more", "close") and o["banks"] for o in ops]
    isdma = [o["sem"] is not None and o["e"] != "g" for o in ops]
    deps = [sorted(d) for d in deps]

    def times(m):
        ns = [dur(o, m) for o in ops]
        ex = [m["LG"] if o["c"][0] == "g" else m["LP"] if o["e"] == "p" else m["LS"] if o["e"] == "s" else 0.0 for o in ops]
        return (ns, [ns[i] if o["sem"] is None else (m["ISS"] if o["e"] == "g" else m["DQ"]) for i, o in enumerate(ops)],
                [x + m["HS"] for x in ex], [x + m["HOP"] for x in ex])

    models = [dict(KN, **x) for x in KN["ALT"]]
    tabs = [times(m) for m in models]
    ns, hold, near, far = times(KN)
    DL, WIN = KN["DL"], KN["WIN"]
    prio = [0.0] * n
    for i in range(n - 1, -1, -1):
        prio[i] = ns[i] + HOP + max([prio[j] for j in succ[i]] or [0.0])
        if "SO%d0" % (NV - 1) in ops[i]["w"]:
            prio[i] += KN["LEAD"]

    after = [[] for _ in ops]
    for i in range(n):
        for j in deps[i]:
            after[j].append(i)
    stale = [o["e"] == "p" and o["lock"] not in ("more", "open") and o["banks"] for o in ops]

    def back(pr):
        left = [len(d) for d in succ]
        ready = [i for i in range(n) if left[i] == 0]
        free = {e: 0.0 for e in "vspgy"}
        end, rt = [0.0] * n, [ns[i] - hold[i] for i in range(n)]
        bank, locked = {}, set()
        while ready:
            cand, t1, i1 = [], 1e18, -1
            for i in ready:
                e = eng[i]
                st = rt[i] if rt[i] > free[e] else free[e]
                if banks[i]:
                    if stale[i] and locked and any(x in locked for x in banks[i]):
                        continue
                    for x in banks[i]:
                        for f, j in bank.get(x, ()):
                            if f != e and end[j] + far[i] > st:
                                st = end[j] + far[i]
                cand.append((st, i))
                t = st + WIN * hold[i]
                if t < t1:
                    t1, i1 = t, i
            e, best, i = eng[i1], -1e18, -1
            for s, j in cand:
                if eng[j] == e and (s < t1 or j == i1) and pr[j] > best:
                    best, i, st = pr[j], j, s
            ready.remove(i)
            for x in banks[i]:
                bank[x] = [(f, j) for f, j in bank.get(x, ()) if f != e] + [(e, i)]
                if ops[i]["lock"] == "close":
                    locked.add(x)
                if ops[i]["lock"] == "open":
                    locked.discard(x)
            end[i] = free[e] = st + hold[i]
            for j in behind[i]:
                left[j] -= 1
                if left[j] == 0:
                    rt[j] = max([end[x] + (near[j] if eng[x] == eng[j] else far[j]) for x in after[j]] or [0.0]) + ns[j] - hold[j]
                    ready.append(j)
        return end

    def place(pr):
        left = [len(d) for d in behind]
        ready = [i for i in range(n) if left[i] == 0]
        free = {e: 0.0 for e in "vspgy"}
        end, start, rt, full = [0.0] * n, [0.0] * n, [0.0] * n, [None] * n
        bank, locked, seq, dma = {}, set(), [], 0.0
        while ready:
            cand, t1, i1 = [], 1e18, -1
            for i in ready:
                e = eng[i]
                st = rt[i] if rt[i] > free[e] else free[e]
                if banks[i]:
                    if fresh[i] and locked and any(x in locked for x in banks[i]):
                        continue
                    for x in banks[i]:
                        for f, j in bank.get(x, ()):
                            if f != e and end[j] + far[j] > st:
                                st = end[j] + far[j]
                cand.append((st, i))
                t = st + WIN * hold[i]
                if t < t1:
                    t1, i1 = t, i
            e, best, i = eng[i1], -1e18, -1
            for s, j in cand:
                if eng[j] == e and (s < t1 or j == i1) and pr[j] > best:
                    best, i, st = pr[j], j, s
            ready.remove(i)
            dep = deps[i]
            for x in banks[i]:
                old = bank.get(x, ())
                dep = dep + [j for f, j in old if f != e]
                bank[x] = [(f, j) for f, j in old if f != e] + [(e, i)]
                if ops[i]["lock"] == "open":
                    locked.add(x)
                if ops[i]["lock"] == "close":
                    locked.discard(x)
            full[i], start[i] = dep, st
            end[i] = st + ns[i]
            if isdma[i]:
                end[i] = dma = max(st + DL, dma) + ns[i] - DL
            free[e] = st + hold[i]
            seq.append(i)
            for j in succ[i]:
                left[j] -= 1
                if left[j] == 0:
                    rt[j] = max([end[x] + (near[x] if eng[x] == eng[j] else far[x]) for x in deps[j]] or [0.0])
                    ready.append(j)
        return seq, full, start, max(end)

    def retime(plan, m, tab):
        free, end, dma = {e: 0.0 for e in "vspgy"}, [0.0] * n, 0.0
        for i in plan[0]:
            st = free[eng[i]]
            for j in plan[1][i]:
                t = end[j] + tab[2 if eng[j] == eng[i] else 3][j]
                if t > st:
                    st = t
            end[i] = st + tab[0][i]
            if isdma[i]:
                end[i] = dma = max(st + DL, dma) + tab[0][i] - DL
            free[eng[i]] = st + tab[1][i]
        return max(end)

    def score(plan):
        return (plan[3] + sum(retime(plan, m, t) * m["WT"] for m, t in zip(models, tabs))) / (1 + len(models))

    names = sorted(set(o["k"] for o in ops))
    names += [x for x in names if x[0] == "m"] * 2
    where = {}
    for i, o in enumerate(ops):
        where.setdefault(o["k"], []).append(i)
    pr = [prio[i] + KN["BIAS"].get(ops[i]["k"], 0.0) for i in range(n)]
    best = place(pr)
    cost = top = score(best)
    base, rnd = best[3], [KN["SEED"]]
    now = best

    def draw(k):
        rnd[0] = (rnd[0] * 1103515245 + 12345) % 2147483648
        return (rnd[0] >> 8) % k

    for it in range(KN["ITER"]):
        if it % KN["FB"] == 0 or it < KN["FB0"]:
            trial = back([now[2][i] + ns[i] for i in range(n)])
        else:
            trial = list(pr)
            for _ in range(1 + draw(KN["MOVES"])):
                d = KN["JIT"] * (draw(2001) - 1000) / 1000.0
                for i in where[names[draw(len(names))]]:
                    trial[i] += d
        plan = place(trial)
        if plan[3] > base + 1500 and it >= KN["FB0"]:
            continue
        c = score(plan)
        if c <= cost + KN["TEMP"] * (1 - it / KN["ITER"]) or it < KN["FB0"]:
            pr, cost, base, now = trial, c, plan[3], plan
            if c < top:
                best, top = plan, c
    return best + (top, ops)


def dur(o, m):
    kind, x = o["c"]
    if kind in ("GA", "SCA"):
        return (50 if o["e"] == "v" else 65) + x * m[kind] * m["CY"]
    if kind == "c":
        return m["FV" if o["e"] == "v" else "FS"] + max(m["MX"], x) * m["CY"]
    if kind == "q":
        return m["FS"] + (max(m["MX"], x) + x * m["PSN"]) * m["CY"]
    if kind == "g":
        return 150 + 2 * x * m["CY"]
    if kind == "p":
        return x * m["PCY"]
    if kind == "r":
        return m["RT"] + 128 * x / m["RW"]
    return m["DL"] + 128 * x / m["BW"]


PLAN = []


def rank_program(g, core, T, topo):
    rank = T.rank_of(core)
    if rank is None:
        return
    ops = build(T, topo, core, rank)
    if not PLAN:
        PLAN.append(greedy(ops))
    seq, deps, start = PLAN[0][:3]
    queue = {"v": g.vector, "s": g.scalar, "p": g.tensor, "g": g, "y": g.sync}
    count = {}
    known = {e: {} for e in queue}
    mark = {}
    sent = 0
    for i in seq:
        o = ops[i]
        e, q = o["e"], queue[o["e"]]
        for j in sorted(deps[i], key=lambda j: -start[j]):
            sem, val, seen = mark[j]
            if known[e].get(sem, 0) < val:
                q.wait_ge(T.sem[sem], val)
                known[e][sem] = val
                for s, x in seen.items():
                    if known[e].get(s, 0) < x:
                        known[e][s] = x
        for f in o["f"]:
            ins = f(q)
        if o["sem"] is None:
            ins.then_inc(T.sem[e], 1)
            count[e] = count.get(e, 0) + 1
            mark[i] = (e, count[e], dict(known[e]))
        elif e == "g":
            sent += KN["NE"]
            count[o["sem"]] = KN["NE"]
            mark[i] = (o["sem"], KN["NE"], {})
        else:
            ins.then_inc(T.sem[o["sem"]], 16)
            count[o["sem"]] = count.get(o["sem"], 0) + 16
            mark[i] = (o["sem"], count[o["sem"]], dict(known[e]))
    count["sent"] = sent
    for s, x in count.items():
        g.sync.wait_ge(T.sem[s], x)
